import numpy as np
import ml_dtypes


def mxq(x, axis, fmt="e4m3"):
    dtype, down = {"e4m3": (ml_dtypes.float8_e4m3fn, 7), "e5m2": (ml_dtypes.float8_e5m2, 14)}[fmt]
    v = np.moveaxis(np.asarray(x, np.float32).astype(ml_dtypes.bfloat16).astype(np.float64), axis, -1)
    blocks = v.reshape(v.shape[:-1] + (-1, 32))
    amax = np.abs(blocks).max(-1, keepdims=True)
    byte = np.maximum(np.where(amax > 0, np.frexp(amax)[1] - 1 + 127, 0) - down, 1)
    scale = np.exp2(byte - 127.0)
    codes = (blocks / scale).astype(np.float32).astype(dtype).astype(np.float64)
    return np.moveaxis((codes * scale).reshape(v.shape), -1, axis)


WIDE = False


def mx_kscale(k):
    if not WIDE:
        return np.ones(k)
    levels = np.array([10, -10, 5, -5, 0])
    if k % 512:
        return np.exp2(np.random.permutation(np.resize(levels, k // 32))).repeat(32)
    a = np.empty((k // 512, 16))
    for p in range(k // 512):
        a[p, :8] = np.random.permutation(np.resize(levels, 8))
        for g in range(8):
            far = levels[np.abs(levels - a[p, g]) >= 10]
            a[p, g + 8] = far[np.random.randint(len(far))]
    return np.exp2(a.ravel()).repeat(32)


def f64(x):
    return np.asarray(x).astype(np.float64)


def striped(idx):
    return np.tile(idx.reshape(-1, 16).T, (8, 1)).astype(np.uint16)


def unstriped(offs):
    return offs[:16].T.reshape(-1).astype(np.int64)


E2M1 = np.array([0.0, 0.5, 1.0, 1.5, 2.0, 3.0, 4.0, 6.0, -0.0, -0.5, -1.0, -1.5, -2.0, -3.0, -4.0, -6.0])


def pack_weight(w, fmt):
    k, n = w.shape
    w = f64(np.asarray(w, np.float32).astype(ml_dtypes.bfloat16)).reshape(k // 32, 32, n)
    amax = np.abs(w).max(1)
    if fmt == "e4m3":
        byte = np.frexp(amax)[1] - 1 + 127 - 7
    else:
        mant, ex = np.frexp(amax / 6.0)
        byte = np.where(mant > 0.5, ex, ex - 1) + 127
    byte = np.clip(np.where(amax > 0, byte, 1), 1, 254)
    scaled = (w * np.exp2(127.0 - byte)[:, None, :]).reshape(k, n).astype(np.float32)
    by_word = np.ascontiguousarray(scaled.reshape(k // 512, 128, 4, n).transpose(0, 1, 3, 2))
    if fmt == "e4m3":
        words = by_word.astype(ml_dtypes.float8_e4m3fn).view(np.uint8)
    else:
        c = by_word.astype(ml_dtypes.float4_e2m1fn).view(np.uint8) & 0xF
        words = (c[..., 0::2] | (c[..., 1::2] << 4)).reshape(k // 512, 128, 2 * n)
    return np.ascontiguousarray(words), np.ascontiguousarray(byte.astype(np.uint8).reshape(k // 512, 16, n))


def unpack_weight(words, scales, fmt):
    g, _, n = scales.shape
    words = np.ascontiguousarray(words).reshape(g, 128, n, -1)
    if fmt == "e4m3":
        vals = words.view(ml_dtypes.float8_e4m3fn).astype(np.float64)
    else:
        nib = np.empty((g, 128, n, 4), np.uint8)
        nib[..., 0::2] = words & 0xF
        nib[..., 1::2] = words >> 4
        vals = E2M1[nib]
    vals = vals * np.repeat(np.exp2(scales.astype(np.float64) - 127.0), 8, axis=1)[..., None]
    return vals.transpose(0, 1, 3, 2).reshape(g * 512, n)


def gelu(v):
    return 0.5 * v * (1.0 + np.tanh(np.sqrt(2.0 / np.pi) * (v + 0.044715 * v**3)))


K, M, T, S = 1536, 1024, 2048, 1024


def setup_inputs():
    n = np.random.standard_normal
    s = mx_kscale(K)[:, None]
    w = n((K, M)) / np.sqrt(K) / s
    v = pack_weight(n((K, T)) * s, "e4m3")
    p_w4 = pack_weight(w[512:], "e2m1")
    return {
        "tab_words": v[0],
        "tab_scales": v[1],
        "w8": (w[:512]).astype(np.float32),
        "w4_words": p_w4[0],
        "w4_scales": p_w4[1],
        "rT": n((M, T)).astype(np.float32),
        "b": (0.3 * n(1024)).astype(np.float32),
        "offs": striped(np.random.permutation(T)[:S]),
    }


def reference(tab_words, tab_scales, w8, w4_words, w4_scales, rT, b, offs):
    tab_ = unpack_weight(tab_words, tab_scales, "e4m3")[:, unstriped(offs)]
    w8_ = mxq(f64(w8), 0, "e4m3")
    w4_ = unpack_weight(w4_words, w4_scales, "e2m1")
    y = w8_.T @ tab_[:512] + w4_.T @ tab_[512:]
    return (gelu(y + f64(b)[:, None])) + f64(rT)[:, unstriped(offs)]

@@ -1,0 +1,177 @@
+from contextlib import ExitStack
+
+import concourse.mybir as mybir
+from concourse.masks import make_identity
+
+K, M, T, S = 1536, 1024, 2048, 1024
+FLOPS = 2 * K * M * S
+
+F32 = mybir.dt.float32
+BF16 = mybir.dt.bfloat16
+I32 = mybir.dt.int32
+U32 = mybir.dt.uint32
+U16 = mybir.dt.uint16
+U8 = mybir.dt.uint8
+FP8X4 = mybir.dt.float8_e4m3fn_x4
+FP4X4 = mybir.dt.float4_e2m1fn_x4
+GELU = mybir.ActivationFunctionType.Gelu_apprx_tanh
+ADD = mybir.AluOpType.add
+
+P = 128
+PACK = 4
+PASSES = K // (P * PACK)
+FP4_PASSES = PASSES - 1
+QUADS = 4
+QUAD = 32
+ROWS = 4
+BANK = 512
+TILES = M // P
+HALVES = S // BANK
+W8_PARTS = 2
+W8_COLS = M // W8_PARTS
+MOVED = 112
+RING = 6
+
+
+def tile_list_tabres_gelu_kernel(tc, tab_words, tab_scales, w8, w4_words, w4_scales, rT, b, offs, out):
+    nc = tc.nc
+    with ExitStack() as ctx:
+        held = ctx.enter_context(tc.tile_pool(name="held", bufs=1))
+        ring = ctx.enter_context(tc.tile_pool(name="ring", bufs=RING))
+        psum = ctx.enter_context(tc.psum_pool(name="psum", bufs=6))
+        psum_b = ctx.enter_context(tc.psum_pool(name="psum_b", bufs=1))
+
+        offsets = held.tile([P, S // 16], U16, name="offsets")
+        nc.sync.dma_start(offsets[:], offs)
+
+        scale_table = held.tile([P, T // 4], I32, name="scale_table", align_bytes=64)
+        w4_planes = held.tile([P, FP4_PASSES, M // 4], I32, name="w4_planes", align_bytes=64)
+        moved_planes = held.tile([P, FP4_PASSES, S // 4], I32, name="moved_planes", align_bytes=64)
+        nc.gpsimd.memset(scale_table[:], 0)
+        nc.vector.memset(w4_planes[:], 0)
+        nc.vector.memset(moved_planes[:], 0)
+        for q in range(QUADS):
+            nc.gpsimd.dma_start(
+                out=scale_table[QUAD * q : QUAD * q + PASSES * ROWS, :],
+                in_=tab_scales[:, ROWS * q : ROWS * (q + 1), :].bitcast(I32),
+            )
+
+        word_tables = []
+        residuals = []
+        w8_raw = [held.tile([P, PACK, W8_COLS], F32, name="w8_raw%d" % h) for h in range(W8_PARTS)]
+        w4_codes = held.tile([P, FP4_PASSES, 2 * M], U8, name="w4_codes", align_bytes=64)
+
+        def load_words(a):
+            word_tables.append(ring.tile([P, T], U32, name="window", align_bytes=64))
+            nc.sync.dma_start(out=word_tables[a][:].bitcast(I32), in_=tab_words[a].rearrange("p t i -> p (t i)").bitcast(I32))
+
+        def load_residual(m):
+            residuals.append(ring.tile([P, T], F32, name="window", align_bytes=64))
+            nc.sync.dma_start(out=residuals[m][:], in_=rT[m * P : (m + 1) * P, :])
+
+        def load_w8(h):
+            nc.sync.dma_start(out=w8_raw[h][:], in_=w8[:, h * W8_COLS : (h + 1) * W8_COLS].rearrange("(p j) n -> p j n", j=PACK))
+
+        for a in range(PASSES):
+            load_words(a)
+        for q in range(QUADS):
+            nc.sync.dma_start(
+                out=w4_planes[QUAD * q : QUAD * q + ROWS, :, :],
+                in_=w4_scales[:, ROWS * q : ROWS * (q + 1), :].rearrange("a r n -> r a n").bitcast(I32),
+            )
+        bias_rows = held.tile([P, P], F32, name="bias_rows")
+        nc.vector.memset(bias_rows[:], 0.0)
+        nc.sync.dma_start(out=bias_rows[0:TILES, :], in_=b.rearrange("(m p) -> m p", p=P))
+        load_residual(0)
+        load_w8(0)
+        nc.sync.dma_start(out=w4_codes[:].bitcast(I32), in_=w4_words.rearrange("a p n -> p a n").bitcast(I32))
+        load_residual(1)
+        load_w8(1)
+        load_residual(2)
+
+        warm = held.tile([P, 1], F32, name="warm")
+        nc.vector.memset(warm[:], 0.0)
+        nc.scalar.activation(warm[:], warm[:], GELU)
+
+        identity = held.tile([P, P], F32, name="identity")
+        make_identity(nc, identity[:])
+        bias_psum = psum_b.tile([P, P], F32, name="bias_psum")
+        nc.tensor.transpose(bias_psum[:], bias_rows[:], identity[:])
+        bias = held.tile([P, TILES], F32, name="bias")
+        nc.scalar.copy(bias[:], bias_psum[:, 0:TILES])
+
+        picked_words = [held.tile([P, S], U32, name="picked_words%d" % a, align_bytes=64) for a in range(PASSES)]
+        picked_scales = held.tile([P, S], U8, name="picked_scales", align_bytes=64)
+        picked_res = [held.tile([P, S], F32, name="picked_res%d" % m) for m in range(TILES)]
+
+        def gather_words(a):
+            nc.vector.tensor_copy(picked_words[a][:], word_tables[a][:].indirect(offsets[:]))
+
+        def gather_residual(m):
+            nc.vector.tensor_copy(picked_res[m][:], residuals[m][:].indirect(offsets[:]))
+
+        gather_words(0)
+        load_residual(3)
+        nc.vector.tensor_copy(picked_scales[:], scale_table[:].bitcast(U8).indirect(offsets[:]))
+        for a in range(1, PASSES):
+            nc.scalar.dma_start(
+                out=moved_planes[0:MOVED, a - 1, :],
+                in_=picked_scales[ROWS * a : ROWS * a + MOVED, :].bitcast(I32),
+            )
+        gather_words(1)
+        load_residual(4)
+        gather_words(2)
+        load_residual(5)
+
+        w8_codes = held.tile([P, M], U32, name="w8_codes", align_bytes=64)
+        w8_plane = held.tile([P, M], U8, name="w8_plane", align_bytes=64)
+        w8_grouped = [held.tile([P, W8_COLS, PACK], BF16, name="w8_grouped%d" % h, align_bytes=64) for h in range(W8_PARTS)]
+        for h in range(W8_PARTS):
+            cols = slice(h * W8_COLS, (h + 1) * W8_COLS)
+            nc.scalar.copy(w8_grouped[h][:], w8_raw[h][:].rearrange("p j n -> p n j"))
+            nc.vector.quantize_mx(
+                out=w8_codes[:, cols].bitcast(FP8X4),
+                scales=w8_plane[:, cols],
+                in_=w8_grouped[h][:].rearrange("p n j -> p (n j)"),
+            )
+        for m in range(TILES):
+            gather_residual(m)
+            if m + RING < TILES:
+                load_residual(m + RING)
+
+        results = [held.tile([P, S], F32, name="result%d" % m) for m in range(TILES)]
+        w4_scale_bytes = w4_planes[:].bitcast(U8)
+        moved_bytes = moved_planes[:].bitcast(U8)
+        for m in range(TILES):
+            rows = slice(m * P, (m + 1) * P)
+            for h in range(HALVES):
+                cols = slice(h * BANK, (h + 1) * BANK)
+                acc = psum.tile([P, BANK], F32, name="acc")
+                for a in range(FP4_PASSES):
+                    nc.tensor.matmul_mx(
+                        out=acc[:],
+                        lhsT=w4_codes[:, a, 2 * m * P : 2 * (m + 1) * P].bitcast(FP4X4),
+                        lhsT_scale=w4_scale_bytes[:, a, rows],
+                        rhs=picked_words[a + 1][:, cols].bitcast(FP8X4),
+                        rhs_scale=moved_bytes[:, a, cols],
+                        start=(a == 0),
+                        stop=False,
+                    )
+                nc.tensor.matmul_mx(
+                    out=acc[:],
+                    lhsT=w8_codes[:, rows].bitcast(FP8X4),
+                    lhsT_scale=w8_plane[:, rows],
+                    rhs=picked_words[0][:, cols].bitcast(FP8X4),
+                    rhs_scale=picked_scales[:, cols],
+                    start=False,
+                    stop=True,
+                )
+                nc.scalar.activation(results[m][:, cols], acc[:], GELU, bias=bias[:, m : m + 1])
+
+        for m in range(TILES):
+            parts = HALVES if m == TILES - 1 else 1
+            width = S // parts
+            for h in range(parts):
+                cols = slice(h * width, (h + 1) * width)
+                nc.vector.tensor_tensor(results[m][:, cols], results[m][:, cols], picked_res[m][:, cols], ADD)
+                nc.sync.dma_start(out=out[m * P : (m + 1) * P, cols], in_=results[m][:, cols])

@@ -29,8 +29,9 @@ TILES = M // P
 HALVES = S // BANK
 W8_PARTS = 2
 W8_COLS = M // W8_PARTS
-MOVED = 112
-RING = 6
+RING = 11
+QUANTISE_AFTER = 1
+POOL_TILES = 4
 
 
 def tile_list_tabres_gelu_kernel(tc, tab_words, tab_scales, w8, w4_words, w4_scales, rT, b, offs, out):
@@ -44,17 +45,11 @@ def tile_list_tabres_gelu_kernel(tc, tab_words, tab_scales, w8, w4_words, w4_sca
         offsets = held.tile([P, S // 16], U16, name="offsets")
         nc.sync.dma_start(offsets[:], offs)
 
-        scale_table = held.tile([P, T // 4], I32, name="scale_table", align_bytes=64)
+        scale_tables = held.tile([P, FP4_PASSES, T // 4], I32, name="scale_tables", align_bytes=64)
         w4_planes = held.tile([P, FP4_PASSES, M // 4], I32, name="w4_planes", align_bytes=64)
-        moved_planes = held.tile([P, FP4_PASSES, S // 4], I32, name="moved_planes", align_bytes=64)
-        nc.gpsimd.memset(scale_table[:], 0)
+        nc.vector.memset(scale_tables[:, 0, :], 0)
+        nc.gpsimd.memset(scale_tables[:, 1, :], 0)
         nc.vector.memset(w4_planes[:], 0)
-        nc.vector.memset(moved_planes[:], 0)
-        for q in range(QUADS):
-            nc.gpsimd.dma_start(
-                out=scale_table[QUAD * q : QUAD * q + PASSES * ROWS, :],
-                in_=tab_scales[:, ROWS * q : ROWS * (q + 1), :].bitcast(I32),
-            )
 
         word_tables = []
         residuals = []
@@ -63,7 +58,9 @@ def tile_list_tabres_gelu_kernel(tc, tab_words, tab_scales, w8, w4_words, w4_sca
 
         def load_words(a):
             word_tables.append(ring.tile([P, T], U32, name="window", align_bytes=64))
-            nc.sync.dma_start(out=word_tables[a][:].bitcast(I32), in_=tab_words[a].rearrange("p t i -> p (t i)").bitcast(I32))
+            words = tab_words[a].rearrange("p t i -> p (t i)").bitcast(I32)
+            for cols in (slice(0, T // 2), slice(T // 2, T)):
+                nc.sync.dma_start(out=word_tables[a][:, cols].bitcast(I32), in_=words[:, cols])
 
         def load_residual(m):
             residuals.append(ring.tile([P, T], F32, name="window", align_bytes=64))
@@ -72,22 +69,33 @@ def tile_list_tabres_gelu_kernel(tc, tab_words, tab_scales, w8, w4_words, w4_sca
         def load_w8(h):
             nc.sync.dma_start(out=w8_raw[h][:], in_=w8[:, h * W8_COLS : (h + 1) * W8_COLS].rearrange("(p j) n -> p j n", j=PACK))
 
+        bias_rows = held.tile([P, P], F32, name="bias_rows")
+        nc.gpsimd.memset(bias_rows[:], 0.0)
         for a in range(PASSES):
             load_words(a)
         for q in range(QUADS):
             nc.sync.dma_start(
+                out=scale_tables[QUAD * q + ROWS : QUAD * q + 2 * ROWS, 0, :],
+                in_=tab_scales[0, ROWS * q : ROWS * (q + 1), :].bitcast(I32),
+            )
+        load_residual(0)
+        for q in range(QUADS):
+            nc.sync.dma_start(
+                out=scale_tables[QUAD * q : QUAD * q + ROWS, :, :],
+                in_=tab_scales[1:PASSES, ROWS * q : ROWS * (q + 1), :].rearrange("a r t -> r a t").bitcast(I32),
+            )
+        for q in range(QUADS):
+            nc.gpsimd.dma_start(
                 out=w4_planes[QUAD * q : QUAD * q + ROWS, :, :],
                 in_=w4_scales[:, ROWS * q : ROWS * (q + 1), :].rearrange("a r n -> r a n").bitcast(I32),
             )
-        bias_rows = held.tile([P, P], F32, name="bias_rows")
-        nc.vector.memset(bias_rows[:], 0.0)
-        nc.sync.dma_start(out=bias_rows[0:TILES, :], in_=b.rearrange("(m p) -> m p", p=P))
-        load_residual(0)
+        nc.gpsimd.dma_start(out=bias_rows[0:TILES, :], in_=b.rearrange("(m p) -> m p", p=P))
         load_w8(0)
-        nc.sync.dma_start(out=w4_codes[:].bitcast(I32), in_=w4_words.rearrange("a p n -> p a n").bitcast(I32))
-        load_residual(1)
         load_w8(1)
-        load_residual(2)
+        load_residual(1)
+        nc.sync.dma_start(out=w4_codes[:].bitcast(I32), in_=w4_words.rearrange("a p n -> p a n").bitcast(I32))
+        for m in range(2, TILES):
+            load_residual(m)
 
         warm = held.tile([P, 1], F32, name="warm")
         nc.vector.memset(warm[:], 0.0)
@@ -101,7 +109,7 @@ def tile_list_tabres_gelu_kernel(tc, tab_words, tab_scales, w8, w4_words, w4_sca
         nc.scalar.copy(bias[:], bias_psum[:, 0:TILES])
 
         picked_words = [held.tile([P, S], U32, name="picked_words%d" % a, align_bytes=64) for a in range(PASSES)]
-        picked_scales = held.tile([P, S], U8, name="picked_scales", align_bytes=64)
+        picked_scales = [held.tile([P, S], U8, name="picked_scales%d" % a, align_bytes=64) for a in range(FP4_PASSES)]
         picked_res = [held.tile([P, S], F32, name="picked_res%d" % m) for m in range(TILES)]
 
         def gather_words(a):
@@ -110,38 +118,27 @@ def tile_list_tabres_gelu_kernel(tc, tab_words, tab_scales, w8, w4_words, w4_sca
         def gather_residual(m):
             nc.vector.tensor_copy(picked_res[m][:], residuals[m][:].indirect(offsets[:]))
 
-        gather_words(0)
-        load_residual(3)
-        nc.vector.tensor_copy(picked_scales[:], scale_table[:].bitcast(U8).indirect(offsets[:]))
-        for a in range(1, PASSES):
-            nc.scalar.dma_start(
-                out=moved_planes[0:MOVED, a - 1, :],
-                in_=picked_scales[ROWS * a : ROWS * a + MOVED, :].bitcast(I32),
-            )
-        gather_words(1)
-        load_residual(4)
-        gather_words(2)
-        load_residual(5)
-
         w8_codes = held.tile([P, M], U32, name="w8_codes", align_bytes=64)
         w8_plane = held.tile([P, M], U8, name="w8_plane", align_bytes=64)
-        w8_grouped = [held.tile([P, W8_COLS, PACK], BF16, name="w8_grouped%d" % h, align_bytes=64) for h in range(W8_PARTS)]
+        w8_grouped = held.tile([P, M, PACK], BF16, name="w8_grouped", align_bytes=64)
         for h in range(W8_PARTS):
-            cols = slice(h * W8_COLS, (h + 1) * W8_COLS)
-            nc.scalar.copy(w8_grouped[h][:], w8_raw[h][:].rearrange("p j n -> p n j"))
-            nc.vector.quantize_mx(
-                out=w8_codes[:, cols].bitcast(FP8X4),
-                scales=w8_plane[:, cols],
-                in_=w8_grouped[h][:].rearrange("p n j -> p (n j)"),
-            )
+            nc.scalar.copy(w8_grouped[:, h * W8_COLS : (h + 1) * W8_COLS, :], w8_raw[h][:].rearrange("p j n -> p n j"))
+
+        for a in range(PASSES):
+            gather_words(a)
+        for a in range(FP4_PASSES):
+            nc.vector.tensor_copy(picked_scales[a][:], scale_tables[:, a, :].bitcast(U8).indirect(offsets[:]))
         for m in range(TILES):
             gather_residual(m)
-            if m + RING < TILES:
-                load_residual(m + RING)
+            if m == QUANTISE_AFTER:
+                nc.vector.quantize_mx(
+                    out=w8_codes[:].bitcast(FP8X4),
+                    scales=w8_plane[:],
+                    in_=w8_grouped[:].rearrange("p n j -> p (n j)"),
+                )
 
         results = [held.tile([P, S], F32, name="result%d" % m) for m in range(TILES)]
         w4_scale_bytes = w4_planes[:].bitcast(U8)
-        moved_bytes = moved_planes[:].bitcast(U8)
         for m in range(TILES):
             rows = slice(m * P, (m + 1) * P)
             for h in range(HALVES):
@@ -153,7 +150,7 @@ def tile_list_tabres_gelu_kernel(tc, tab_words, tab_scales, w8, w4_words, w4_sca
                         lhsT=w4_codes[:, a, 2 * m * P : 2 * (m + 1) * P].bitcast(FP4X4),
                         lhsT_scale=w4_scale_bytes[:, a, rows],
                         rhs=picked_words[a + 1][:, cols].bitcast(FP8X4),
-                        rhs_scale=moved_bytes[:, a, cols],
+                        rhs_scale=picked_scales[a][:, cols],
                         start=(a == 0),
                         stop=False,
                     )
@@ -162,7 +159,7 @@ def tile_list_tabres_gelu_kernel(tc, tab_words, tab_scales, w8, w4_words, w4_sca
                     lhsT=w8_codes[:, rows].bitcast(FP8X4),
                     lhsT_scale=w8_plane[:, rows],
                     rhs=picked_words[0][:, cols].bitcast(FP8X4),
-                    rhs_scale=picked_scales[:, cols],
+                    rhs_scale=picked_scales[0][ROWS:P, cols],
                     start=False,
                     stop=True,
                 )
@@ -173,5 +170,6 @@ def tile_list_tabres_gelu_kernel(tc, tab_words, tab_scales, w8, w4_words, w4_sca
             width = S // parts
             for h in range(parts):
                 cols = slice(h * width, (h + 1) * width)
-                nc.vector.tensor_tensor(results[m][:, cols], results[m][:, cols], picked_res[m][:, cols], ADD)
+                engine = nc.gpsimd if m < POOL_TILES else nc.vector
+                engine.tensor_tensor(results[m][:, cols], results[m][:, cols], picked_res[m][:, cols], ADD)
                 nc.sync.dma_start(out=out[m * P : (m + 1) * P, cols], in_=results[m][:, cols])

@@ -30,8 +30,8 @@ HALVES = S // BANK
 W8_PARTS = 2
 W8_COLS = M // W8_PARTS
 RING = 11
-QUANTISE_AFTER = 1
-POOL_TILES = 4
+QUANTISE_AFTER = 0
+POOL_TILES = 6
 
 
 def tile_list_tabres_gelu_kernel(tc, tab_words, tab_scales, w8, w4_words, w4_scales, rT, b, offs, out):
@@ -58,9 +58,7 @@ def tile_list_tabres_gelu_kernel(tc, tab_words, tab_scales, w8, w4_words, w4_sca
 
         def load_words(a):
             word_tables.append(ring.tile([P, T], U32, name="window", align_bytes=64))
-            words = tab_words[a].rearrange("p t i -> p (t i)").bitcast(I32)
-            for cols in (slice(0, T // 2), slice(T // 2, T)):
-                nc.sync.dma_start(out=word_tables[a][:, cols].bitcast(I32), in_=words[:, cols])
+            nc.sync.dma_start(out=word_tables[a][:].bitcast(I32), in_=tab_words[a].rearrange("p t i -> p (t i)").bitcast(I32))
 
         def load_residual(m):
             residuals.append(ring.tile([P, T], F32, name="window", align_bytes=64))
@@ -69,32 +67,25 @@ def tile_list_tabres_gelu_kernel(tc, tab_words, tab_scales, w8, w4_words, w4_sca
         def load_w8(h):
             nc.sync.dma_start(out=w8_raw[h][:], in_=w8[:, h * W8_COLS : (h + 1) * W8_COLS].rearrange("(p j) n -> p j n", j=PACK))
 
+        table_rows = tab_scales.bitcast(I32).rearrange("a (q r) t -> r q a t", r=ROWS)
+        w4_rows = w4_scales.bitcast(I32).rearrange("a (q r) n -> r q a n", r=ROWS)
+        for r in range(ROWS):
+            nc.gpsimd.dma_start(out=scale_tables[r:P:QUAD, :, :], in_=table_rows[r][:, 1:PASSES, :])
+        for r in range(ROWS):
+            nc.gpsimd.dma_start(out=scale_tables[ROWS + r : P : QUAD, 0, :], in_=table_rows[r][:, 0, :])
+        for r in range(ROWS):
+            nc.gpsimd.dma_start(out=w4_planes[r:P:QUAD, :, :], in_=w4_rows[r])
         bias_rows = held.tile([P, P], F32, name="bias_rows")
-        nc.gpsimd.memset(bias_rows[:], 0.0)
+        nc.vector.memset(bias_rows[:], 0.0)
+        nc.gpsimd.dma_start(out=bias_rows[0:TILES, :], in_=b.rearrange("(m p) -> m p", p=P))
+
         for a in range(PASSES):
             load_words(a)
-        for q in range(QUADS):
-            nc.sync.dma_start(
-                out=scale_tables[QUAD * q + ROWS : QUAD * q + 2 * ROWS, 0, :],
-                in_=tab_scales[0, ROWS * q : ROWS * (q + 1), :].bitcast(I32),
-            )
         load_residual(0)
-        for q in range(QUADS):
-            nc.sync.dma_start(
-                out=scale_tables[QUAD * q : QUAD * q + ROWS, :, :],
-                in_=tab_scales[1:PASSES, ROWS * q : ROWS * (q + 1), :].rearrange("a r t -> r a t").bitcast(I32),
-            )
-        for q in range(QUADS):
-            nc.gpsimd.dma_start(
-                out=w4_planes[QUAD * q : QUAD * q + ROWS, :, :],
-                in_=w4_scales[:, ROWS * q : ROWS * (q + 1), :].rearrange("a r n -> r a n").bitcast(I32),
-            )
-        nc.gpsimd.dma_start(out=bias_rows[0:TILES, :], in_=b.rearrange("(m p) -> m p", p=P))
         load_w8(0)
         load_w8(1)
-        load_residual(1)
         nc.sync.dma_start(out=w4_codes[:].bitcast(I32), in_=w4_words.rearrange("a p n -> p a n").bitcast(I32))
-        for m in range(2, TILES):
+        for m in range(1, TILES):
             load_residual(m)
 
         warm = held.tile([P, 1], F32, name="warm")
@@ -110,13 +101,13 @@ def tile_list_tabres_gelu_kernel(tc, tab_words, tab_scales, w8, w4_words, w4_sca
 
         picked_words = [held.tile([P, S], U32, name="picked_words%d" % a, align_bytes=64) for a in range(PASSES)]
         picked_scales = [held.tile([P, S], U8, name="picked_scales%d" % a, align_bytes=64) for a in range(FP4_PASSES)]
-        picked_res = [held.tile([P, S], F32, name="picked_res%d" % m) for m in range(TILES)]
+        picked_res = held.tile([P, TILES, S], F32, name="picked_res")
 
         def gather_words(a):
             nc.vector.tensor_copy(picked_words[a][:], word_tables[a][:].indirect(offsets[:]))
 
         def gather_residual(m):
-            nc.vector.tensor_copy(picked_res[m][:], residuals[m][:].indirect(offsets[:]))
+            nc.vector.tensor_copy(picked_res[:, m, :], residuals[m][:].indirect(offsets[:]))
 
         w8_codes = held.tile([P, M], U32, name="w8_codes", align_bytes=64)
         w8_plane = held.tile([P, M], U8, name="w8_plane", align_bytes=64)
@@ -137,7 +128,7 @@ def tile_list_tabres_gelu_kernel(tc, tab_words, tab_scales, w8, w4_words, w4_sca
                     in_=w8_grouped[:].rearrange("p n j -> p (n j)"),
                 )
 
-        results = [held.tile([P, S], F32, name="result%d" % m) for m in range(TILES)]
+        results = held.tile([P, TILES, S], F32, name="results")
         w4_scale_bytes = w4_planes[:].bitcast(U8)
         for m in range(TILES):
             rows = slice(m * P, (m + 1) * P)
@@ -163,13 +154,14 @@ def tile_list_tabres_gelu_kernel(tc, tab_words, tab_scales, w8, w4_words, w4_sca
                     start=False,
                     stop=True,
                 )
-                nc.scalar.activation(results[m][:, cols], acc[:], GELU, bias=bias[:, m : m + 1])
+                nc.scalar.activation(results[:, m, cols], acc[:], GELU, bias=bias[:, m : m + 1])
 
-        for m in range(TILES):
-            parts = HALVES if m == TILES - 1 else 1
-            width = S // parts
-            for h in range(parts):
-                cols = slice(h * width, (h + 1) * width)
-                engine = nc.gpsimd if m < POOL_TILES else nc.vector
-                engine.tensor_tensor(results[m][:, cols], results[m][:, cols], picked_res[m][:, cols], ADD)
-                nc.sync.dma_start(out=out[m * P : (m + 1) * P, cols], in_=results[m][:, cols])
+        out_tiles = out.rearrange("(m p) j -> p m j", p=P)
+        for m in range(POOL_TILES):
+            nc.gpsimd.tensor_tensor(results[:, m, :], results[:, m, :], picked_res[:, m, :], ADD)
+            nc.sync.dma_start(out=out_tiles[:, m, :], in_=results[:, m, :])
+        last = slice(POOL_TILES, TILES)
+        for h in range(HALVES):
+            cols = slice(h * BANK, (h + 1) * BANK)
+            nc.vector.tensor_tensor(results[:, last, cols], results[:, last, cols], picked_res[:, last, cols], ADD)
+            nc.sync.dma_start(out=out_tiles[:, last, cols], in_=results[:, last, cols])

@@ -30,8 +30,6 @@ HALVES = S // BANK
 W8_PARTS = 2
 W8_COLS = M // W8_PARTS
 RING = 11
-QUANTISE_AFTER = 0
-POOL_TILES = 6
 
 
 def tile_list_tabres_gelu_kernel(tc, tab_words, tab_scales, w8, w4_words, w4_scales, rT, b, offs, out):
@@ -101,13 +99,9 @@ def tile_list_tabres_gelu_kernel(tc, tab_words, tab_scales, w8, w4_words, w4_sca
 
         picked_words = [held.tile([P, S], U32, name="picked_words%d" % a, align_bytes=64) for a in range(PASSES)]
         picked_scales = [held.tile([P, S], U8, name="picked_scales%d" % a, align_bytes=64) for a in range(FP4_PASSES)]
-        picked_res = held.tile([P, TILES, S], F32, name="picked_res")
 
         def gather_words(a):
             nc.vector.tensor_copy(picked_words[a][:], word_tables[a][:].indirect(offsets[:]))
-
-        def gather_residual(m):
-            nc.vector.tensor_copy(picked_res[:, m, :], residuals[m][:].indirect(offsets[:]))
 
         w8_codes = held.tile([P, M], U32, name="w8_codes", align_bytes=64)
         w8_plane = held.tile([P, M], U8, name="w8_plane", align_bytes=64)
@@ -119,14 +113,11 @@ def tile_list_tabres_gelu_kernel(tc, tab_words, tab_scales, w8, w4_words, w4_sca
             gather_words(a)
         for a in range(FP4_PASSES):
             nc.vector.tensor_copy(picked_scales[a][:], scale_tables[:, a, :].bitcast(U8).indirect(offsets[:]))
-        for m in range(TILES):
-            gather_residual(m)
-            if m == QUANTISE_AFTER:
-                nc.vector.quantize_mx(
-                    out=w8_codes[:].bitcast(FP8X4),
-                    scales=w8_plane[:],
-                    in_=w8_grouped[:].rearrange("p n j -> p (n j)"),
-                )
+        nc.vector.quantize_mx(
+            out=w8_codes[:].bitcast(FP8X4),
+            scales=w8_plane[:],
+            in_=w8_grouped[:].rearrange("p n j -> p (n j)"),
+        )
 
         results = held.tile([P, TILES, S], F32, name="results")
         w4_scale_bytes = w4_planes[:].bitcast(U8)
@@ -157,11 +148,13 @@ def tile_list_tabres_gelu_kernel(tc, tab_words, tab_scales, w8, w4_words, w4_sca
                 nc.scalar.activation(results[:, m, cols], acc[:], GELU, bias=bias[:, m : m + 1])
 
         out_tiles = out.rearrange("(m p) j -> p m j", p=P)
-        for m in range(POOL_TILES):
-            nc.gpsimd.tensor_tensor(results[:, m, :], results[:, m, :], picked_res[:, m, :], ADD)
-            nc.sync.dma_start(out=out_tiles[:, m, :], in_=results[:, m, :])
-        last = slice(POOL_TILES, TILES)
+        summed = held.tile([P, TILES, S], F32, name="summed")
+        for m in range(TILES - 1):
+            nc.vector.tensor_tensor(summed[:, m, :], residuals[m][:].indirect(offsets[:]), results[:, m, :], ADD)
+            nc.sync.dma_start(out=out_tiles[:, m, :], in_=summed[:, m, :])
+        last = TILES - 1
         for h in range(HALVES):
             cols = slice(h * BANK, (h + 1) * BANK)
-            nc.vector.tensor_tensor(results[:, last, cols], results[:, last, cols], picked_res[:, last, cols], ADD)
-            nc.sync.dma_start(out=out_tiles[:, last, cols], in_=results[:, last, cols])
+            entries = offsets[:, h * BANK // 16 : (h + 1) * BANK // 16]
+            nc.vector.tensor_tensor(summed[:, last, cols], residuals[last][:].indirect(entries), results[:, last, cols], ADD)
+            nc.sync.dma_start(out=out_tiles[:, last, cols], in_=summed[:, last, cols])

@@ -21,140 +21,145 @@ P = 128
 PACK = 4
 PASSES = K // (P * PACK)
 FP4_PASSES = PASSES - 1
-QUADS = 4
 QUAD = 32
 ROWS = 4
 BANK = 512
 TILES = M // P
 HALVES = S // BANK
+LIST_ROWS = 16
 W8_PARTS = 2
 W8_COLS = M // W8_PARTS
-RING = 11
 
 
 def tile_list_tabres_gelu_kernel(tc, tab_words, tab_scales, w8, w4_words, w4_scales, rT, b, offs, out):
     nc = tc.nc
     with ExitStack() as ctx:
         held = ctx.enter_context(tc.tile_pool(name="held", bufs=1))
-        ring = ctx.enter_context(tc.tile_pool(name="ring", bufs=RING))
-        psum = ctx.enter_context(tc.psum_pool(name="psum", bufs=6))
+        reused = ctx.enter_context(tc.tile_pool(name="reused", bufs=1))
+        psum = ctx.enter_context(tc.psum_pool(name="psum", bufs=7))
         psum_b = ctx.enter_context(tc.psum_pool(name="psum_b", bufs=1))
 
-        offsets = held.tile([P, S // 16], U16, name="offsets")
+        offsets = held.tile([P, S // LIST_ROWS], U16, name="offsets")
         nc.sync.dma_start(offsets[:], offs)
 
-        scale_tables = held.tile([P, FP4_PASSES, T // 4], I32, name="scale_tables", align_bytes=64)
+        def entries(h):
+            return offsets[:, h * BANK // LIST_ROWS : (h + 1) * BANK // LIST_ROWS]
+
+        scale_tables = reused.tile([P, PASSES, T // 4], I32, name="scale_tables", align_bytes=64, offset=0)
         w4_planes = held.tile([P, FP4_PASSES, M // 4], I32, name="w4_planes", align_bytes=64)
-        nc.vector.memset(scale_tables[:, 0, :], 0)
-        nc.gpsimd.memset(scale_tables[:, 1, :], 0)
+        bias_rows = held.tile([P, P], F32, name="bias_rows")
+        warm = held.tile([P, 1], F32, name="warm")
+        identity = held.tile([P, P], F32, name="identity")
+        nc.vector.memset(scale_tables[:], 0)
         nc.vector.memset(w4_planes[:], 0)
-
-        word_tables = []
-        residuals = []
-        w8_raw = [held.tile([P, PACK, W8_COLS], F32, name="w8_raw%d" % h) for h in range(W8_PARTS)]
-        w4_codes = held.tile([P, FP4_PASSES, 2 * M], U8, name="w4_codes", align_bytes=64)
-
-        def load_words(a):
-            word_tables.append(ring.tile([P, T], U32, name="window", align_bytes=64))
-            nc.sync.dma_start(out=word_tables[a][:].bitcast(I32), in_=tab_words[a].rearrange("p t i -> p (t i)").bitcast(I32))
-
-        def load_residual(m):
-            residuals.append(ring.tile([P, T], F32, name="window", align_bytes=64))
-            nc.sync.dma_start(out=residuals[m][:], in_=rT[m * P : (m + 1) * P, :])
-
-        def load_w8(h):
-            nc.sync.dma_start(out=w8_raw[h][:], in_=w8[:, h * W8_COLS : (h + 1) * W8_COLS].rearrange("(p j) n -> p j n", j=PACK))
+        nc.vector.memset(bias_rows[:], 0.0)
+        nc.vector.memset(warm[:], 0.0)
+        make_identity(nc, identity[:])
 
         table_rows = tab_scales.bitcast(I32).rearrange("a (q r) t -> r q a t", r=ROWS)
+        for r in range(ROWS):
+            nc.gpsimd.dma_start(out=scale_tables[r:P:QUAD, :, :], in_=table_rows[r])
+
+        word_tables = [held.tile([P, T], U32, name="word_table%d" % a, align_bytes=64) for a in range(PASSES)]
+        residuals = [held.tile([P, T], F32, name="residual%d" % m, align_bytes=64) for m in range(TILES)]
+        w8_raw = held.tile([P, PACK, M], F32, name="w8_raw")
+        w4_codes = held.tile([P, FP4_PASSES, 2 * M], U8, name="w4_codes", align_bytes=64)
+
+        def load_words(a, cols):
+            words = tab_words[a].rearrange("p t i -> p (t i)").bitcast(I32)
+            nc.sync.dma_start(out=word_tables[a][:, cols].bitcast(I32), in_=words[:, cols])
+
+        load_words(0, slice(0, T // 2))
+        load_words(0, slice(T // 2, T))
+
         w4_rows = w4_scales.bitcast(I32).rearrange("a (q r) n -> r q a n", r=ROWS)
         for r in range(ROWS):
-            nc.gpsimd.dma_start(out=scale_tables[r:P:QUAD, :, :], in_=table_rows[r][:, 1:PASSES, :])
-        for r in range(ROWS):
-            nc.gpsimd.dma_start(out=scale_tables[ROWS + r : P : QUAD, 0, :], in_=table_rows[r][:, 0, :])
-        for r in range(ROWS):
-            nc.gpsimd.dma_start(out=w4_planes[r:P:QUAD, :, :], in_=w4_rows[r])
-        bias_rows = held.tile([P, P], F32, name="bias_rows")
-        nc.vector.memset(bias_rows[:], 0.0)
-        nc.gpsimd.dma_start(out=bias_rows[0:TILES, :], in_=b.rearrange("(m p) -> m p", p=P))
+            nc.scalar.dma_start(out=w4_planes[r:P:QUAD, :, :], in_=w4_rows[r])
+        nc.scalar.dma_start(out=bias_rows[0:TILES, :], in_=b.rearrange("(m p) -> m p", p=P))
 
-        for a in range(PASSES):
-            load_words(a)
-        load_residual(0)
-        load_w8(0)
-        load_w8(1)
+        load_words(1, slice(0, T))
+        nc.sync.dma_start(out=w8_raw[:], in_=w8.rearrange("(p j) n -> p j n", j=PACK))
+        load_words(2, slice(0, T))
         nc.sync.dma_start(out=w4_codes[:].bitcast(I32), in_=w4_words.rearrange("a p n -> p a n").bitcast(I32))
-        for m in range(1, TILES):
-            load_residual(m)
+        for m in range(TILES):
+            nc.sync.dma_start(out=residuals[m][:], in_=rT[m * P : (m + 1) * P, :])
 
-        warm = held.tile([P, 1], F32, name="warm")
-        nc.vector.memset(warm[:], 0.0)
         nc.scalar.activation(warm[:], warm[:], GELU)
 
-        identity = held.tile([P, P], F32, name="identity")
-        make_identity(nc, identity[:])
         bias_psum = psum_b.tile([P, P], F32, name="bias_psum")
         nc.tensor.transpose(bias_psum[:], bias_rows[:], identity[:])
         bias = held.tile([P, TILES], F32, name="bias")
         nc.scalar.copy(bias[:], bias_psum[:, 0:TILES])
 
-        picked_words = [held.tile([P, S], U32, name="picked_words%d" % a, align_bytes=64) for a in range(PASSES)]
-        picked_scales = [held.tile([P, S], U8, name="picked_scales%d" % a, align_bytes=64) for a in range(FP4_PASSES)]
-
-        def gather_words(a):
-            nc.vector.tensor_copy(picked_words[a][:], word_tables[a][:].indirect(offsets[:]))
-
-        w8_codes = held.tile([P, M], U32, name="w8_codes", align_bytes=64)
-        w8_plane = held.tile([P, M], U8, name="w8_plane", align_bytes=64)
         w8_grouped = held.tile([P, M, PACK], BF16, name="w8_grouped", align_bytes=64)
-        for h in range(W8_PARTS):
-            nc.scalar.copy(w8_grouped[:, h * W8_COLS : (h + 1) * W8_COLS, :], w8_raw[h][:].rearrange("p j n -> p n j"))
+        for part in range(W8_PARTS):
+            cols = slice(part * W8_COLS, (part + 1) * W8_COLS)
+            nc.scalar.copy(
+                w8_grouped[:, cols, :].rearrange("p (c i) j -> p c j i", i=4),
+                w8_raw[:, :, cols].rearrange("p j (c i) -> p c j i", i=4),
+            )
 
+        picked_words = [held.tile([P, S], U32, name="picked_words%d" % a, align_bytes=64) for a in range(PASSES - 1)]
+        picked_scales = [held.tile([P, S], U8, name="picked_scales%d" % a, align_bytes=64) for a in range(PASSES)]
+        for a in range(PASSES - 1):
+            nc.vector.tensor_copy(picked_words[a][:], word_tables[a][:].indirect(offsets[:]))
         for a in range(PASSES):
-            gather_words(a)
-        for a in range(FP4_PASSES):
             nc.vector.tensor_copy(picked_scales[a][:], scale_tables[:, a, :].bitcast(U8).indirect(offsets[:]))
-        nc.vector.quantize_mx(
-            out=w8_codes[:].bitcast(FP8X4),
-            scales=w8_plane[:],
-            in_=w8_grouped[:].rearrange("p n j -> p (n j)"),
-        )
 
-        results = held.tile([P, TILES, S], F32, name="results")
+        picked_words.append(reused.tile([P, S], U32, name="picked_words_last", align_bytes=64, offset=0))
+        w8_plane = reused.tile([P, M], U8, name="w8_plane", align_bytes=64, offset=4 * S)
+        w8_codes = held.tile([P, M], U32, name="w8_codes", align_bytes=64)
+
+        def quantise(part):
+            cols = slice(part * W8_COLS, (part + 1) * W8_COLS)
+            nc.vector.quantize_mx(
+                out=w8_codes[:, cols].bitcast(FP8X4),
+                scales=w8_plane[:, cols],
+                in_=w8_grouped[:, cols, :].rearrange("p n j -> p (n j)"),
+            )
+
+        quantise(0)
+        for h in range(HALVES):
+            cols = slice(h * BANK, (h + 1) * BANK)
+            nc.vector.tensor_copy(picked_words[PASSES - 1][:, cols], word_tables[PASSES - 1][:].indirect(entries(h)))
+        quantise(1)
+
+        activated = held.tile([P, TILES, S], F32, name="activated")
+        summed = held.tile([P, TILES, S], F32, name="summed")
         w4_scale_bytes = w4_planes[:].bitcast(U8)
+        out_tiles = out.rearrange("(m p) j -> p m j", p=P)
         for m in range(TILES):
             rows = slice(m * P, (m + 1) * P)
             for h in range(HALVES):
                 cols = slice(h * BANK, (h + 1) * BANK)
                 acc = psum.tile([P, BANK], F32, name="acc")
+                nc.tensor.matmul_mx(
+                    out=acc[:],
+                    lhsT=w8_codes[:, rows].bitcast(FP8X4),
+                    lhsT_scale=w8_plane[:, rows],
+                    rhs=picked_words[0][:, cols].bitcast(FP8X4),
+                    rhs_scale=picked_scales[0][:, cols],
+                    start=True,
+                    stop=False,
+                )
                 for a in range(FP4_PASSES):
                     nc.tensor.matmul_mx(
                         out=acc[:],
                         lhsT=w4_codes[:, a, 2 * m * P : 2 * (m + 1) * P].bitcast(FP4X4),
                         lhsT_scale=w4_scale_bytes[:, a, rows],
                         rhs=picked_words[a + 1][:, cols].bitcast(FP8X4),
-                        rhs_scale=picked_scales[a][:, cols],
-                        start=(a == 0),
-                        stop=False,
+                        rhs_scale=picked_scales[a + 1][:, cols],
+                        start=False,
+                        stop=(a == FP4_PASSES - 1),
                     )
-                nc.tensor.matmul_mx(
-                    out=acc[:],
-                    lhsT=w8_codes[:, rows].bitcast(FP8X4),
-                    lhsT_scale=w8_plane[:, rows],
-                    rhs=picked_words[0][:, cols].bitcast(FP8X4),
-                    rhs_scale=picked_scales[0][ROWS:P, cols],
-                    start=False,
-                    stop=True,
-                )
-                nc.scalar.activation(results[:, m, cols], acc[:], GELU, bias=bias[:, m : m + 1])
-
-        out_tiles = out.rearrange("(m p) j -> p m j", p=P)
-        summed = held.tile([P, TILES, S], F32, name="summed")
-        for m in range(TILES - 1):
-            nc.vector.tensor_tensor(summed[:, m, :], residuals[m][:].indirect(offsets[:]), results[:, m, :], ADD)
-            nc.sync.dma_start(out=out_tiles[:, m, :], in_=summed[:, m, :])
-        last = TILES - 1
-        for h in range(HALVES):
-            cols = slice(h * BANK, (h + 1) * BANK)
-            entries = offsets[:, h * BANK // 16 : (h + 1) * BANK // 16]
-            nc.vector.tensor_tensor(summed[:, last, cols], residuals[last][:].indirect(entries), results[:, last, cols], ADD)
-            nc.sync.dma_start(out=out_tiles[:, last, cols], in_=summed[:, last, cols])
+                nc.scalar.activation(activated[:, m, cols], acc[:], GELU, bias=bias[:, m : m + 1])
+            if m in (0, TILES - 1):
+                for h in range(HALVES):
+                    cols = slice(h * BANK, (h + 1) * BANK)
+                    nc.vector.tensor_tensor(summed[:, m, cols], residuals[m][:].indirect(entries(h)), activated[:, m, cols], ADD)
+                    if m == TILES - 1:
+                        nc.sync.dma_start(out=out_tiles[:, m, cols], in_=summed[:, m, cols])
+            else:
+                nc.vector.tensor_tensor(summed[:, m, :], residuals[m][:].indirect(offsets[:]), activated[:, m, :], ADD)
+            if m < TILES - 1:
+                nc.sync.dma_start(out=out_tiles[:, m, :], in_=summed[:, m, :])

@@ -27,6 +27,8 @@ BANK = 512
 TILES = M // P
 HALVES = S // BANK
 LIST_ROWS = 16
+MOVED_ROWS = 112
+WINDOWS = 7
 W8_PARTS = 2
 W8_COLS = M // W8_PARTS
 
@@ -36,6 +38,7 @@ def tile_list_tabres_gelu_kernel(tc, tab_words, tab_scales, w8, w4_words, w4_sca
     with ExitStack() as ctx:
         held = ctx.enter_context(tc.tile_pool(name="held", bufs=1))
         reused = ctx.enter_context(tc.tile_pool(name="reused", bufs=1))
+        ring = ctx.enter_context(tc.tile_pool(name="ring", bufs=WINDOWS))
         psum = ctx.enter_context(tc.psum_pool(name="psum", bufs=7))
         psum_b = ctx.enter_context(tc.psum_pool(name="psum_b", bufs=1))
 
@@ -45,23 +48,25 @@ def tile_list_tabres_gelu_kernel(tc, tab_words, tab_scales, w8, w4_words, w4_sca
         def entries(h):
             return offsets[:, h * BANK // LIST_ROWS : (h + 1) * BANK // LIST_ROWS]
 
-        scale_tables = reused.tile([P, PASSES, T // 4], I32, name="scale_tables", align_bytes=64, offset=0)
+        scale_table = reused.tile([P, T // 4], I32, name="scale_table", align_bytes=64, offset=4 * S - T // 4)
+        moved_planes = held.tile([P, FP4_PASSES, S // 4], I32, name="moved_planes", align_bytes=64)
         w4_planes = held.tile([P, FP4_PASSES, M // 4], I32, name="w4_planes", align_bytes=64)
         bias_rows = held.tile([P, P], F32, name="bias_rows")
         warm = held.tile([P, 1], F32, name="warm")
         identity = held.tile([P, P], F32, name="identity")
-        nc.vector.memset(scale_tables[:], 0)
+        nc.vector.memset(scale_table[:], 0)
         nc.vector.memset(w4_planes[:], 0)
+        nc.vector.memset(moved_planes[:], 0)
         nc.vector.memset(bias_rows[:], 0.0)
         nc.vector.memset(warm[:], 0.0)
         make_identity(nc, identity[:])
 
-        table_rows = tab_scales.bitcast(I32).rearrange("a (q r) t -> r q a t", r=ROWS)
-        for r in range(ROWS):
-            nc.gpsimd.dma_start(out=scale_tables[r:P:QUAD, :, :], in_=table_rows[r])
+        table_rows = tab_scales.bitcast(I32)
+        for q in range(P // QUAD):
+            nc.gpsimd.dma_start(out=scale_table[q * QUAD : q * QUAD + PASSES * ROWS, :], in_=table_rows[:, q * ROWS : (q + 1) * ROWS, :])
 
-        word_tables = [held.tile([P, T], U32, name="word_table%d" % a, align_bytes=64) for a in range(PASSES)]
-        residuals = [held.tile([P, T], F32, name="residual%d" % m, align_bytes=64) for m in range(TILES)]
+        word_tables = [ring.tile([P, T], U32, name="window", align_bytes=64) for a in range(PASSES)]
+        residuals = [ring.tile([P, T], F32, name="window", align_bytes=64) for m in range(TILES)]
         w8_raw = held.tile([P, PACK, M], F32, name="w8_raw")
         w4_codes = held.tile([P, FP4_PASSES, 2 * M], U8, name="w4_codes", align_bytes=64)
 
@@ -77,8 +82,8 @@ def tile_list_tabres_gelu_kernel(tc, tab_words, tab_scales, w8, w4_words, w4_sca
             nc.scalar.dma_start(out=w4_planes[r:P:QUAD, :, :], in_=w4_rows[r])
         nc.scalar.dma_start(out=bias_rows[0:TILES, :], in_=b.rearrange("(m p) -> m p", p=P))
 
-        load_words(1, slice(0, T))
         nc.sync.dma_start(out=w8_raw[:], in_=w8.rearrange("(p j) n -> p j n", j=PACK))
+        load_words(1, slice(0, T))
         load_words(2, slice(0, T))
         nc.sync.dma_start(out=w4_codes[:].bitcast(I32), in_=w4_words.rearrange("a p n -> p a n").bitcast(I32))
         for m in range(TILES):
@@ -99,15 +104,18 @@ def tile_list_tabres_gelu_kernel(tc, tab_words, tab_scales, w8, w4_words, w4_sca
                 w8_raw[:, :, cols].rearrange("p j (c i) -> p c j i", i=4),
             )
 
-        picked_words = [held.tile([P, S], U32, name="picked_words%d" % a, align_bytes=64) for a in range(PASSES - 1)]
-        picked_scales = [held.tile([P, S], U8, name="picked_scales%d" % a, align_bytes=64) for a in range(PASSES)]
-        for a in range(PASSES - 1):
-            nc.vector.tensor_copy(picked_words[a][:], word_tables[a][:].indirect(offsets[:]))
-        for a in range(PASSES):
-            nc.vector.tensor_copy(picked_scales[a][:], scale_tables[:, a, :].bitcast(U8).indirect(offsets[:]))
+        picked_words = [held.tile([P, S], U32, name="picked_words0", align_bytes=64)]
+        picked_scales = held.tile([P, S], U8, name="picked_scales", align_bytes=64)
+        nc.vector.tensor_copy(picked_words[0][:], word_tables[0][:].indirect(offsets[:]))
+        nc.vector.tensor_copy(picked_scales[:], scale_table[:].bitcast(U8).indirect(offsets[:]))
+        for a in range(FP4_PASSES):
+            first = (a + 1) * ROWS
+            nc.scalar.dma_start(out=moved_planes[0:MOVED_ROWS, a, :], in_=picked_scales[first : first + MOVED_ROWS, :].bitcast(I32))
 
-        picked_words.append(reused.tile([P, S], U32, name="picked_words_last", align_bytes=64, offset=0))
+        picked_words.append(reused.tile([P, S], U32, name="picked_words1", align_bytes=64, offset=0))
         w8_plane = reused.tile([P, M], U8, name="w8_plane", align_bytes=64, offset=4 * S)
+        picked_words.append(reused.tile([P, S], U32, name="picked_words2", align_bytes=64, offset=4 * S + M))
+        nc.vector.tensor_copy(picked_words[1][:], word_tables[1][:].indirect(offsets[:]))
         w8_codes = held.tile([P, M], U32, name="w8_codes", align_bytes=64)
 
         def quantise(part):
@@ -127,6 +135,7 @@ def tile_list_tabres_gelu_kernel(tc, tab_words, tab_scales, w8, w4_words, w4_sca
         activated = held.tile([P, TILES, S], F32, name="activated")
         summed = held.tile([P, TILES, S], F32, name="summed")
         w4_scale_bytes = w4_planes[:].bitcast(U8)
+        moved_bytes = moved_planes[:].bitcast(U8)
         out_tiles = out.rearrange("(m p) j -> p m j", p=P)
         for m in range(TILES):
             rows = slice(m * P, (m + 1) * P)
@@ -138,7 +147,7 @@ def tile_list_tabres_gelu_kernel(tc, tab_words, tab_scales, w8, w4_words, w4_sca
                     lhsT=w8_codes[:, rows].bitcast(FP8X4),
                     lhsT_scale=w8_plane[:, rows],
                     rhs=picked_words[0][:, cols].bitcast(FP8X4),
-                    rhs_scale=picked_scales[0][:, cols],
+                    rhs_scale=picked_scales[:, cols],
                     start=True,
                     stop=False,
                 )
@@ -148,7 +157,7 @@ def tile_list_tabres_gelu_kernel(tc, tab_words, tab_scales, w8, w4_words, w4_sca
                         lhsT=w4_codes[:, a, 2 * m * P : 2 * (m + 1) * P].bitcast(FP4X4),
                         lhsT_scale=w4_scale_bytes[:, a, rows],
                         rhs=picked_words[a + 1][:, cols].bitcast(FP8X4),
-                        rhs_scale=picked_scales[a + 1][:, cols],
+                        rhs_scale=moved_bytes[:, a, cols],
                         start=False,
                         stop=(a == FP4_PASSES - 1),
                     )

@@ -28,7 +28,9 @@ TILES = M // P
 HALVES = S // BANK
 LIST_ROWS = 16
 MOVED_ROWS = 112
-WINDOWS = 7
+WINDOWS = 4
+BLOCKS = BANK // P
+TURNED = range(1, 5)
 W8_PARTS = 2
 W8_COLS = M // W8_PARTS
 
@@ -39,16 +41,14 @@ def tile_list_tabres_gelu_kernel(tc, tab_words, tab_scales, w8, w4_words, w4_sca
         held = ctx.enter_context(tc.tile_pool(name="held", bufs=1))
         reused = ctx.enter_context(tc.tile_pool(name="reused", bufs=1))
         ring = ctx.enter_context(tc.tile_pool(name="ring", bufs=WINDOWS))
-        psum = ctx.enter_context(tc.psum_pool(name="psum", bufs=7))
-        psum_b = ctx.enter_context(tc.psum_pool(name="psum_b", bufs=1))
+        pair = ctx.enter_context(tc.tile_pool(name="pair", bufs=2))
+        psum = ctx.enter_context(tc.psum_pool(name="psum", bufs=8))
 
         offsets = held.tile([P, S // LIST_ROWS], U16, name="offsets")
         nc.sync.dma_start(offsets[:], offs)
 
-        def entries(h):
-            return offsets[:, h * BANK // LIST_ROWS : (h + 1) * BANK // LIST_ROWS]
-
-        scale_table = reused.tile([P, T // 4], I32, name="scale_table", align_bytes=64, offset=4 * S - T // 4)
+        w8_half_bytes = 4 * PACK * W8_COLS
+        scale_table = reused.tile([P, T // 4], I32, name="scale_table", align_bytes=64, offset=w8_half_bytes - T // 2)
         moved_planes = held.tile([P, FP4_PASSES, S // 4], I32, name="moved_planes", align_bytes=64)
         w4_planes = held.tile([P, FP4_PASSES, M // 4], I32, name="w4_planes", align_bytes=64)
         bias_rows = held.tile([P, P], F32, name="bias_rows")
@@ -65,58 +65,30 @@ def tile_list_tabres_gelu_kernel(tc, tab_words, tab_scales, w8, w4_words, w4_sca
         for q in range(P // QUAD):
             nc.gpsimd.dma_start(out=scale_table[q * QUAD : q * QUAD + PASSES * ROWS, :], in_=table_rows[:, q * ROWS : (q + 1) * ROWS, :])
 
-        word_tables = [ring.tile([P, T], U32, name="window", align_bytes=64) for a in range(PASSES)]
-        residuals = [ring.tile([P, T], F32, name="window", align_bytes=64) for m in range(TILES)]
-        w8_raw = held.tile([P, PACK, M], F32, name="w8_raw")
+        word_tables = [held.tile([P, T], U32, name="word_table0", align_bytes=64)]
+        word_tables.extend(ring.tile([P, T], U32, name="window", align_bytes=64) for a in range(1, PASSES))
         w4_codes = held.tile([P, FP4_PASSES, 2 * M], U8, name="w4_codes", align_bytes=64)
+        w8_grouped = held.tile([P, M, PACK], BF16, name="w8_grouped", align_bytes=64)
+        w8_codes = held.tile([P, M], U32, name="w8_codes", align_bytes=64)
+        w8_plane = held.tile([P, M], U8, name="w8_plane", align_bytes=64)
+        residuals = []
 
         def load_words(a, cols):
             words = tab_words[a].rearrange("p t i -> p (t i)").bitcast(I32)
             nc.sync.dma_start(out=word_tables[a][:, cols].bitcast(I32), in_=words[:, cols])
 
-        load_words(0, slice(0, T // 2))
-        load_words(0, slice(T // 2, T))
-
-        w4_rows = w4_scales.bitcast(I32).rearrange("a (q r) n -> r q a n", r=ROWS)
-        for r in range(ROWS):
-            nc.scalar.dma_start(out=w4_planes[r:P:QUAD, :, :], in_=w4_rows[r])
-        nc.scalar.dma_start(out=bias_rows[0:TILES, :], in_=b.rearrange("(m p) -> m p", p=P))
-
-        nc.sync.dma_start(out=w8_raw[:], in_=w8.rearrange("(p j) n -> p j n", j=PACK))
-        load_words(1, slice(0, T))
-        load_words(2, slice(0, T))
-        nc.sync.dma_start(out=w4_codes[:].bitcast(I32), in_=w4_words.rearrange("a p n -> p a n").bitcast(I32))
-        for m in range(TILES):
+        def load_residual():
+            m = len(residuals)
+            residuals.append(ring.tile([P, T], F32, name="window", align_bytes=64))
             nc.sync.dma_start(out=residuals[m][:], in_=rT[m * P : (m + 1) * P, :])
 
-        nc.scalar.activation(warm[:], warm[:], GELU)
-
-        bias_psum = psum_b.tile([P, P], F32, name="bias_psum")
-        nc.tensor.transpose(bias_psum[:], bias_rows[:], identity[:])
-        bias = held.tile([P, TILES], F32, name="bias")
-        nc.scalar.copy(bias[:], bias_psum[:, 0:TILES])
-
-        w8_grouped = held.tile([P, M, PACK], BF16, name="w8_grouped", align_bytes=64)
-        for part in range(W8_PARTS):
+        def load_and_group_w8(part, raw):
             cols = slice(part * W8_COLS, (part + 1) * W8_COLS)
+            nc.sync.dma_start(out=raw[:], in_=w8[:, cols].rearrange("(p j) n -> p j n", j=PACK))
             nc.scalar.copy(
                 w8_grouped[:, cols, :].rearrange("p (c i) j -> p c j i", i=4),
-                w8_raw[:, :, cols].rearrange("p j (c i) -> p c j i", i=4),
+                raw[:].rearrange("p j (c i) -> p c j i", i=4),
             )
-
-        picked_words = [held.tile([P, S], U32, name="picked_words0", align_bytes=64)]
-        picked_scales = held.tile([P, S], U8, name="picked_scales", align_bytes=64)
-        nc.vector.tensor_copy(picked_words[0][:], word_tables[0][:].indirect(offsets[:]))
-        nc.vector.tensor_copy(picked_scales[:], scale_table[:].bitcast(U8).indirect(offsets[:]))
-        for a in range(FP4_PASSES):
-            first = (a + 1) * ROWS
-            nc.scalar.dma_start(out=moved_planes[0:MOVED_ROWS, a, :], in_=picked_scales[first : first + MOVED_ROWS, :].bitcast(I32))
-
-        picked_words.append(reused.tile([P, S], U32, name="picked_words1", align_bytes=64, offset=0))
-        w8_plane = reused.tile([P, M], U8, name="w8_plane", align_bytes=64, offset=4 * S)
-        picked_words.append(reused.tile([P, S], U32, name="picked_words2", align_bytes=64, offset=4 * S + M))
-        nc.vector.tensor_copy(picked_words[1][:], word_tables[1][:].indirect(offsets[:]))
-        w8_codes = held.tile([P, M], U32, name="w8_codes", align_bytes=64)
 
         def quantise(part):
             cols = slice(part * W8_COLS, (part + 1) * W8_COLS)
@@ -126,10 +98,48 @@ def tile_list_tabres_gelu_kernel(tc, tab_words, tab_scales, w8, w4_words, w4_sca
                 in_=w8_grouped[:, cols, :].rearrange("p n j -> p (n j)"),
             )
 
+        for a in range(2):
+            load_words(a, slice(0, T // 2))
+            load_words(a, slice(T // 2, T))
+
+        w4_rows = w4_scales.bitcast(I32).rearrange("a (q r) n -> r q a n", r=ROWS)
+        for r in range(ROWS):
+            nc.scalar.dma_start(out=w4_planes[r:P:QUAD, :, :], in_=w4_rows[r])
+        nc.scalar.dma_start(out=bias_rows[0:TILES, :], in_=b.rearrange("(m p) -> m p", p=P))
+        nc.scalar.activation(warm[:], warm[:], GELU)
+
+        bias_psum = psum.tile([P, BANK], F32, name="bank")
+        nc.tensor.transpose(bias_psum[:, 0:P], bias_rows[:], identity[:])
+        bias = held.tile([P, TILES], F32, name="bias")
+        nc.scalar.copy(bias[:], bias_psum[:, 0:TILES])
+
+        picked_words = [held.tile([P, S], U32, name="picked_words0", align_bytes=64)]
+        picked_scales = held.tile([P, S], U8, name="picked_scales", align_bytes=64)
+        nc.vector.tensor_copy(picked_words[0][:], word_tables[0][:].indirect(offsets[:]))
+        nc.vector.tensor_copy(picked_scales[:], scale_table[:].bitcast(U8).indirect(offsets[:]))
+        for a in range(FP4_PASSES):
+            first = (a + 1) * ROWS
+            nc.sync.dma_start(out=moved_planes[0:MOVED_ROWS, a, :], in_=picked_scales[first : first + MOVED_ROWS, :].bitcast(I32))
+
+        load_words(2, slice(0, T))
+        load_and_group_w8(0, ring.tile([P, PACK, W8_COLS], F32, name="window", align_bytes=64))
+        nc.sync.dma_start(out=w4_codes[:].bitcast(I32), in_=w4_words.rearrange("a p n -> p a n").bitcast(I32))
+        load_residual()
+        load_and_group_w8(1, reused.tile([P, PACK, W8_COLS], F32, name="w8_second_half", align_bytes=64, offset=0))
+        for m in range(1, TILES):
+            load_residual()
+
+        picked_words.append(reused.tile([P, S], U32, name="picked_words1", align_bytes=64, offset=w8_half_bytes))
+        picked_words.append(held.tile([P, S], U32, name="picked_words2", align_bytes=64))
+        for a in range(1, PASSES):
+            nc.vector.tensor_copy(picked_words[a][:], word_tables[a][:].indirect(offsets[:]))
         quantise(0)
-        for h in range(HALVES):
-            cols = slice(h * BANK, (h + 1) * BANK)
-            nc.vector.tensor_copy(picked_words[PASSES - 1][:, cols], word_tables[PASSES - 1][:].indirect(entries(h)))
+
+        def gather_residual(m, picked):
+            nc.vector.tensor_copy(picked[:], residuals[m][:].indirect(offsets[:]))
+            return picked
+
+        picked_first = gather_residual(0, held.tile([P, S], F32, name="picked_res%d" % TURNED[0]))
         quantise(1)
 
         activated = held.tile([P, TILES, S], F32, name="activated")
@@ -141,7 +151,7 @@ def tile_list_tabres_gelu_kernel(tc, tab_words, tab_scales, w8, w4_words, w4_sca
             rows = slice(m * P, (m + 1) * P)
             for h in range(HALVES):
                 cols = slice(h * BANK, (h + 1) * BANK)
-                acc = psum.tile([P, BANK], F32, name="acc")
+                acc = psum.tile([P, BANK], F32, name="bank")
                 nc.tensor.matmul_mx(
                     out=acc[:],
                     lhsT=w8_codes[:, rows].bitcast(FP8X4),
@@ -162,13 +172,44 @@ def tile_list_tabres_gelu_kernel(tc, tab_words, tab_scales, w8, w4_words, w4_sca
                         stop=(a == FP4_PASSES - 1),
                     )
                 nc.scalar.activation(activated[:, m, cols], acc[:], GELU, bias=bias[:, m : m + 1])
-            if m in (0, TILES - 1):
-                for h in range(HALVES):
-                    cols = slice(h * BANK, (h + 1) * BANK)
-                    nc.vector.tensor_tensor(summed[:, m, cols], residuals[m][:].indirect(entries(h)), activated[:, m, cols], ADD)
-                    if m == TILES - 1:
-                        nc.sync.dma_start(out=out_tiles[:, m, cols], in_=summed[:, m, cols])
-            else:
-                nc.vector.tensor_tensor(summed[:, m, :], residuals[m][:].indirect(offsets[:]), activated[:, m, :], ADD)
-            if m < TILES - 1:
-                nc.sync.dma_start(out=out_tiles[:, m, :], in_=summed[:, m, :])
+
+        def add_and_store(m, picked, cols):
+            nc.vector.tensor_tensor(summed[:, m, cols], activated[:, m, cols], picked[:, cols], ADD)
+            nc.sync.dma_start(out=out_tiles[:, m, cols], in_=summed[:, m, cols])
+
+        def add_by_transposes(m, picked):
+            turned = pair.tile([P, S], F32, name="turned")
+            for h in range(HALVES):
+                sums = psum.tile([P, BANK], F32, name="bank")
+                for c in range(BLOCKS):
+                    block = slice(h * BANK + c * P, h * BANK + (c + 1) * P)
+                    for first, term in ((True, activated[:, m, block]), (False, picked[:, block])):
+                        nc.tensor.matmul(sums[:, c * P : (c + 1) * P], lhsT=term, rhs=identity[:], start=first, stop=not first, is_transpose=True)
+                nc.scalar.copy(turned[:, h * BANK : (h + 1) * BANK], sums[:])
+            return turned
+
+        def turn_back_and_store(m, turned):
+            for h in range(HALVES):
+                back = psum.tile([P, BANK], F32, name="bank")
+                for c in range(BLOCKS):
+                    nc.tensor.transpose(back[:, c * P : (c + 1) * P], turned[:, h * BANK + c * P : h * BANK + (c + 1) * P], identity[:])
+                nc.scalar.copy(summed[:, m, h * BANK : (h + 1) * BANK], back[:])
+            nc.sync.dma_start(out=out_tiles[:, m, :], in_=summed[:, m, :])
+
+        add_and_store(0, picked_first, slice(0, S))
+
+        picked_turned = {m: gather_residual(m, held.tile([P, S], F32, name="picked_res%d" % m)) for m in TURNED}
+        turned = {}
+        for m in TURNED:
+            turned[m] = add_by_transposes(m, picked_turned[m])
+            if m - 1 in turned:
+                turn_back_and_store(m - 1, turned[m - 1])
+        turn_back_and_store(TURNED[-1], turned[TURNED[-1]])
+
+        picked = gather_residual(TURNED[-1] + 1, pair.tile([P, S], F32, name="picked_late"))
+        for m in range(TURNED[-1] + 1, TILES - 1):
+            following = gather_residual(m + 1, pair.tile([P, S], F32, name="picked_late"))
+            add_and_store(m, picked, slice(0, S))
+            picked = following
+        for h in range(HALVES):
+            add_and_store(TILES - 1, picked, slice(h * BANK, (h + 1) * BANK))

@@ -29,8 +29,6 @@ HALVES = S // BANK
 LIST_ROWS = 16
 MOVED_ROWS = 112
 WINDOWS = 4
-BLOCKS = BANK // P
-TURNED = range(1, 5)
 W8_PARTS = 2
 W8_COLS = M // W8_PARTS
 
@@ -41,7 +39,6 @@ def tile_list_tabres_gelu_kernel(tc, tab_words, tab_scales, w8, w4_words, w4_sca
         held = ctx.enter_context(tc.tile_pool(name="held", bufs=1))
         reused = ctx.enter_context(tc.tile_pool(name="reused", bufs=1))
         ring = ctx.enter_context(tc.tile_pool(name="ring", bufs=WINDOWS))
-        pair = ctx.enter_context(tc.tile_pool(name="pair", bufs=2))
         psum = ctx.enter_context(tc.psum_pool(name="psum", bufs=8))
 
         offsets = held.tile([P, S // LIST_ROWS], U16, name="offsets")
@@ -60,10 +57,6 @@ def tile_list_tabres_gelu_kernel(tc, tab_words, tab_scales, w8, w4_words, w4_sca
         nc.vector.memset(bias_rows[:], 0.0)
         nc.vector.memset(warm[:], 0.0)
         make_identity(nc, identity[:])
-
-        table_rows = tab_scales.bitcast(I32)
-        for q in range(P // QUAD):
-            nc.gpsimd.dma_start(out=scale_table[q * QUAD : q * QUAD + PASSES * ROWS, :], in_=table_rows[:, q * ROWS : (q + 1) * ROWS, :])
 
         word_tables = [held.tile([P, T], U32, name="word_table0", align_bytes=64)]
         word_tables.extend(ring.tile([P, T], U32, name="window", align_bytes=64) for a in range(1, PASSES))
@@ -102,16 +95,10 @@ def tile_list_tabres_gelu_kernel(tc, tab_words, tab_scales, w8, w4_words, w4_sca
             load_words(a, slice(0, T // 2))
             load_words(a, slice(T // 2, T))
 
-        w4_rows = w4_scales.bitcast(I32).rearrange("a (q r) n -> r q a n", r=ROWS)
-        for r in range(ROWS):
-            nc.scalar.dma_start(out=w4_planes[r:P:QUAD, :, :], in_=w4_rows[r])
-        nc.scalar.dma_start(out=bias_rows[0:TILES, :], in_=b.rearrange("(m p) -> m p", p=P))
+        table_rows = tab_scales.bitcast(I32)
+        for q in range(P // QUAD):
+            nc.sync.dma_start(out=scale_table[q * QUAD : q * QUAD + PASSES * ROWS, :], in_=table_rows[:, q * ROWS : (q + 1) * ROWS, :])
         nc.scalar.activation(warm[:], warm[:], GELU)
-
-        bias_psum = psum.tile([P, BANK], F32, name="bank")
-        nc.tensor.transpose(bias_psum[:, 0:P], bias_rows[:], identity[:])
-        bias = held.tile([P, TILES], F32, name="bias")
-        nc.scalar.copy(bias[:], bias_psum[:, 0:TILES])
 
         picked_words = [held.tile([P, S], U32, name="picked_words0", align_bytes=64)]
         picked_scales = held.tile([P, S], U8, name="picked_scales", align_bytes=64)
@@ -123,6 +110,14 @@ def tile_list_tabres_gelu_kernel(tc, tab_words, tab_scales, w8, w4_words, w4_sca
 
         load_words(2, slice(0, T))
         load_and_group_w8(0, ring.tile([P, PACK, W8_COLS], F32, name="window", align_bytes=64))
+        w4_rows = w4_scales.bitcast(I32).rearrange("a (q r) n -> r q a n", r=ROWS)
+        for r in range(ROWS):
+            nc.sync.dma_start(out=w4_planes[r:P:QUAD, :, :], in_=w4_rows[r])
+        nc.sync.dma_start(out=bias_rows[0:TILES, :], in_=b.rearrange("(m p) -> m p", p=P))
+        bias_psum = psum.tile([P, BANK], F32, name="bank")
+        nc.tensor.transpose(bias_psum[:, 0:P], bias_rows[:], identity[:])
+        bias = held.tile([P, TILES], F32, name="bias")
+        nc.scalar.copy(bias[:], bias_psum[:, 0:TILES])
         nc.sync.dma_start(out=w4_codes[:].bitcast(I32), in_=w4_words.rearrange("a p n -> p a n").bitcast(I32))
         load_residual()
         load_and_group_w8(1, reused.tile([P, PACK, W8_COLS], F32, name="w8_second_half", align_bytes=64, offset=0))
@@ -133,14 +128,8 @@ def tile_list_tabres_gelu_kernel(tc, tab_words, tab_scales, w8, w4_words, w4_sca
         picked_words.append(held.tile([P, S], U32, name="picked_words2", align_bytes=64))
         for a in range(1, PASSES):
             nc.vector.tensor_copy(picked_words[a][:], word_tables[a][:].indirect(offsets[:]))
-        quantise(0)
-
-        def gather_residual(m, picked):
-            nc.vector.tensor_copy(picked[:], residuals[m][:].indirect(offsets[:]))
-            return picked
-
-        picked_first = gather_residual(0, held.tile([P, S], F32, name="picked_res%d" % TURNED[0]))
-        quantise(1)
+        for part in range(W8_PARTS):
+            quantise(part)
 
         activated = held.tile([P, TILES, S], F32, name="activated")
         summed = held.tile([P, TILES, S], F32, name="summed")
@@ -172,44 +161,11 @@ def tile_list_tabres_gelu_kernel(tc, tab_words, tab_scales, w8, w4_words, w4_sca
                         stop=(a == FP4_PASSES - 1),
                     )
                 nc.scalar.activation(activated[:, m, cols], acc[:], GELU, bias=bias[:, m : m + 1])
-
-        def add_and_store(m, picked, cols):
-            nc.vector.tensor_tensor(summed[:, m, cols], activated[:, m, cols], picked[:, cols], ADD)
-            nc.sync.dma_start(out=out_tiles[:, m, cols], in_=summed[:, m, cols])
-
-        def add_by_transposes(m, picked):
-            turned = pair.tile([P, S], F32, name="turned")
-            for h in range(HALVES):
-                sums = psum.tile([P, BANK], F32, name="bank")
-                for c in range(BLOCKS):
-                    block = slice(h * BANK + c * P, h * BANK + (c + 1) * P)
-                    for first, term in ((True, activated[:, m, block]), (False, picked[:, block])):
-                        nc.tensor.matmul(sums[:, c * P : (c + 1) * P], lhsT=term, rhs=identity[:], start=first, stop=not first, is_transpose=True)
-                nc.scalar.copy(turned[:, h * BANK : (h + 1) * BANK], sums[:])
-            return turned
-
-        def turn_back_and_store(m, turned):
-            for h in range(HALVES):
-                back = psum.tile([P, BANK], F32, name="bank")
-                for c in range(BLOCKS):
-                    nc.tensor.transpose(back[:, c * P : (c + 1) * P], turned[:, h * BANK + c * P : h * BANK + (c + 1) * P], identity[:])
-                nc.scalar.copy(summed[:, m, h * BANK : (h + 1) * BANK], back[:])
-            nc.sync.dma_start(out=out_tiles[:, m, :], in_=summed[:, m, :])
-
-        add_and_store(0, picked_first, slice(0, S))
-
-        picked_turned = {m: gather_residual(m, held.tile([P, S], F32, name="picked_res%d" % m)) for m in TURNED}
-        turned = {}
-        for m in TURNED:
-            turned[m] = add_by_transposes(m, picked_turned[m])
-            if m - 1 in turned:
-                turn_back_and_store(m - 1, turned[m - 1])
-        turn_back_and_store(TURNED[-1], turned[TURNED[-1]])
-
-        picked = gather_residual(TURNED[-1] + 1, pair.tile([P, S], F32, name="picked_late"))
-        for m in range(TURNED[-1] + 1, TILES - 1):
-            following = gather_residual(m + 1, pair.tile([P, S], F32, name="picked_late"))
-            add_and_store(m, picked, slice(0, S))
-            picked = following
-        for h in range(HALVES):
-            add_and_store(TILES - 1, picked, slice(h * BANK, (h + 1) * BANK))
+            for h in range(HALVES) if m in (0, TILES - 1) else [None]:
+                cols = slice(0, S) if h is None else slice(h * BANK, (h + 1) * BANK)
+                entries = offsets[:, cols.start // LIST_ROWS : cols.stop // LIST_ROWS]
+                nc.vector.tensor_tensor(summed[:, m, cols], residuals[m][:].indirect(entries), activated[:, m, cols], ADD)
+                if m == TILES - 1:
+                    nc.sync.dma_start(out=out_tiles[:, m, cols], in_=summed[:, m, cols])
+            if m < TILES - 1:
+                nc.sync.dma_start(out=out_tiles[:, m, :], in_=summed[:, m, :])

@@ -31,6 +31,7 @@ MOVED_ROWS = 112
 WINDOWS = 4
 W8_PARTS = 2
 W8_COLS = M // W8_PARTS
+EARLY_TILES = W8_COLS // P
 
 
 def tile_list_tabres_gelu_kernel(tc, tab_words, tab_scales, w8, w4_words, w4_scales, rT, b, offs, out):
@@ -44,14 +45,14 @@ def tile_list_tabres_gelu_kernel(tc, tab_words, tab_scales, w8, w4_words, w4_sca
         offsets = held.tile([P, S // LIST_ROWS], U16, name="offsets")
         nc.sync.dma_start(offsets[:], offs)
 
-        w8_half_bytes = 4 * PACK * W8_COLS
-        scale_table = reused.tile([P, T // 4], I32, name="scale_table", align_bytes=64, offset=w8_half_bytes - T // 2)
+        picked_bytes = 4 * S
+        scale_table = reused.tile([P, T // 4], I32, name="scale_table", align_bytes=64, offset=picked_bytes - T // 4)
         moved_planes = held.tile([P, FP4_PASSES, S // 4], I32, name="moved_planes", align_bytes=64)
         w4_planes = held.tile([P, FP4_PASSES, M // 4], I32, name="w4_planes", align_bytes=64)
         bias_rows = held.tile([P, P], F32, name="bias_rows")
         warm = held.tile([P, 1], F32, name="warm")
         identity = held.tile([P, P], F32, name="identity")
-        nc.vector.memset(scale_table[:], 0)
+        nc.gpsimd.memset(scale_table[:], 0)
         nc.vector.memset(w4_planes[:], 0)
         nc.vector.memset(moved_planes[:], 0)
         nc.vector.memset(bias_rows[:], 0.0)
@@ -61,55 +62,58 @@ def tile_list_tabres_gelu_kernel(tc, tab_words, tab_scales, w8, w4_words, w4_sca
         word_tables = [held.tile([P, T], U32, name="word_table0", align_bytes=64)]
         word_tables.extend(ring.tile([P, T], U32, name="window", align_bytes=64) for a in range(1, PASSES))
         w4_codes = held.tile([P, FP4_PASSES, 2 * M], U8, name="w4_codes", align_bytes=64)
-        w8_grouped = held.tile([P, M, PACK], BF16, name="w8_grouped", align_bytes=64)
-        w8_codes = held.tile([P, M], U32, name="w8_codes", align_bytes=64)
-        w8_plane = held.tile([P, M], U8, name="w8_plane", align_bytes=64)
+        w8_grouped = [
+            ring.tile([P, W8_COLS, PACK], BF16, name="window", align_bytes=64),
+            held.tile([P, W8_COLS, PACK], BF16, name="w8_grouped1", align_bytes=64),
+        ]
+        w8_codes = []
+        w8_planes = []
         residuals = []
 
         def load_words(a, cols):
             words = tab_words[a].rearrange("p t i -> p (t i)").bitcast(I32)
             nc.sync.dma_start(out=word_tables[a][:, cols].bitcast(I32), in_=words[:, cols])
 
-        def load_residual():
+        def load_residual(window):
             m = len(residuals)
-            residuals.append(ring.tile([P, T], F32, name="window", align_bytes=64))
-            nc.sync.dma_start(out=residuals[m][:], in_=rT[m * P : (m + 1) * P, :])
+            residuals.append(window)
+            nc.sync.dma_start(out=window[:], in_=rT[m * P : (m + 1) * P, :])
 
-        def load_and_group_w8(part, raw):
+        def load_and_group_w8(part, raw, pieces):
             cols = slice(part * W8_COLS, (part + 1) * W8_COLS)
-            nc.sync.dma_start(out=raw[:], in_=w8[:, cols].rearrange("(p j) n -> p j n", j=PACK))
+            rows = w8[:, cols].rearrange("(p j) n -> p j n", j=PACK)
+            for j in range(0, PACK, PACK // pieces):
+                nc.sync.dma_start(out=raw[:, j : j + PACK // pieces, :], in_=rows[:, j : j + PACK // pieces, :])
             nc.scalar.copy(
-                w8_grouped[:, cols, :].rearrange("p (c i) j -> p c j i", i=4),
+                w8_grouped[part][:].rearrange("p (c i) j -> p c j i", i=4),
                 raw[:].rearrange("p j (c i) -> p c j i", i=4),
             )
 
-        def quantise(part):
-            cols = slice(part * W8_COLS, (part + 1) * W8_COLS)
+        def quantise(part, codes, plane):
+            w8_codes.append(codes)
+            w8_planes.append(plane)
             nc.vector.quantize_mx(
-                out=w8_codes[:, cols].bitcast(FP8X4),
-                scales=w8_plane[:, cols],
-                in_=w8_grouped[:, cols, :].rearrange("p n j -> p (n j)"),
+                out=codes[:].bitcast(FP8X4),
+                scales=plane[:],
+                in_=w8_grouped[part][:].rearrange("p n j -> p (n j)"),
             )
 
-        for a in range(2):
-            load_words(a, slice(0, T // 2))
-            load_words(a, slice(T // 2, T))
+        nc.scalar.activation(warm[:], warm[:], GELU)
+        load_words(0, slice(0, T // 2))
+        load_words(0, slice(T // 2, T))
+        load_and_group_w8(0, ring.tile([P, PACK, W8_COLS], F32, name="window", align_bytes=64), 2)
 
         table_rows = tab_scales.bitcast(I32)
         for q in range(P // QUAD):
             nc.sync.dma_start(out=scale_table[q * QUAD : q * QUAD + PASSES * ROWS, :], in_=table_rows[:, q * ROWS : (q + 1) * ROWS, :])
-        nc.scalar.activation(warm[:], warm[:], GELU)
 
         picked_words = [held.tile([P, S], U32, name="picked_words0", align_bytes=64)]
         picked_scales = held.tile([P, S], U8, name="picked_scales", align_bytes=64)
         nc.vector.tensor_copy(picked_words[0][:], word_tables[0][:].indirect(offsets[:]))
         nc.vector.tensor_copy(picked_scales[:], scale_table[:].bitcast(U8).indirect(offsets[:]))
-        for a in range(FP4_PASSES):
-            first = (a + 1) * ROWS
-            nc.sync.dma_start(out=moved_planes[0:MOVED_ROWS, a, :], in_=picked_scales[first : first + MOVED_ROWS, :].bitcast(I32))
 
-        load_words(2, slice(0, T))
-        load_and_group_w8(0, ring.tile([P, PACK, W8_COLS], F32, name="window", align_bytes=64))
+        load_words(1, slice(0, T))
+        nc.sync.dma_start(out=w4_codes[:].bitcast(I32), in_=w4_words.rearrange("a p n -> p a n").bitcast(I32))
         w4_rows = w4_scales.bitcast(I32).rearrange("a (q r) n -> r q a n", r=ROWS)
         for r in range(ROWS):
             nc.sync.dma_start(out=w4_planes[r:P:QUAD, :, :], in_=w4_rows[r])
@@ -118,54 +122,72 @@ def tile_list_tabres_gelu_kernel(tc, tab_words, tab_scales, w8, w4_words, w4_sca
         nc.tensor.transpose(bias_psum[:, 0:P], bias_rows[:], identity[:])
         bias = held.tile([P, TILES], F32, name="bias")
         nc.scalar.copy(bias[:], bias_psum[:, 0:TILES])
-        nc.sync.dma_start(out=w4_codes[:].bitcast(I32), in_=w4_words.rearrange("a p n -> p a n").bitcast(I32))
-        load_residual()
-        load_and_group_w8(1, reused.tile([P, PACK, W8_COLS], F32, name="w8_second_half", align_bytes=64, offset=0))
-        for m in range(1, TILES):
-            load_residual()
+        load_words(2, slice(0, T))
+        for a in range(FP4_PASSES):
+            first = (a + 1) * ROWS
+            nc.sync.dma_start(out=moved_planes[0:MOVED_ROWS, a, :], in_=picked_scales[first : first + MOVED_ROWS, :].bitcast(I32))
+        load_and_group_w8(1, reused.tile([P, PACK, W8_COLS], F32, name="w8_second_half", align_bytes=64, offset=picked_bytes + W8_COLS), 1)
+        for m in range(TILES):
+            load_residual(ring.tile([P, T], F32, name="window", align_bytes=64))
 
-        picked_words.append(reused.tile([P, S], U32, name="picked_words1", align_bytes=64, offset=w8_half_bytes))
+        quantise(0, held.tile([P, W8_COLS], U32, name="w8_codes0", align_bytes=64), reused.tile([P, W8_COLS], U8, name="w8_plane0", align_bytes=64, offset=picked_bytes))
+        picked_words.append(reused.tile([P, S], U32, name="picked_words1", align_bytes=64, offset=0))
         picked_words.append(held.tile([P, S], U32, name="picked_words2", align_bytes=64))
         for a in range(1, PASSES):
             nc.vector.tensor_copy(picked_words[a][:], word_tables[a][:].indirect(offsets[:]))
-        for part in range(W8_PARTS):
-            quantise(part)
+
+        quantise(1, held.tile([P, W8_COLS], U32, name="w8_codes1", align_bytes=64), held.tile([P, W8_COLS], U8, name="w8_plane1", align_bytes=64))
 
         activated = held.tile([P, TILES, S], F32, name="activated")
         summed = held.tile([P, TILES, S], F32, name="summed")
         w4_scale_bytes = w4_planes[:].bitcast(U8)
         moved_bytes = moved_planes[:].bitcast(U8)
         out_tiles = out.rearrange("(m p) j -> p m j", p=P)
-        for m in range(TILES):
+
+        def multiply(m, banks, a, start, stop):
             rows = slice(m * P, (m + 1) * P)
             for h in range(HALVES):
                 cols = slice(h * BANK, (h + 1) * BANK)
-                acc = psum.tile([P, BANK], F32, name="bank")
+                if a == 0:
+                    part, within = m // EARLY_TILES, slice(m % EARLY_TILES * P, (m % EARLY_TILES + 1) * P)
+                    weights = w8_codes[part][:, within].bitcast(FP8X4)
+                    weight_scales, token_scales = w8_planes[part][:, within], picked_scales[:, cols]
+                else:
+                    weights = w4_codes[:, a - 1, 2 * m * P : 2 * (m + 1) * P].bitcast(FP4X4)
+                    weight_scales, token_scales = w4_scale_bytes[:, a - 1, rows], moved_bytes[:, a - 1, cols]
                 nc.tensor.matmul_mx(
-                    out=acc[:],
-                    lhsT=w8_codes[:, rows].bitcast(FP8X4),
-                    lhsT_scale=w8_plane[:, rows],
-                    rhs=picked_words[0][:, cols].bitcast(FP8X4),
-                    rhs_scale=picked_scales[:, cols],
-                    start=True,
-                    stop=False,
+                    out=banks[h][:],
+                    lhsT=weights,
+                    lhsT_scale=weight_scales,
+                    rhs=picked_words[a][:, cols].bitcast(FP8X4),
+                    rhs_scale=token_scales,
+                    start=start,
+                    stop=stop,
                 )
-                for a in range(FP4_PASSES):
-                    nc.tensor.matmul_mx(
-                        out=acc[:],
-                        lhsT=w4_codes[:, a, 2 * m * P : 2 * (m + 1) * P].bitcast(FP4X4),
-                        lhsT_scale=w4_scale_bytes[:, a, rows],
-                        rhs=picked_words[a + 1][:, cols].bitcast(FP8X4),
-                        rhs_scale=moved_bytes[:, a, cols],
-                        start=False,
-                        stop=(a == FP4_PASSES - 1),
-                    )
-                nc.scalar.activation(activated[:, m, cols], acc[:], GELU, bias=bias[:, m : m + 1])
-            for h in range(HALVES) if m in (0, TILES - 1) else [None]:
-                cols = slice(0, S) if h is None else slice(h * BANK, (h + 1) * BANK)
+
+        def finish(m, banks):
+            for h in range(HALVES):
+                nc.scalar.activation(activated[:, m, h * BANK : (h + 1) * BANK], banks[h][:], GELU, bias=bias[:, m : m + 1])
+            pieces = HALVES if m == TILES - 1 else 1
+            for piece in range(pieces):
+                cols = slice(piece * S // pieces, (piece + 1) * S // pieces)
                 entries = offsets[:, cols.start // LIST_ROWS : cols.stop // LIST_ROWS]
                 nc.vector.tensor_tensor(summed[:, m, cols], residuals[m][:].indirect(entries), activated[:, m, cols], ADD)
-                if m == TILES - 1:
-                    nc.sync.dma_start(out=out_tiles[:, m, cols], in_=summed[:, m, cols])
-            if m < TILES - 1:
-                nc.sync.dma_start(out=out_tiles[:, m, :], in_=summed[:, m, :])
+                nc.sync.dma_start(out=out_tiles[:, m, cols], in_=summed[:, m, cols])
+
+        def new_banks():
+            return [psum.tile([P, BANK], F32, name="bank") for h in range(HALVES)]
+
+        early_banks = [new_banks() for m in range(EARLY_TILES)]
+        for m in range(EARLY_TILES):
+            multiply(m, early_banks[m], 0, True, False)
+        for m in range(EARLY_TILES):
+            for a in range(1, PASSES):
+                multiply(m, early_banks[m], a, False, a == PASSES - 1)
+            finish(m, early_banks[m])
+        for m in range(EARLY_TILES, TILES):
+            banks = new_banks()
+            order = (1, 2, 0) if m % 2 == 0 else (0, 1, 2)
+            for a in order:
+                multiply(m, banks, a, a == order[0], a == order[-1])
+            finish(m, banks)

@@ -28,10 +28,10 @@ TILES = M // P
 HALVES = S // BANK
 LIST_ROWS = 16
 MOVED_ROWS = 112
-WINDOWS = 4
 W8_PARTS = 2
 W8_COLS = M // W8_PARTS
-EARLY_TILES = W8_COLS // P
+PART_TILES = W8_COLS // P
+EARLY_TILES = 2
 
 
 def tile_list_tabres_gelu_kernel(tc, tab_words, tab_scales, w8, w4_words, w4_scales, rT, b, offs, out):
@@ -39,11 +39,10 @@ def tile_list_tabres_gelu_kernel(tc, tab_words, tab_scales, w8, w4_words, w4_sca
     with ExitStack() as ctx:
         held = ctx.enter_context(tc.tile_pool(name="held", bufs=1))
         reused = ctx.enter_context(tc.tile_pool(name="reused", bufs=1))
-        ring = ctx.enter_context(tc.tile_pool(name="ring", bufs=WINDOWS))
+        staged = ctx.enter_context(tc.tile_pool(name="staged", bufs=1))
         psum = ctx.enter_context(tc.psum_pool(name="psum", bufs=8))
 
         offsets = held.tile([P, S // LIST_ROWS], U16, name="offsets")
-        nc.sync.dma_start(offsets[:], offs)
 
         picked_bytes = 4 * S
         scale_table = reused.tile([P, T // 4], I32, name="scale_table", align_bytes=64, offset=picked_bytes - T // 4)
@@ -60,11 +59,13 @@ def tile_list_tabres_gelu_kernel(tc, tab_words, tab_scales, w8, w4_words, w4_sca
         make_identity(nc, identity[:])
 
         word_tables = [held.tile([P, T], U32, name="word_table0", align_bytes=64)]
-        word_tables.extend(ring.tile([P, T], U32, name="window", align_bytes=64) for a in range(1, PASSES))
+        window_bytes = 4 * T
+        word_tables.extend(staged.tile([P, T], U32, name="word_table%d" % a, align_bytes=64, offset=(a - 1) * window_bytes) for a in range(1, PASSES))
         w4_codes = held.tile([P, FP4_PASSES, 2 * M], U8, name="w4_codes", align_bytes=64)
+        w8_raw = staged.tile([P, PACK, M], F32, name="w8_raw", align_bytes=64, offset=2 * window_bytes)
         w8_grouped = [
-            ring.tile([P, W8_COLS, PACK], BF16, name="window", align_bytes=64),
-            held.tile([P, W8_COLS, PACK], BF16, name="w8_grouped1", align_bytes=64),
+            staged.tile([P, W8_COLS, PACK], BF16, name="w8_grouped%d" % part, align_bytes=64, offset=4 * window_bytes + part * window_bytes // 2)
+            for part in range(W8_PARTS)
         ]
         w8_codes = []
         w8_planes = []
@@ -79,14 +80,11 @@ def tile_list_tabres_gelu_kernel(tc, tab_words, tab_scales, w8, w4_words, w4_sca
             residuals.append(window)
             nc.sync.dma_start(out=window[:], in_=rT[m * P : (m + 1) * P, :])
 
-        def load_and_group_w8(part, raw, pieces):
+        def group_w8(part):
             cols = slice(part * W8_COLS, (part + 1) * W8_COLS)
-            rows = w8[:, cols].rearrange("(p j) n -> p j n", j=PACK)
-            for j in range(0, PACK, PACK // pieces):
-                nc.sync.dma_start(out=raw[:, j : j + PACK // pieces, :], in_=rows[:, j : j + PACK // pieces, :])
             nc.scalar.copy(
                 w8_grouped[part][:].rearrange("p (c i) j -> p c j i", i=4),
-                raw[:].rearrange("p j (c i) -> p c j i", i=4),
+                w8_raw[:, :, cols].rearrange("p j (c i) -> p c j i", i=4),
             )
 
         def quantise(part, codes, plane):
@@ -101,7 +99,9 @@ def tile_list_tabres_gelu_kernel(tc, tab_words, tab_scales, w8, w4_words, w4_sca
         nc.scalar.activation(warm[:], warm[:], GELU)
         load_words(0, slice(0, T // 2))
         load_words(0, slice(T // 2, T))
-        load_and_group_w8(0, ring.tile([P, PACK, W8_COLS], F32, name="window", align_bytes=64), 2)
+        nc.sync.dma_start(offsets[:], offs)
+        load_words(1, slice(0, T // 2))
+        load_words(1, slice(T // 2, T))
 
         table_rows = tab_scales.bitcast(I32)
         for q in range(P // QUAD):
@@ -112,7 +112,10 @@ def tile_list_tabres_gelu_kernel(tc, tab_words, tab_scales, w8, w4_words, w4_sca
         nc.vector.tensor_copy(picked_words[0][:], word_tables[0][:].indirect(offsets[:]))
         nc.vector.tensor_copy(picked_scales[:], scale_table[:].bitcast(U8).indirect(offsets[:]))
 
-        load_words(1, slice(0, T))
+        nc.sync.dma_start(out=w8_raw[:], in_=w8.rearrange("(p j) n -> p j n", j=PACK))
+        for part in range(W8_PARTS):
+            group_w8(part)
+        load_words(2, slice(0, T))
         nc.sync.dma_start(out=w4_codes[:].bitcast(I32), in_=w4_words.rearrange("a p n -> p a n").bitcast(I32))
         w4_rows = w4_scales.bitcast(I32).rearrange("a (q r) n -> r q a n", r=ROWS)
         for r in range(ROWS):
@@ -122,20 +125,20 @@ def tile_list_tabres_gelu_kernel(tc, tab_words, tab_scales, w8, w4_words, w4_sca
         nc.tensor.transpose(bias_psum[:, 0:P], bias_rows[:], identity[:])
         bias = held.tile([P, TILES], F32, name="bias")
         nc.scalar.copy(bias[:], bias_psum[:, 0:TILES])
-        load_words(2, slice(0, T))
         for a in range(FP4_PASSES):
             first = (a + 1) * ROWS
             nc.sync.dma_start(out=moved_planes[0:MOVED_ROWS, a, :], in_=picked_scales[first : first + MOVED_ROWS, :].bitcast(I32))
-        load_and_group_w8(1, reused.tile([P, PACK, W8_COLS], F32, name="w8_second_half", align_bytes=64, offset=picked_bytes + W8_COLS), 1)
-        for m in range(TILES):
-            load_residual(ring.tile([P, T], F32, name="window", align_bytes=64))
+        load_residual(reused.tile([P, T], F32, name="first_residual", align_bytes=64, offset=picked_bytes + W8_COLS))
+        for m in range(1, TILES - 2):
+            load_residual(staged.tile([P, T], F32, name="residual%d" % m, align_bytes=64, offset=(m - 1) * window_bytes))
+        load_residual(reused.tile([P, T], F32, name="seventh_residual", align_bytes=64, offset=picked_bytes + W8_COLS))
+        load_residual(staged.tile([P, T], F32, name="eighth_residual", align_bytes=64, offset=0))
 
-        quantise(0, held.tile([P, W8_COLS], U32, name="w8_codes0", align_bytes=64), reused.tile([P, W8_COLS], U8, name="w8_plane0", align_bytes=64, offset=picked_bytes))
         picked_words.append(reused.tile([P, S], U32, name="picked_words1", align_bytes=64, offset=0))
         picked_words.append(held.tile([P, S], U32, name="picked_words2", align_bytes=64))
         for a in range(1, PASSES):
             nc.vector.tensor_copy(picked_words[a][:], word_tables[a][:].indirect(offsets[:]))
-
+        quantise(0, held.tile([P, W8_COLS], U32, name="w8_codes0", align_bytes=64), reused.tile([P, W8_COLS], U8, name="w8_plane0", align_bytes=64, offset=picked_bytes))
         quantise(1, held.tile([P, W8_COLS], U32, name="w8_codes1", align_bytes=64), held.tile([P, W8_COLS], U8, name="w8_plane1", align_bytes=64))
 
         activated = held.tile([P, TILES, S], F32, name="activated")
@@ -149,7 +152,7 @@ def tile_list_tabres_gelu_kernel(tc, tab_words, tab_scales, w8, w4_words, w4_sca
             for h in range(HALVES):
                 cols = slice(h * BANK, (h + 1) * BANK)
                 if a == 0:
-                    part, within = m // EARLY_TILES, slice(m % EARLY_TILES * P, (m % EARLY_TILES + 1) * P)
+                    part, within = m // PART_TILES, slice(m % PART_TILES * P, (m % PART_TILES + 1) * P)
                     weights = w8_codes[part][:, within].bitcast(FP8X4)
                     weight_scales, token_scales = w8_planes[part][:, within], picked_scales[:, cols]
                 else:
@@ -181,13 +184,8 @@ def tile_list_tabres_gelu_kernel(tc, tab_words, tab_scales, w8, w4_words, w4_sca
         early_banks = [new_banks() for m in range(EARLY_TILES)]
         for m in range(EARLY_TILES):
             multiply(m, early_banks[m], 0, True, False)
-        for m in range(EARLY_TILES):
-            for a in range(1, PASSES):
-                multiply(m, early_banks[m], a, False, a == PASSES - 1)
-            finish(m, early_banks[m])
-        for m in range(EARLY_TILES, TILES):
-            banks = new_banks()
-            order = (1, 2, 0) if m % 2 == 0 else (0, 1, 2)
-            for a in order:
-                multiply(m, banks, a, a == order[0], a == order[-1])
+        for m in range(TILES):
+            banks = early_banks[m] if m < EARLY_TILES else new_banks()
+            for a in range(1 if m < EARLY_TILES else 0, PASSES):
+                multiply(m, banks, a, a == 0, a == PASSES - 1)
             finish(m, banks)

@@ -40,7 +40,7 @@ def tile_list_tabres_gelu_kernel(tc, tab_words, tab_scales, w8, w4_words, w4_sca
         held = ctx.enter_context(tc.tile_pool(name="held", bufs=1))
         reused = ctx.enter_context(tc.tile_pool(name="reused", bufs=1))
         staged = ctx.enter_context(tc.tile_pool(name="staged", bufs=1))
-        psum = ctx.enter_context(tc.psum_pool(name="psum", bufs=8))
+        psum = ctx.enter_context(tc.psum_pool(name="psum", bufs=EARLY_TILES * HALVES))
 
         offsets = held.tile([P, S // LIST_ROWS], U16, name="offsets")
 
@@ -60,11 +60,12 @@ def tile_list_tabres_gelu_kernel(tc, tab_words, tab_scales, w8, w4_words, w4_sca
 
         word_tables = [held.tile([P, T], U32, name="word_table0", align_bytes=64)]
         window_bytes = 4 * T
+        codes_bytes = 4 * W8_COLS
         word_tables.extend(staged.tile([P, T], U32, name="word_table%d" % a, align_bytes=64, offset=(a - 1) * window_bytes) for a in range(1, PASSES))
         w4_codes = held.tile([P, FP4_PASSES, 2 * M], U8, name="w4_codes", align_bytes=64)
-        w8_raw = staged.tile([P, PACK, M], F32, name="w8_raw", align_bytes=64, offset=2 * window_bytes)
+        w8_raw = staged.tile([P, PACK, M], F32, name="w8_raw", align_bytes=64, offset=2 * window_bytes + codes_bytes)
         w8_grouped = [
-            staged.tile([P, W8_COLS, PACK], BF16, name="w8_grouped%d" % part, align_bytes=64, offset=4 * window_bytes + part * window_bytes // 2)
+            staged.tile([P, W8_COLS, PACK], BF16, name="w8_grouped%d" % part, align_bytes=64, offset=4 * window_bytes + codes_bytes + part * window_bytes // 2)
             for part in range(W8_PARTS)
         ]
         w8_codes = []
@@ -115,7 +116,6 @@ def tile_list_tabres_gelu_kernel(tc, tab_words, tab_scales, w8, w4_words, w4_sca
         nc.sync.dma_start(out=w8_raw[:], in_=w8.rearrange("(p j) n -> p j n", j=PACK))
         for part in range(W8_PARTS):
             group_w8(part)
-        load_words(2, slice(0, T))
         nc.sync.dma_start(out=w4_codes[:].bitcast(I32), in_=w4_words.rearrange("a p n -> p a n").bitcast(I32))
         w4_rows = w4_scales.bitcast(I32).rearrange("a (q r) n -> r q a n", r=ROWS)
         for r in range(ROWS):
@@ -125,12 +125,13 @@ def tile_list_tabres_gelu_kernel(tc, tab_words, tab_scales, w8, w4_words, w4_sca
         nc.tensor.transpose(bias_psum[:, 0:P], bias_rows[:], identity[:])
         bias = held.tile([P, TILES], F32, name="bias")
         nc.scalar.copy(bias[:], bias_psum[:, 0:TILES])
+        load_words(2, slice(0, T))
         for a in range(FP4_PASSES):
             first = (a + 1) * ROWS
             nc.sync.dma_start(out=moved_planes[0:MOVED_ROWS, a, :], in_=picked_scales[first : first + MOVED_ROWS, :].bitcast(I32))
         load_residual(reused.tile([P, T], F32, name="first_residual", align_bytes=64, offset=picked_bytes + W8_COLS))
         for m in range(1, TILES - 2):
-            load_residual(staged.tile([P, T], F32, name="residual%d" % m, align_bytes=64, offset=(m - 1) * window_bytes))
+            load_residual(staged.tile([P, T], F32, name="residual%d" % m, align_bytes=64, offset=(m - 1) * window_bytes + (codes_bytes if m > 1 else 0)))
         load_residual(reused.tile([P, T], F32, name="seventh_residual", align_bytes=64, offset=picked_bytes + W8_COLS))
         load_residual(staged.tile([P, T], F32, name="eighth_residual", align_bytes=64, offset=0))
 
@@ -139,7 +140,7 @@ def tile_list_tabres_gelu_kernel(tc, tab_words, tab_scales, w8, w4_words, w4_sca
         for a in range(1, PASSES):
             nc.vector.tensor_copy(picked_words[a][:], word_tables[a][:].indirect(offsets[:]))
         quantise(0, held.tile([P, W8_COLS], U32, name="w8_codes0", align_bytes=64), reused.tile([P, W8_COLS], U8, name="w8_plane0", align_bytes=64, offset=picked_bytes))
-        quantise(1, held.tile([P, W8_COLS], U32, name="w8_codes1", align_bytes=64), held.tile([P, W8_COLS], U8, name="w8_plane1", align_bytes=64))
+        quantise(1, staged.tile([P, W8_COLS], U32, name="w8_codes1", align_bytes=64, offset=window_bytes), held.tile([P, W8_COLS], U8, name="w8_plane1", align_bytes=64))
 
         activated = held.tile([P, TILES, S], F32, name="activated")
         summed = held.tile([P, TILES, S], F32, name="summed")

@@ -32,6 +32,10 @@ W8_PARTS = 2
 W8_COLS = M // W8_PARTS
 PART_TILES = W8_COLS // P
 EARLY_TILES = 2
+LOADED_AFTER = {0: (4,), 1: (5, 6), 2: (7,)}
+PASS_ORDERS = [[0, 2, 1], [2, 1, 0]]
+OVERLAP = 64
+WINDOW = 4 * T
 
 
 def tile_list_tabres_gelu_kernel(tc, tab_words, tab_scales, w8, w4_words, w4_scales, rT, b, offs, out):
@@ -40,153 +44,189 @@ def tile_list_tabres_gelu_kernel(tc, tab_words, tab_scales, w8, w4_words, w4_sca
         held = ctx.enter_context(tc.tile_pool(name="held", bufs=1))
         reused = ctx.enter_context(tc.tile_pool(name="reused", bufs=1))
         staged = ctx.enter_context(tc.tile_pool(name="staged", bufs=1))
+        paired = ctx.enter_context(tc.tile_pool(name="paired", bufs=1))
         psum = ctx.enter_context(tc.psum_pool(name="psum", bufs=EARLY_TILES * HALVES))
+        turned = ctx.enter_context(tc.psum_pool(name="turned", bufs=1))
 
         offsets = held.tile([P, S // LIST_ROWS], U16, name="offsets")
 
-        picked_bytes = 4 * S
-        scale_table = reused.tile([P, T // 4], I32, name="scale_table", align_bytes=64, offset=picked_bytes - T // 4)
+        scale_place = 4 * S - OVERLAP
+        first_place = scale_place + T - OVERLAP
+        grouped_place = first_place + WINDOW
+        scale_table = reused.tile([P, T // 4], I32, name="scale_table", align_bytes=64, offset=scale_place)
         moved_planes = held.tile([P, FP4_PASSES, S // 4], I32, name="moved_planes", align_bytes=64)
         w4_planes = held.tile([P, FP4_PASSES, M // 4], I32, name="w4_planes", align_bytes=64)
         bias_rows = held.tile([P, P], F32, name="bias_rows")
         warm = held.tile([P, 1], F32, name="warm")
         identity = held.tile([P, P], F32, name="identity")
         nc.gpsimd.memset(scale_table[:], 0)
-        nc.vector.memset(w4_planes[:], 0)
-        nc.vector.memset(moved_planes[:], 0)
         nc.vector.memset(bias_rows[:], 0.0)
+        nc.vector.memset(w4_planes[:], 0)
         nc.vector.memset(warm[:], 0.0)
+        nc.vector.memset(moved_planes[:], 0)
         make_identity(nc, identity[:])
+        nc.scalar.activation(warm[:], warm[:], GELU)
 
-        word_tables = [held.tile([P, T], U32, name="word_table0", align_bytes=64)]
-        window_bytes = 4 * T
-        codes_bytes = 4 * W8_COLS
-        word_tables.extend(staged.tile([P, T], U32, name="word_table%d" % a, align_bytes=64, offset=(a - 1) * window_bytes) for a in range(1, PASSES))
-        w4_codes = held.tile([P, FP4_PASSES, 2 * M], U8, name="w4_codes", align_bytes=64)
-        w8_raw = staged.tile([P, PACK, M], F32, name="w8_raw", align_bytes=64, offset=2 * window_bytes + codes_bytes)
-        w8_grouped = [
-            staged.tile([P, W8_COLS, PACK], BF16, name="w8_grouped%d" % part, align_bytes=64, offset=4 * window_bytes + codes_bytes + part * window_bytes // 2)
-            for part in range(W8_PARTS)
+        def staged_window(name, place, dtype):
+            return staged.tile([P, T], dtype, name=name, align_bytes=64, offset=place * (WINDOW - OVERLAP) + (OVERLAP if place > 3 else 0))
+
+        word_tables = [
+            held.tile([P, T], U32, name="word_table0", align_bytes=64),
+            staged_window("word_table1", 2, U32),
+            staged_window("word_table2", 5, U32),
         ]
-        w8_codes = []
-        w8_planes = []
-        residuals = []
+        w4_codes = held.tile([P, FP4_PASSES, 2 * M], U8, name="w4_codes", align_bytes=64)
+        w8_raw = [
+            held.tile([P, PACK, W8_COLS], F32, name="w8_raw0", align_bytes=64),
+            staged.tile([P, PACK, W8_COLS], F32, name="w8_raw1", align_bytes=64, offset=3 * (WINDOW - OVERLAP)),
+        ]
+        w8_grouped = [
+            reused.tile([P, W8_COLS, PACK], BF16, name="w8_grouped0", align_bytes=64, offset=grouped_place),
+            held.tile([P, W8_COLS, PACK], BF16, name="w8_grouped1", align_bytes=64),
+        ]
+        w8_codes = [
+            staged.tile([P, W8_COLS], U32, name="w8_codes0", align_bytes=64, offset=2 * WINDOW),
+            held.tile([P, W8_COLS], U32, name="w8_codes1", align_bytes=64),
+        ]
+        third_place = 4 * WINDOW - 3 * OVERLAP
+        w8_planes = [
+            held.tile([P, W8_COLS], U8, name="w8_plane0", align_bytes=64),
+            staged.tile([P, W8_COLS], U8, name="w8_plane1", align_bytes=64, offset=third_place),
+        ]
+        residuals = [
+            reused.tile([P, T], F32, name="residual0", align_bytes=64, offset=first_place),
+            staged_window("residual1", 1, F32),
+            staged_window("residual2", 4, F32),
+            staged_window("residual3", 6, F32),
+            reused.tile([P, T], F32, name="residual4", align_bytes=64, offset=first_place),
+            staged_window("residual5", 0, F32),
+            staged.tile([P, T], F32, name="residual6", align_bytes=64, offset=WINDOW),
+            staged.tile([P, T], F32, name="residual7", align_bytes=64, offset=third_place + W8_COLS),
+        ]
+        w8_rows = w8.rearrange("(p j) n -> p j n", j=PACK)
+
+        def half_list(h):
+            return offsets[:, h * BANK // LIST_ROWS : (h + 1) * BANK // LIST_ROWS]
 
         def load_words(a, cols):
             words = tab_words[a].rearrange("p t i -> p (t i)").bitcast(I32)
             nc.sync.dma_start(out=word_tables[a][:, cols].bitcast(I32), in_=words[:, cols])
 
-        def load_residual(window):
-            m = len(residuals)
-            residuals.append(window)
-            nc.sync.dma_start(out=window[:], in_=rT[m * P : (m + 1) * P, :])
+        def load_residual(m):
+            nc.sync.dma_start(out=residuals[m][:], in_=rT[m * P : (m + 1) * P, :])
 
         def group_w8(part):
-            cols = slice(part * W8_COLS, (part + 1) * W8_COLS)
             nc.scalar.copy(
                 w8_grouped[part][:].rearrange("p (c i) j -> p c j i", i=4),
-                w8_raw[:, :, cols].rearrange("p j (c i) -> p c j i", i=4),
+                w8_raw[part][:].rearrange("p j (c i) -> p c j i", i=4),
             )
 
-        def quantise(part, codes, plane):
-            w8_codes.append(codes)
-            w8_planes.append(plane)
+        def quantise(part):
             nc.vector.quantize_mx(
-                out=codes[:].bitcast(FP8X4),
-                scales=plane[:],
+                out=w8_codes[part][:].bitcast(FP8X4),
+                scales=w8_planes[part][:],
                 in_=w8_grouped[part][:].rearrange("p n j -> p (n j)"),
             )
 
-        nc.scalar.activation(warm[:], warm[:], GELU)
         load_words(0, slice(0, T // 2))
         load_words(0, slice(T // 2, T))
         nc.sync.dma_start(offsets[:], offs)
-        load_words(1, slice(0, T // 2))
-        load_words(1, slice(T // 2, T))
-
+        for half in range(2):
+            rows = slice(2 * half, 2 * half + 2)
+            nc.sync.dma_start(out=w8_raw[0][:, rows, :], in_=w8_rows[:, rows, 0:W8_COLS])
         table_rows = tab_scales.bitcast(I32)
         for q in range(P // QUAD):
-            nc.sync.dma_start(out=scale_table[q * QUAD : q * QUAD + PASSES * ROWS, :], in_=table_rows[:, q * ROWS : (q + 1) * ROWS, :])
-
-        picked_words = [held.tile([P, S], U32, name="picked_words0", align_bytes=64)]
-        picked_scales = held.tile([P, S], U8, name="picked_scales", align_bytes=64)
-        nc.vector.tensor_copy(picked_words[0][:], word_tables[0][:].indirect(offsets[:]))
-        nc.vector.tensor_copy(picked_scales[:], scale_table[:].bitcast(U8).indirect(offsets[:]))
-
-        nc.sync.dma_start(out=w8_raw[:], in_=w8.rearrange("(p j) n -> p j n", j=PACK))
-        for part in range(W8_PARTS):
-            group_w8(part)
-        nc.sync.dma_start(out=w4_codes[:].bitcast(I32), in_=w4_words.rearrange("a p n -> p a n").bitcast(I32))
+            first = q * QUAD + ROWS
+            nc.sync.dma_start(out=scale_table[first : first + PASSES * ROWS, :], in_=table_rows[:, q * ROWS : (q + 1) * ROWS, :])
+        load_words(1, slice(0, T))
+        nc.sync.dma_start(out=bias_rows[0:TILES, :], in_=b.rearrange("(m p) -> m p", p=P))
         w4_rows = w4_scales.bitcast(I32).rearrange("a (q r) n -> r q a n", r=ROWS)
         for r in range(ROWS):
             nc.sync.dma_start(out=w4_planes[r:P:QUAD, :, :], in_=w4_rows[r])
-        nc.sync.dma_start(out=bias_rows[0:TILES, :], in_=b.rearrange("(m p) -> m p", p=P))
-        bias_psum = psum.tile([P, BANK], F32, name="bank")
+            if r == 1:
+                load_words(2, slice(0, T))
+        nc.sync.dma_start(out=w4_codes[:].bitcast(I32), in_=w4_words.rearrange("a p n -> p a n").bitcast(I32))
+
+        picked_words = [
+            held.tile([P, S], U32, name="picked_words0", align_bytes=64),
+            reused.tile([P, S], U32, name="picked_words1", align_bytes=64, offset=0),
+            reused.tile([P, S], U32, name="picked_words2", align_bytes=64, offset=grouped_place),
+        ]
+        picked_scales = held.tile([P, S], U8, name="picked_scales", align_bytes=64)
+        nc.vector.tensor_copy(picked_words[0][:], word_tables[0][:].indirect(offsets[:]))
+        nc.vector.tensor_copy(picked_scales[:], scale_table[:].bitcast(U8).indirect(offsets[:]))
+        for a in range(FP4_PASSES):
+            first = (a + 2) * ROWS
+            nc.sync.dma_start(out=moved_planes[0:MOVED_ROWS, a, :], in_=picked_scales[first : first + MOVED_ROWS, :].bitcast(I32))
+        group_w8(0)
+        nc.vector.tensor_copy(picked_words[1][:], word_tables[1][:].indirect(offsets[:]))
+        quantise(0)
+        for h in range(HALVES):
+            nc.vector.tensor_copy(picked_words[2][:, h * BANK : (h + 1) * BANK], word_tables[2][:].indirect(half_list(h)))
+        load_residual(0)
+        load_residual(1)
+        nc.sync.dma_start(out=w8_raw[1][:], in_=w8_rows[:, :, W8_COLS:M])
+        load_residual(2)
+        load_residual(3)
+
+        bias_psum = turned.tile([P, BANK], F32, name="bias_psum")
         nc.tensor.transpose(bias_psum[:, 0:P], bias_rows[:], identity[:])
         bias = held.tile([P, TILES], F32, name="bias")
         nc.scalar.copy(bias[:], bias_psum[:, 0:TILES])
-        load_words(2, slice(0, T))
-        for a in range(FP4_PASSES):
-            first = (a + 1) * ROWS
-            nc.sync.dma_start(out=moved_planes[0:MOVED_ROWS, a, :], in_=picked_scales[first : first + MOVED_ROWS, :].bitcast(I32))
-        load_residual(reused.tile([P, T], F32, name="first_residual", align_bytes=64, offset=picked_bytes + W8_COLS))
-        for m in range(1, TILES - 2):
-            load_residual(staged.tile([P, T], F32, name="residual%d" % m, align_bytes=64, offset=(m - 1) * window_bytes + (codes_bytes if m > 1 else 0)))
-        load_residual(reused.tile([P, T], F32, name="seventh_residual", align_bytes=64, offset=picked_bytes + W8_COLS))
-        load_residual(staged.tile([P, T], F32, name="eighth_residual", align_bytes=64, offset=0))
-
-        picked_words.append(reused.tile([P, S], U32, name="picked_words1", align_bytes=64, offset=0))
-        picked_words.append(held.tile([P, S], U32, name="picked_words2", align_bytes=64))
-        for a in range(1, PASSES):
-            nc.vector.tensor_copy(picked_words[a][:], word_tables[a][:].indirect(offsets[:]))
-        quantise(0, held.tile([P, W8_COLS], U32, name="w8_codes0", align_bytes=64), reused.tile([P, W8_COLS], U8, name="w8_plane0", align_bytes=64, offset=picked_bytes))
-        quantise(1, staged.tile([P, W8_COLS], U32, name="w8_codes1", align_bytes=64, offset=window_bytes), held.tile([P, W8_COLS], U8, name="w8_plane1", align_bytes=64))
 
         activated = held.tile([P, TILES, S], F32, name="activated")
-        summed = held.tile([P, TILES, S], F32, name="summed")
+        summed = [paired.tile([P, 2, S], F32, name="summed%d" % u, align_bytes=64, offset=u * WINDOW) for u in range(TILES // 2)]
         w4_scale_bytes = w4_planes[:].bitcast(U8)
         moved_bytes = moved_planes[:].bitcast(U8)
         out_tiles = out.rearrange("(m p) j -> p m j", p=P)
 
-        def multiply(m, banks, a, start, stop):
+        def multiply(m, h, bank, a):
             rows = slice(m * P, (m + 1) * P)
-            for h in range(HALVES):
-                cols = slice(h * BANK, (h + 1) * BANK)
-                if a == 0:
-                    part, within = m // PART_TILES, slice(m % PART_TILES * P, (m % PART_TILES + 1) * P)
-                    weights = w8_codes[part][:, within].bitcast(FP8X4)
-                    weight_scales, token_scales = w8_planes[part][:, within], picked_scales[:, cols]
-                else:
-                    weights = w4_codes[:, a - 1, 2 * m * P : 2 * (m + 1) * P].bitcast(FP4X4)
-                    weight_scales, token_scales = w4_scale_bytes[:, a - 1, rows], moved_bytes[:, a - 1, cols]
-                nc.tensor.matmul_mx(
-                    out=banks[h][:],
-                    lhsT=weights,
-                    lhsT_scale=weight_scales,
-                    rhs=picked_words[a][:, cols].bitcast(FP8X4),
-                    rhs_scale=token_scales,
-                    start=start,
-                    stop=stop,
-                )
-
-        def finish(m, banks):
-            for h in range(HALVES):
-                nc.scalar.activation(activated[:, m, h * BANK : (h + 1) * BANK], banks[h][:], GELU, bias=bias[:, m : m + 1])
-            pieces = HALVES if m == TILES - 1 else 1
-            for piece in range(pieces):
-                cols = slice(piece * S // pieces, (piece + 1) * S // pieces)
-                entries = offsets[:, cols.start // LIST_ROWS : cols.stop // LIST_ROWS]
-                nc.vector.tensor_tensor(summed[:, m, cols], residuals[m][:].indirect(entries), activated[:, m, cols], ADD)
-                nc.sync.dma_start(out=out_tiles[:, m, cols], in_=summed[:, m, cols])
+            cols = slice(h * BANK, (h + 1) * BANK)
+            if a == 0:
+                part, within = m // PART_TILES, slice(m % PART_TILES * P, (m % PART_TILES + 1) * P)
+                weights = w8_codes[part][:, within].bitcast(FP8X4)
+                weight_scales, token_scales = w8_planes[part][:, within], picked_scales[ROWS:P, cols]
+            else:
+                weights = w4_codes[:, a - 1, 2 * m * P : 2 * (m + 1) * P].bitcast(FP4X4)
+                weight_scales, token_scales = w4_scale_bytes[:, a - 1, rows], moved_bytes[:, a - 1, cols]
+            nc.tensor.matmul_mx(
+                out=bank[:],
+                lhsT=weights,
+                lhsT_scale=weight_scales,
+                rhs=picked_words[a][:, cols].bitcast(FP8X4),
+                rhs_scale=token_scales,
+                start=a == PASS_ORDERS[m // PART_TILES][0],
+                stop=a == PASS_ORDERS[m // PART_TILES][-1],
+            )
 
         def new_banks():
             return [psum.tile([P, BANK], F32, name="bank") for h in range(HALVES)]
 
         early_banks = [new_banks() for m in range(EARLY_TILES)]
         for m in range(EARLY_TILES):
-            multiply(m, early_banks[m], 0, True, False)
+            for h in range(HALVES):
+                multiply(m, h, early_banks[m][h], 0)
         for m in range(TILES):
             banks = early_banks[m] if m < EARLY_TILES else new_banks()
-            for a in range(1 if m < EARLY_TILES else 0, PASSES):
-                multiply(m, banks, a, a == 0, a == PASSES - 1)
-            finish(m, banks)
+            for h in range(HALVES):
+                cols = slice(h * BANK, (h + 1) * BANK)
+                for a in PASS_ORDERS[m // PART_TILES][1 if m < EARLY_TILES else 0 :]:
+                    multiply(m, h, banks[h], a)
+                nc.scalar.activation(activated[:, m, cols], banks[h][:], GELU, bias=bias[:, m : m + 1])
+                if m in (0, TILES - 1):
+                    nc.vector.tensor_tensor(summed[m // 2][:, m % 2, cols], residuals[m][:].indirect(half_list(h)), activated[:, m, cols], ADD)
+                if m == TILES - 1:
+                    nc.sync.dma_start(out=out_tiles[:, m, cols], in_=summed[m // 2][:, m % 2, cols])
+            if m not in (0, TILES - 1):
+                nc.vector.tensor_tensor(summed[m // 2][:, m % 2, :], residuals[m][:].indirect(offsets[:]), activated[:, m, :], ADD)
+            for later in LOADED_AFTER.get(m, ()):
+                load_residual(later)
+            if m == 1:
+                group_w8(1)
+            if m == 2:
+                quantise(1)
+            if m == TILES - 2:
+                nc.sync.dma_start(out=out_tiles[:, m, :], in_=summed[m // 2][:, m % 2, :])
+            elif m % 2 == 1 and m < TILES - 2:
+                nc.sync.dma_start(out=out_tiles[:, m - 1 : m + 1, :], in_=summed[m // 2][:])

@@ -32,7 +32,8 @@ W8_PARTS = 2
 W8_COLS = M // W8_PARTS
 PART_TILES = W8_COLS // P
 EARLY_TILES = 2
-LOADED_AFTER = {0: (4,), 1: (5, 6), 2: (7,)}
+STORE_ENDS = [4, 6, 7]
+LOADED_AFTER = {0: (5,), 1: (6,), 2: (7,)}
 PASS_ORDERS = [[0, 2, 1], [2, 1, 0]]
 OVERLAP = 64
 WINDOW = 4 * T
@@ -44,22 +45,26 @@ def tile_list_tabres_gelu_kernel(tc, tab_words, tab_scales, w8, w4_words, w4_sca
         held = ctx.enter_context(tc.tile_pool(name="held", bufs=1))
         reused = ctx.enter_context(tc.tile_pool(name="reused", bufs=1))
         staged = ctx.enter_context(tc.tile_pool(name="staged", bufs=1))
-        paired = ctx.enter_context(tc.tile_pool(name="paired", bufs=1))
+        spare = ctx.enter_context(tc.tile_pool(name="spare", bufs=1))
         psum = ctx.enter_context(tc.psum_pool(name="psum", bufs=EARLY_TILES * HALVES))
         turned = ctx.enter_context(tc.psum_pool(name="turned", bufs=1))
 
         offsets = held.tile([P, S // LIST_ROWS], U16, name="offsets")
 
-        scale_place = 4 * S - OVERLAP
+        scale_place = 0
         first_place = scale_place + T - OVERLAP
         grouped_place = first_place + WINDOW
         scale_table = reused.tile([P, T // 4], I32, name="scale_table", align_bytes=64, offset=scale_place)
         moved_planes = held.tile([P, FP4_PASSES, S // 4], I32, name="moved_planes", align_bytes=64)
         w4_planes = held.tile([P, FP4_PASSES, M // 4], I32, name="w4_planes", align_bytes=64)
         bias_rows = held.tile([P, P], F32, name="bias_rows")
-        warm = held.tile([P, 1], F32, name="warm")
+        warm = staged.tile([P, 1], F32, name="warm", align_bytes=64, offset=5 * WINDOW)
         identity = held.tile([P, P], F32, name="identity")
         nc.gpsimd.memset(scale_table[:], 0)
+        table_rows = tab_scales.bitcast(I32)
+        for q in range(P // QUAD):
+            first = q * QUAD + ROWS
+            nc.gpsimd.dma_start(out=scale_table[first : first + PASSES * ROWS, :], in_=table_rows[:, q * ROWS : (q + 1) * ROWS, :])
         nc.vector.memset(bias_rows[:], 0.0)
         nc.vector.memset(w4_planes[:], 0)
         nc.vector.memset(warm[:], 0.0)
@@ -71,46 +76,46 @@ def tile_list_tabres_gelu_kernel(tc, tab_words, tab_scales, w8, w4_words, w4_sca
             return staged.tile([P, T], dtype, name=name, align_bytes=64, offset=place * (WINDOW - OVERLAP) + (OVERLAP if place > 3 else 0))
 
         word_tables = [
-            held.tile([P, T], U32, name="word_table0", align_bytes=64),
+            spare.tile([P, T], U32, name="word_table0", align_bytes=64, offset=0),
             staged_window("word_table1", 2, U32),
             staged_window("word_table2", 5, U32),
         ]
         w4_codes = held.tile([P, FP4_PASSES, 2 * M], U8, name="w4_codes", align_bytes=64)
         w8_raw = [
             held.tile([P, PACK, W8_COLS], F32, name="w8_raw0", align_bytes=64),
-            staged.tile([P, PACK, W8_COLS], F32, name="w8_raw1", align_bytes=64, offset=3 * (WINDOW - OVERLAP)),
+            staged.tile([P, PACK, W8_COLS], F32, name="w8_raw1", align_bytes=64, offset=WINDOW - OVERLAP),
         ]
         w8_grouped = [
             reused.tile([P, W8_COLS, PACK], BF16, name="w8_grouped0", align_bytes=64, offset=grouped_place),
             held.tile([P, W8_COLS, PACK], BF16, name="w8_grouped1", align_bytes=64),
         ]
         w8_codes = [
-            staged.tile([P, W8_COLS], U32, name="w8_codes0", align_bytes=64, offset=2 * WINDOW),
+            held.tile([P, W8_COLS], U32, name="w8_codes0", align_bytes=64),
             held.tile([P, W8_COLS], U32, name="w8_codes1", align_bytes=64),
         ]
-        third_place = 4 * WINDOW - 3 * OVERLAP
+        third_end = 4 * WINDOW - 3 * OVERLAP
         w8_planes = [
-            held.tile([P, W8_COLS], U8, name="w8_plane0", align_bytes=64),
-            staged.tile([P, W8_COLS], U8, name="w8_plane1", align_bytes=64, offset=third_place),
+            reused.tile([P, W8_COLS], U8, name="w8_plane0", align_bytes=64, offset=0),
+            staged.tile([P, W8_COLS], U8, name="w8_plane1", align_bytes=64, offset=third_end - W8_COLS),
         ]
         residuals = [
-            reused.tile([P, T], F32, name="residual0", align_bytes=64, offset=first_place),
-            staged_window("residual1", 1, F32),
-            staged_window("residual2", 4, F32),
-            staged_window("residual3", 6, F32),
-            reused.tile([P, T], F32, name="residual4", align_bytes=64, offset=first_place),
-            staged_window("residual5", 0, F32),
-            staged.tile([P, T], F32, name="residual6", align_bytes=64, offset=WINDOW),
-            staged.tile([P, T], F32, name="residual7", align_bytes=64, offset=third_place + W8_COLS),
+            spare.tile([P, T], F32, name="residual0", align_bytes=64, offset=0),
+            reused.tile([P, T], F32, name="residual1", align_bytes=64, offset=first_place),
+            staged_window("residual2", 3, F32),
+            staged_window("residual3", 4, F32),
+            staged_window("residual4", 6, F32),
+            spare.tile([P, T], F32, name="residual5", align_bytes=64, offset=0),
+            reused.tile([P, T], F32, name="residual6", align_bytes=64, offset=first_place),
+            staged.tile([P, T], F32, name="residual7", align_bytes=64, offset=third_end - W8_COLS - WINDOW),
         ]
         w8_rows = w8.rearrange("(p j) n -> p j n", j=PACK)
 
         def half_list(h):
             return offsets[:, h * BANK // LIST_ROWS : (h + 1) * BANK // LIST_ROWS]
 
-        def load_words(a, cols):
+        def load_words(a):
             words = tab_words[a].rearrange("p t i -> p (t i)").bitcast(I32)
-            nc.sync.dma_start(out=word_tables[a][:, cols].bitcast(I32), in_=words[:, cols])
+            nc.sync.dma_start(out=word_tables[a][:].bitcast(I32), in_=words)
 
         def load_residual(m):
             nc.sync.dma_start(out=residuals[m][:], in_=rT[m * P : (m + 1) * P, :])
@@ -128,46 +133,38 @@ def tile_list_tabres_gelu_kernel(tc, tab_words, tab_scales, w8, w4_words, w4_sca
                 in_=w8_grouped[part][:].rearrange("p n j -> p (n j)"),
             )
 
-        load_words(0, slice(0, T // 2))
-        load_words(0, slice(T // 2, T))
+        load_words(0)
         nc.sync.dma_start(offsets[:], offs)
-        for half in range(2):
-            rows = slice(2 * half, 2 * half + 2)
-            nc.sync.dma_start(out=w8_raw[0][:, rows, :], in_=w8_rows[:, rows, 0:W8_COLS])
-        table_rows = tab_scales.bitcast(I32)
-        for q in range(P // QUAD):
-            first = q * QUAD + ROWS
-            nc.sync.dma_start(out=scale_table[first : first + PASSES * ROWS, :], in_=table_rows[:, q * ROWS : (q + 1) * ROWS, :])
-        load_words(1, slice(0, T))
+        nc.sync.dma_start(out=w4_codes[:].bitcast(I32), in_=w4_words.rearrange("a p n -> p a n").bitcast(I32))
+        nc.sync.dma_start(out=w8_raw[0][:], in_=w8_rows[:, :, 0:W8_COLS])
+        load_words(1)
         nc.sync.dma_start(out=bias_rows[0:TILES, :], in_=b.rearrange("(m p) -> m p", p=P))
         w4_rows = w4_scales.bitcast(I32).rearrange("a (q r) n -> r q a n", r=ROWS)
         for r in range(ROWS):
             nc.sync.dma_start(out=w4_planes[r:P:QUAD, :, :], in_=w4_rows[r])
-            if r == 1:
-                load_words(2, slice(0, T))
-        nc.sync.dma_start(out=w4_codes[:].bitcast(I32), in_=w4_words.rearrange("a p n -> p a n").bitcast(I32))
+        load_words(2)
 
         picked_words = [
             held.tile([P, S], U32, name="picked_words0", align_bytes=64),
-            reused.tile([P, S], U32, name="picked_words1", align_bytes=64, offset=0),
-            reused.tile([P, S], U32, name="picked_words2", align_bytes=64, offset=grouped_place),
+            reused.tile([P, S], U32, name="picked_words1", align_bytes=64, offset=grouped_place),
+            staged.tile([P, S], U32, name="picked_words2", align_bytes=64, offset=2 * WINDOW),
         ]
         picked_scales = held.tile([P, S], U8, name="picked_scales", align_bytes=64)
         nc.vector.tensor_copy(picked_words[0][:], word_tables[0][:].indirect(offsets[:]))
+        load_residual(0)
         nc.vector.tensor_copy(picked_scales[:], scale_table[:].bitcast(U8).indirect(offsets[:]))
         for a in range(FP4_PASSES):
             first = (a + 2) * ROWS
             nc.sync.dma_start(out=moved_planes[0:MOVED_ROWS, a, :], in_=picked_scales[first : first + MOVED_ROWS, :].bitcast(I32))
         group_w8(0)
-        nc.vector.tensor_copy(picked_words[1][:], word_tables[1][:].indirect(offsets[:]))
         quantise(0)
+        nc.vector.tensor_copy(picked_words[1][:], word_tables[1][:].indirect(offsets[:]))
         for h in range(HALVES):
             nc.vector.tensor_copy(picked_words[2][:, h * BANK : (h + 1) * BANK], word_tables[2][:].indirect(half_list(h)))
-        load_residual(0)
         load_residual(1)
         nc.sync.dma_start(out=w8_raw[1][:], in_=w8_rows[:, :, W8_COLS:M])
-        load_residual(2)
-        load_residual(3)
+        for m in range(2, 5):
+            load_residual(m)
 
         bias_psum = turned.tile([P, BANK], F32, name="bias_psum")
         nc.tensor.transpose(bias_psum[:, 0:P], bias_rows[:], identity[:])
@@ -175,7 +172,7 @@ def tile_list_tabres_gelu_kernel(tc, tab_words, tab_scales, w8, w4_words, w4_sca
         nc.scalar.copy(bias[:], bias_psum[:, 0:TILES])
 
         activated = held.tile([P, TILES, S], F32, name="activated")
-        summed = [paired.tile([P, 2, S], F32, name="summed%d" % u, align_bytes=64, offset=u * WINDOW) for u in range(TILES // 2)]
+        summed = held.tile([P, TILES, S], F32, name="summed")
         w4_scale_bytes = w4_planes[:].bitcast(U8)
         moved_bytes = moved_planes[:].bitcast(U8)
         out_tiles = out.rearrange("(m p) j -> p m j", p=P)
@@ -215,18 +212,18 @@ def tile_list_tabres_gelu_kernel(tc, tab_words, tab_scales, w8, w4_words, w4_sca
                     multiply(m, h, banks[h], a)
                 nc.scalar.activation(activated[:, m, cols], banks[h][:], GELU, bias=bias[:, m : m + 1])
                 if m in (0, TILES - 1):
-                    nc.vector.tensor_tensor(summed[m // 2][:, m % 2, cols], residuals[m][:].indirect(half_list(h)), activated[:, m, cols], ADD)
+                    nc.vector.tensor_tensor(summed[:, m, cols], residuals[m][:].indirect(half_list(h)), activated[:, m, cols], ADD)
                 if m == TILES - 1:
-                    nc.sync.dma_start(out=out_tiles[:, m, cols], in_=summed[m // 2][:, m % 2, cols])
+                    nc.sync.dma_start(out=out_tiles[:, m, cols], in_=summed[:, m, cols])
             if m not in (0, TILES - 1):
-                nc.vector.tensor_tensor(summed[m // 2][:, m % 2, :], residuals[m][:].indirect(offsets[:]), activated[:, m, :], ADD)
+                nc.vector.tensor_tensor(summed[:, m, :], residuals[m][:].indirect(offsets[:]), activated[:, m, :], ADD)
             for later in LOADED_AFTER.get(m, ()):
                 load_residual(later)
             if m == 1:
                 group_w8(1)
             if m == 2:
                 quantise(1)
-            if m == TILES - 2:
-                nc.sync.dma_start(out=out_tiles[:, m, :], in_=summed[m // 2][:, m % 2, :])
-            elif m % 2 == 1 and m < TILES - 2:
-                nc.sync.dma_start(out=out_tiles[:, m - 1 : m + 1, :], in_=summed[m // 2][:])
+            if m + 1 in STORE_ENDS:
+                place = STORE_ENDS.index(m + 1)
+                tiles = slice(STORE_ENDS[place - 1] if place else 0, m + 1)
+                nc.sync.dma_start(out=out_tiles[:, tiles, :], in_=summed[:, tiles, :])

@@ -27,87 +27,60 @@ BANK = 512
 TILES = M // P
 HALVES = S // BANK
 LIST_ROWS = 16
-MOVED_ROWS = 112
-W8_PARTS = 2
-W8_COLS = M // W8_PARTS
-PART_TILES = W8_COLS // P
-EARLY_TILES = 2
-STORE_ENDS = [4, 6, 7]
-LOADED_AFTER = {0: (5,), 1: (6,), 2: (7,)}
-PASS_ORDERS = [[0, 2, 1], [2, 1, 0]]
-OVERLAP = 64
+SCALE_ROWS = P * PACK // QUAD
+DEALT_FROM = P - PASSES * SCALE_ROWS
+FIRST_TILES = 5
+W8_PARTS = [(0, FIRST_TILES * P), (FIRST_TILES * P, M)]
+QUANTISED = [(0, 4 * P), (4 * P, FIRST_TILES * P), (FIRST_TILES * P, M)]
 WINDOW = 4 * T
+STORE_ENDS = [4, 6, 7]
 
 
 def tile_list_tabres_gelu_kernel(tc, tab_words, tab_scales, w8, w4_words, w4_scales, rT, b, offs, out):
     nc = tc.nc
     with ExitStack() as ctx:
         held = ctx.enter_context(tc.tile_pool(name="held", bufs=1))
-        reused = ctx.enter_context(tc.tile_pool(name="reused", bufs=1))
-        staged = ctx.enter_context(tc.tile_pool(name="staged", bufs=1))
-        spare = ctx.enter_context(tc.tile_pool(name="spare", bufs=1))
-        psum = ctx.enter_context(tc.psum_pool(name="psum", bufs=EARLY_TILES * HALVES))
+        room = ctx.enter_context(tc.tile_pool(name="room", bufs=1))
+        again = ctx.enter_context(tc.tile_pool(name="again", bufs=1))
+        psum = ctx.enter_context(tc.psum_pool(name="psum", bufs=4))
         turned = ctx.enter_context(tc.psum_pool(name="turned", bufs=1))
 
         offsets = held.tile([P, S // LIST_ROWS], U16, name="offsets")
-
-        scale_place = 0
-        first_place = scale_place + T - OVERLAP
-        grouped_place = first_place + WINDOW
-        scale_table = reused.tile([P, T // 4], I32, name="scale_table", align_bytes=64, offset=scale_place)
-        moved_planes = held.tile([P, FP4_PASSES, S // 4], I32, name="moved_planes", align_bytes=64)
+        scale_room = room.tile([P, (T + (TILES + 3) * WINDOW) // 4], I32, name="scale_room", align_bytes=64, offset=0)
+        scale_table = scale_room[:, 0 : T // 4]
+        token_planes = held.tile([P, PASSES, S // 4], I32, name="token_planes", align_bytes=64)
         w4_planes = held.tile([P, FP4_PASSES, M // 4], I32, name="w4_planes", align_bytes=64)
         bias_rows = held.tile([P, P], F32, name="bias_rows")
-        warm = staged.tile([P, 1], F32, name="warm", align_bytes=64, offset=5 * WINDOW)
         identity = held.tile([P, P], F32, name="identity")
-        nc.gpsimd.memset(scale_table[:], 0)
-        table_rows = tab_scales.bitcast(I32)
+
+        nc.vector.memset(scale_table[0:64, :], 0)
+        nc.vector.memset(scale_table[64:DEALT_FROM, :], 0)
+        nc.vector.memset(bias_rows[0:96, :], 0.0)
+        nc.vector.memset(bias_rows[96 : P - TILES, :], 0.0)
+        nc.vector.memset(token_planes[:], 0)
+        nc.gpsimd.memset(w4_planes[:], 0)
+        w4_rows = w4_scales.bitcast(I32).rearrange("a (q r) n -> q r a n", r=ROWS)
         for q in range(P // QUAD):
-            first = q * QUAD + ROWS
-            nc.gpsimd.dma_start(out=scale_table[first : first + PASSES * ROWS, :], in_=table_rows[:, q * ROWS : (q + 1) * ROWS, :])
-        nc.vector.memset(bias_rows[:], 0.0)
-        nc.vector.memset(w4_planes[:], 0)
-        nc.vector.memset(warm[:], 0.0)
-        nc.vector.memset(moved_planes[:], 0)
+            nc.gpsimd.dma_start(out=w4_planes[q * QUAD : q * QUAD + ROWS, :, :], in_=w4_rows[q])
         make_identity(nc, identity[:])
-        nc.scalar.activation(warm[:], warm[:], GELU)
 
-        def staged_window(name, place, dtype):
-            return staged.tile([P, T], dtype, name=name, align_bytes=64, offset=place * (WINDOW - OVERLAP) + (OVERLAP if place > 3 else 0))
-
-        word_tables = [
-            spare.tile([P, T], U32, name="word_table0", align_bytes=64, offset=0),
-            staged_window("word_table1", 2, U32),
-            staged_window("word_table2", 5, U32),
-        ]
-        w4_codes = held.tile([P, FP4_PASSES, 2 * M], U8, name="w4_codes", align_bytes=64)
+        last_table_place = T + (TILES + 1) * WINDOW
+        word_tables = [held.tile([P, T], U32, name="word_table%d" % a, align_bytes=64) for a in range(FP4_PASSES)]
+        word_tables.append(room.tile([P, T], U32, name="word_table2", align_bytes=64, offset=last_table_place))
+        w4_codes = room.tile([P, FP4_PASSES, 2 * M], U8, name="w4_codes", align_bytes=64, offset=last_table_place + WINDOW)
+        widths = [end - first for first, end in W8_PARTS]
         w8_raw = [
-            held.tile([P, PACK, W8_COLS], F32, name="w8_raw0", align_bytes=64),
-            staged.tile([P, PACK, W8_COLS], F32, name="w8_raw1", align_bytes=64, offset=WINDOW - OVERLAP),
+            held.tile([P, PACK, widths[0]], F32, name="w8_raw0", align_bytes=64),
+            room.tile([P, PACK, widths[1]], F32, name="w8_raw1", align_bytes=64, offset=T + TILES * WINDOW),
         ]
         w8_grouped = [
-            reused.tile([P, W8_COLS, PACK], BF16, name="w8_grouped0", align_bytes=64, offset=grouped_place),
-            held.tile([P, W8_COLS, PACK], BF16, name="w8_grouped1", align_bytes=64),
+            again.tile([P, 4 * P, PACK], BF16, name="w8_grouped0", align_bytes=64, offset=0),
+            room.tile([P, P, PACK], BF16, name="w8_grouped1", align_bytes=64, offset=T),
+            held.tile([P, widths[1], PACK], BF16, name="w8_grouped2", align_bytes=64),
         ]
-        w8_codes = [
-            held.tile([P, W8_COLS], U32, name="w8_codes0", align_bytes=64),
-            held.tile([P, W8_COLS], U32, name="w8_codes1", align_bytes=64),
-        ]
-        third_end = 4 * WINDOW - 3 * OVERLAP
-        w8_planes = [
-            reused.tile([P, W8_COLS], U8, name="w8_plane0", align_bytes=64, offset=0),
-            staged.tile([P, W8_COLS], U8, name="w8_plane1", align_bytes=64, offset=third_end - W8_COLS),
-        ]
-        residuals = [
-            spare.tile([P, T], F32, name="residual0", align_bytes=64, offset=0),
-            reused.tile([P, T], F32, name="residual1", align_bytes=64, offset=first_place),
-            staged_window("residual2", 3, F32),
-            staged_window("residual3", 4, F32),
-            staged_window("residual4", 6, F32),
-            spare.tile([P, T], F32, name="residual5", align_bytes=64, offset=0),
-            reused.tile([P, T], F32, name="residual6", align_bytes=64, offset=first_place),
-            staged.tile([P, T], F32, name="residual7", align_bytes=64, offset=third_end - W8_COLS - WINDOW),
-        ]
+        w8_codes = held.tile([P, M], U32, name="w8_codes", align_bytes=64)
+        w8_plane = held.tile([P, M], U8, name="w8_plane", align_bytes=64)
+        residuals = [room.tile([P, T], F32, name="residual%d" % m, align_bytes=64, offset=T + m * WINDOW) for m in range(TILES)]
         w8_rows = w8.rearrange("(p j) n -> p j n", j=PACK)
 
         def half_list(h):
@@ -117,112 +90,115 @@ def tile_list_tabres_gelu_kernel(tc, tab_words, tab_scales, w8, w4_words, w4_sca
             words = tab_words[a].rearrange("p t i -> p (t i)").bitcast(I32)
             nc.sync.dma_start(out=word_tables[a][:].bitcast(I32), in_=words)
 
+        def load_w8(part):
+            nc.sync.dma_start(out=w8_raw[part][:], in_=w8_rows[:, :, W8_PARTS[part][0] : W8_PARTS[part][1]])
+
         def load_residual(m):
             nc.sync.dma_start(out=residuals[m][:], in_=rT[m * P : (m + 1) * P, :])
 
-        def group_w8(part):
+        def group_w8(piece):
+            first, end = QUANTISED[piece]
+            part = 0 if end <= W8_PARTS[0][1] else 1
+            within = slice(first - W8_PARTS[part][0], end - W8_PARTS[part][0])
             nc.scalar.copy(
-                w8_grouped[part][:].rearrange("p (c i) j -> p c j i", i=4),
-                w8_raw[part][:].rearrange("p j (c i) -> p c j i", i=4),
+                w8_grouped[piece][:].rearrange("p (c i) j -> p c j i", i=4),
+                w8_raw[part][:, :, within].rearrange("p j (c i) -> p c j i", i=4),
             )
 
-        def quantise(part):
+        def quantise(piece):
+            first, end = QUANTISED[piece]
             nc.vector.quantize_mx(
-                out=w8_codes[part][:].bitcast(FP8X4),
-                scales=w8_planes[part][:],
-                in_=w8_grouped[part][:].rearrange("p n j -> p (n j)"),
+                out=w8_codes[:, first:end].bitcast(FP8X4),
+                scales=w8_plane[:, first:end],
+                in_=w8_grouped[piece][:].rearrange("p n j -> p (n j)"),
             )
 
-        load_words(0)
+        table_rows = tab_scales.bitcast(I32)
+        for a in range(PASSES):
+            nc.sync.dma_start(out=scale_table[DEALT_FROM + a : P : PASSES, :], in_=table_rows[a])
         nc.sync.dma_start(offsets[:], offs)
-        nc.sync.dma_start(out=w4_codes[:].bitcast(I32), in_=w4_words.rearrange("a p n -> p a n").bitcast(I32))
-        nc.sync.dma_start(out=w8_raw[0][:], in_=w8_rows[:, :, 0:W8_COLS])
+        load_words(0)
+        nc.sync.dma_start(out=bias_rows[P - TILES : P, :], in_=b.rearrange("(m p) -> m p", p=P))
         load_words(1)
-        nc.sync.dma_start(out=bias_rows[0:TILES, :], in_=b.rearrange("(m p) -> m p", p=P))
-        w4_rows = w4_scales.bitcast(I32).rearrange("a (q r) n -> r q a n", r=ROWS)
-        for r in range(ROWS):
-            nc.sync.dma_start(out=w4_planes[r:P:QUAD, :, :], in_=w4_rows[r])
-        load_words(2)
+        load_w8(0)
 
-        picked_words = [
-            held.tile([P, S], U32, name="picked_words0", align_bytes=64),
-            reused.tile([P, S], U32, name="picked_words1", align_bytes=64, offset=grouped_place),
-            staged.tile([P, S], U32, name="picked_words2", align_bytes=64, offset=2 * WINDOW),
-        ]
         picked_scales = held.tile([P, S], U8, name="picked_scales", align_bytes=64)
-        nc.vector.tensor_copy(picked_words[0][:], word_tables[0][:].indirect(offsets[:]))
-        load_residual(0)
-        nc.vector.tensor_copy(picked_scales[:], scale_table[:].bitcast(U8).indirect(offsets[:]))
+        nc.vector.tensor_copy(picked_scales[:], scale_table.bitcast(U8).indirect(offsets[:]))
+        quad_rows = PASSES * ROWS
+        for q in range(P // QUAD):
+            first = DEALT_FROM + q * quad_rows
+            nc.sync.dma_start(
+                out=token_planes[q * QUAD : q * QUAD + ROWS, :, :],
+                in_=picked_scales[first : first + quad_rows, :].bitcast(I32),
+            )
+        load_words(2)
+        nc.sync.dma_start(out=w4_codes[:].bitcast(I32), in_=w4_words.rearrange("a p n -> p a n").bitcast(I32))
+        for m in range(3):
+            load_residual(m)
+        load_w8(1)
+        for m in range(3, TILES):
+            load_residual(m)
+
+        picked_words = [held.tile([P, S], U32, name="picked_words%d" % a, align_bytes=64) for a in range(FP4_PASSES)]
+        last_words = [
+            again.tile([P, BANK], U32, name="last_words0", align_bytes=64, offset=0),
+            again.tile([P, BANK], U32, name="last_words1", align_bytes=64, offset=4 * BANK),
+        ]
         for a in range(FP4_PASSES):
-            first = (a + 2) * ROWS
-            nc.sync.dma_start(out=moved_planes[0:MOVED_ROWS, a, :], in_=picked_scales[first : first + MOVED_ROWS, :].bitcast(I32))
+            nc.vector.tensor_copy(picked_words[a][:], word_tables[a][:].indirect(offsets[:]))
         group_w8(0)
         quantise(0)
-        nc.vector.tensor_copy(picked_words[1][:], word_tables[1][:].indirect(offsets[:]))
         for h in range(HALVES):
-            nc.vector.tensor_copy(picked_words[2][:, h * BANK : (h + 1) * BANK], word_tables[2][:].indirect(half_list(h)))
-        load_residual(1)
-        nc.sync.dma_start(out=w8_raw[1][:], in_=w8_rows[:, :, W8_COLS:M])
-        for m in range(2, 5):
-            load_residual(m)
+            nc.vector.tensor_copy(last_words[h][:], word_tables[2][:].indirect(half_list(h)))
 
         bias_psum = turned.tile([P, BANK], F32, name="bias_psum")
         nc.tensor.transpose(bias_psum[:, 0:P], bias_rows[:], identity[:])
         bias = held.tile([P, TILES], F32, name="bias")
-        nc.scalar.copy(bias[:], bias_psum[:, 0:TILES])
+        nc.scalar.copy(bias[:], bias_psum[:, P - TILES : P])
 
         activated = held.tile([P, TILES, S], F32, name="activated")
         summed = held.tile([P, TILES, S], F32, name="summed")
         w4_scale_bytes = w4_planes[:].bitcast(U8)
-        moved_bytes = moved_planes[:].bitcast(U8)
+        token_bytes = token_planes[:].bitcast(U8)
         out_tiles = out.rearrange("(m p) j -> p m j", p=P)
 
-        def multiply(m, h, bank, a):
+        def multiply(m, h, bank, a, start, stop):
             rows = slice(m * P, (m + 1) * P)
             cols = slice(h * BANK, (h + 1) * BANK)
             if a == 0:
-                part, within = m // PART_TILES, slice(m % PART_TILES * P, (m % PART_TILES + 1) * P)
-                weights = w8_codes[part][:, within].bitcast(FP8X4)
-                weight_scales, token_scales = w8_planes[part][:, within], picked_scales[ROWS:P, cols]
+                weights, weight_scales = w8_codes[:, rows].bitcast(FP8X4), w8_plane[:, rows]
             else:
                 weights = w4_codes[:, a - 1, 2 * m * P : 2 * (m + 1) * P].bitcast(FP4X4)
-                weight_scales, token_scales = w4_scale_bytes[:, a - 1, rows], moved_bytes[:, a - 1, cols]
+                weight_scales = w4_scale_bytes[:, a - 1, rows]
+            tokens = last_words[h][:] if a == PASSES - 1 else picked_words[a][:, cols]
             nc.tensor.matmul_mx(
                 out=bank[:],
                 lhsT=weights,
                 lhsT_scale=weight_scales,
-                rhs=picked_words[a][:, cols].bitcast(FP8X4),
-                rhs_scale=token_scales,
-                start=a == PASS_ORDERS[m // PART_TILES][0],
-                stop=a == PASS_ORDERS[m // PART_TILES][-1],
+                rhs=tokens.bitcast(FP8X4),
+                rhs_scale=token_bytes[:, a, cols],
+                start=start,
+                stop=stop,
             )
 
-        def new_banks():
-            return [psum.tile([P, BANK], F32, name="bank") for h in range(HALVES)]
-
-        early_banks = [new_banks() for m in range(EARLY_TILES)]
-        for m in range(EARLY_TILES):
-            for h in range(HALVES):
-                multiply(m, h, early_banks[m][h], 0)
         for m in range(TILES):
-            banks = early_banks[m] if m < EARLY_TILES else new_banks()
+            order = [0, 1, 2] if m < FIRST_TILES - 1 else [1, 2, 0]
             for h in range(HALVES):
                 cols = slice(h * BANK, (h + 1) * BANK)
-                for a in PASS_ORDERS[m // PART_TILES][1 if m < EARLY_TILES else 0 :]:
-                    multiply(m, h, banks[h], a)
-                nc.scalar.activation(activated[:, m, cols], banks[h][:], GELU, bias=bias[:, m : m + 1])
+                bank = psum.tile([P, BANK], F32, name="bank")
+                for a in order:
+                    multiply(m, h, bank, a, a == order[0], a == order[-1])
+                nc.scalar.activation(activated[:, m, cols], bank[:], GELU, bias=bias[:, m : m + 1])
+
                 if m in (0, TILES - 1):
                     nc.vector.tensor_tensor(summed[:, m, cols], residuals[m][:].indirect(half_list(h)), activated[:, m, cols], ADD)
                 if m == TILES - 1:
                     nc.sync.dma_start(out=out_tiles[:, m, cols], in_=summed[:, m, cols])
             if m not in (0, TILES - 1):
                 nc.vector.tensor_tensor(summed[:, m, :], residuals[m][:].indirect(offsets[:]), activated[:, m, :], ADD)
-            for later in LOADED_AFTER.get(m, ()):
-                load_residual(later)
-            if m == 1:
-                group_w8(1)
-            if m == 2:
-                quantise(1)
+            if m in (0, 2):
+                group_w8(1 + m // 2)
+                quantise(1 + m // 2)
             if m + 1 in STORE_ENDS:
                 place = STORE_ENDS.index(m + 1)
                 tiles = slice(STORE_ENDS[place - 1] if place else 0, m + 1)

@@ -29,11 +29,10 @@ HALVES = S // BANK
 LIST_ROWS = 16
 SCALE_ROWS = P * PACK // QUAD
 DEALT_FROM = P - PASSES * SCALE_ROWS
-FIRST_TILES = 5
-W8_PARTS = [(0, FIRST_TILES * P), (FIRST_TILES * P, M)]
-QUANTISED = [(0, 4 * P), (4 * P, FIRST_TILES * P), (FIRST_TILES * P, M)]
+W8_PIECES = 2
+W8_COLS = M // W8_PIECES
 WINDOW = 4 * T
-STORE_ENDS = [4, 6, 7]
+STORE_ENDS = [3, 5, 6, 7]
 
 
 def tile_list_tabres_gelu_kernel(tc, tab_words, tab_scales, w8, w4_words, w4_scales, rT, b, offs, out):
@@ -41,12 +40,11 @@ def tile_list_tabres_gelu_kernel(tc, tab_words, tab_scales, w8, w4_words, w4_sca
     with ExitStack() as ctx:
         held = ctx.enter_context(tc.tile_pool(name="held", bufs=1))
         room = ctx.enter_context(tc.tile_pool(name="room", bufs=1))
-        again = ctx.enter_context(tc.tile_pool(name="again", bufs=1))
         psum = ctx.enter_context(tc.psum_pool(name="psum", bufs=4))
         turned = ctx.enter_context(tc.psum_pool(name="turned", bufs=1))
 
         offsets = held.tile([P, S // LIST_ROWS], U16, name="offsets")
-        scale_room = room.tile([P, (T + (TILES + 3) * WINDOW) // 4], I32, name="scale_room", align_bytes=64, offset=0)
+        scale_room = room.tile([P, (T + (TILES + 2) * WINDOW) // 4], I32, name="scale_room", align_bytes=64, offset=0)
         scale_table = scale_room[:, 0 : T // 4]
         token_planes = held.tile([P, PASSES, S // 4], I32, name="token_planes", align_bytes=64)
         w4_planes = held.tile([P, FP4_PASSES, M // 4], I32, name="w4_planes", align_bytes=64)
@@ -64,24 +62,15 @@ def tile_list_tabres_gelu_kernel(tc, tab_words, tab_scales, w8, w4_words, w4_sca
             nc.gpsimd.dma_start(out=w4_planes[q * QUAD : q * QUAD + ROWS, :, :], in_=w4_rows[q])
         make_identity(nc, identity[:])
 
-        last_table_place = T + (TILES + 1) * WINDOW
+        last_table_place = T + TILES * WINDOW
         word_tables = [held.tile([P, T], U32, name="word_table%d" % a, align_bytes=64) for a in range(FP4_PASSES)]
         word_tables.append(room.tile([P, T], U32, name="word_table2", align_bytes=64, offset=last_table_place))
         w4_codes = room.tile([P, FP4_PASSES, 2 * M], U8, name="w4_codes", align_bytes=64, offset=last_table_place + WINDOW)
-        widths = [end - first for first, end in W8_PARTS]
-        w8_raw = [
-            held.tile([P, PACK, widths[0]], F32, name="w8_raw0", align_bytes=64),
-            room.tile([P, PACK, widths[1]], F32, name="w8_raw1", align_bytes=64, offset=T + TILES * WINDOW),
-        ]
-        w8_grouped = [
-            again.tile([P, 4 * P, PACK], BF16, name="w8_grouped0", align_bytes=64, offset=0),
-            room.tile([P, P, PACK], BF16, name="w8_grouped1", align_bytes=64, offset=T),
-            held.tile([P, widths[1], PACK], BF16, name="w8_grouped2", align_bytes=64),
-        ]
+        w8_raw = held.tile([P, PACK, M], F32, name="w8_raw", align_bytes=64)
+        w8_grouped = [held.tile([P, W8_COLS, PACK], BF16, name="w8_grouped%d" % i, align_bytes=64) for i in range(W8_PIECES)]
         w8_codes = held.tile([P, M], U32, name="w8_codes", align_bytes=64)
         w8_plane = held.tile([P, M], U8, name="w8_plane", align_bytes=64)
         residuals = [room.tile([P, T], F32, name="residual%d" % m, align_bytes=64, offset=T + m * WINDOW) for m in range(TILES)]
-        w8_rows = w8.rearrange("(p j) n -> p j n", j=PACK)
 
         def half_list(h):
             return offsets[:, h * BANK // LIST_ROWS : (h + 1) * BANK // LIST_ROWS]
@@ -90,26 +79,21 @@ def tile_list_tabres_gelu_kernel(tc, tab_words, tab_scales, w8, w4_words, w4_sca
             words = tab_words[a].rearrange("p t i -> p (t i)").bitcast(I32)
             nc.sync.dma_start(out=word_tables[a][:].bitcast(I32), in_=words)
 
-        def load_w8(part):
-            nc.sync.dma_start(out=w8_raw[part][:], in_=w8_rows[:, :, W8_PARTS[part][0] : W8_PARTS[part][1]])
-
         def load_residual(m):
             nc.sync.dma_start(out=residuals[m][:], in_=rT[m * P : (m + 1) * P, :])
 
         def group_w8(piece):
-            first, end = QUANTISED[piece]
-            part = 0 if end <= W8_PARTS[0][1] else 1
-            within = slice(first - W8_PARTS[part][0], end - W8_PARTS[part][0])
-            nc.scalar.copy(
+            copy = nc.vector.tensor_copy if piece == 0 else nc.scalar.copy
+            copy(
                 w8_grouped[piece][:].rearrange("p (c i) j -> p c j i", i=4),
-                w8_raw[part][:, :, within].rearrange("p j (c i) -> p c j i", i=4),
+                w8_raw[:, :, piece * W8_COLS : (piece + 1) * W8_COLS].rearrange("p j (c i) -> p c j i", i=4),
             )
 
         def quantise(piece):
-            first, end = QUANTISED[piece]
+            cols = slice(piece * W8_COLS, (piece + 1) * W8_COLS)
             nc.vector.quantize_mx(
-                out=w8_codes[:, first:end].bitcast(FP8X4),
-                scales=w8_plane[:, first:end],
+                out=w8_codes[:, cols].bitcast(FP8X4),
+                scales=w8_plane[:, cols],
                 in_=w8_grouped[piece][:].rearrange("p n j -> p (n j)"),
             )
 
@@ -120,7 +104,7 @@ def tile_list_tabres_gelu_kernel(tc, tab_words, tab_scales, w8, w4_words, w4_sca
         load_words(0)
         nc.sync.dma_start(out=bias_rows[P - TILES : P, :], in_=b.rearrange("(m p) -> m p", p=P))
         load_words(1)
-        load_w8(0)
+        nc.sync.dma_start(out=w8_raw[:], in_=w8.rearrange("(p j) n -> p j n", j=PACK))
 
         picked_scales = held.tile([P, S], U8, name="picked_scales", align_bytes=64)
         nc.vector.tensor_copy(picked_scales[:], scale_table.bitcast(U8).indirect(offsets[:]))
@@ -133,23 +117,18 @@ def tile_list_tabres_gelu_kernel(tc, tab_words, tab_scales, w8, w4_words, w4_sca
             )
         load_words(2)
         nc.sync.dma_start(out=w4_codes[:].bitcast(I32), in_=w4_words.rearrange("a p n -> p a n").bitcast(I32))
-        for m in range(3):
-            load_residual(m)
-        load_w8(1)
-        for m in range(3, TILES):
+        for m in range(TILES):
             load_residual(m)
 
-        picked_words = [held.tile([P, S], U32, name="picked_words%d" % a, align_bytes=64) for a in range(FP4_PASSES)]
-        last_words = [
-            again.tile([P, BANK], U32, name="last_words0", align_bytes=64, offset=0),
-            again.tile([P, BANK], U32, name="last_words1", align_bytes=64, offset=4 * BANK),
-        ]
+        picked_words = [held.tile([P, S], U32, name="picked_words%d" % a, align_bytes=64) for a in range(PASSES)]
         for a in range(FP4_PASSES):
             nc.vector.tensor_copy(picked_words[a][:], word_tables[a][:].indirect(offsets[:]))
-        group_w8(0)
+        for piece in range(W8_PIECES):
+            group_w8(piece)
         quantise(0)
         for h in range(HALVES):
-            nc.vector.tensor_copy(last_words[h][:], word_tables[2][:].indirect(half_list(h)))
+            nc.vector.tensor_copy(picked_words[2][:, h * BANK : (h + 1) * BANK], word_tables[2][:].indirect(half_list(h)))
+        quantise(1)
 
         bias_psum = turned.tile([P, BANK], F32, name="bias_psum")
         nc.tensor.transpose(bias_psum[:, 0:P], bias_rows[:], identity[:])
@@ -157,7 +136,7 @@ def tile_list_tabres_gelu_kernel(tc, tab_words, tab_scales, w8, w4_words, w4_sca
         nc.scalar.copy(bias[:], bias_psum[:, P - TILES : P])
 
         activated = held.tile([P, TILES, S], F32, name="activated")
-        summed = held.tile([P, TILES, S], F32, name="summed")
+        picked = held.tile([P, TILES, S], F32, name="picked")
         w4_scale_bytes = w4_planes[:].bitcast(U8)
         token_bytes = token_planes[:].bitcast(U8)
         out_tiles = out.rearrange("(m p) j -> p m j", p=P)
@@ -170,36 +149,31 @@ def tile_list_tabres_gelu_kernel(tc, tab_words, tab_scales, w8, w4_words, w4_sca
             else:
                 weights = w4_codes[:, a - 1, 2 * m * P : 2 * (m + 1) * P].bitcast(FP4X4)
                 weight_scales = w4_scale_bytes[:, a - 1, rows]
-            tokens = last_words[h][:] if a == PASSES - 1 else picked_words[a][:, cols]
             nc.tensor.matmul_mx(
                 out=bank[:],
                 lhsT=weights,
                 lhsT_scale=weight_scales,
-                rhs=tokens.bitcast(FP8X4),
+                rhs=picked_words[a][:, cols].bitcast(FP8X4),
                 rhs_scale=token_bytes[:, a, cols],
                 start=start,
                 stop=stop,
             )
 
         for m in range(TILES):
-            order = [0, 1, 2] if m < FIRST_TILES - 1 else [1, 2, 0]
+            if m < TILES - 1:
+                nc.vector.tensor_copy(picked[:, m, :], residuals[m][:].indirect(offsets[:]))
             for h in range(HALVES):
                 cols = slice(h * BANK, (h + 1) * BANK)
                 bank = psum.tile([P, BANK], F32, name="bank")
-                for a in order:
-                    multiply(m, h, bank, a, a == order[0], a == order[-1])
+                for a in range(PASSES):
+                    multiply(m, h, bank, a, a == 0, a == PASSES - 1)
                 nc.scalar.activation(activated[:, m, cols], bank[:], GELU, bias=bias[:, m : m + 1])
-
-                if m in (0, TILES - 1):
-                    nc.vector.tensor_tensor(summed[:, m, cols], residuals[m][:].indirect(half_list(h)), activated[:, m, cols], ADD)
                 if m == TILES - 1:
-                    nc.sync.dma_start(out=out_tiles[:, m, cols], in_=summed[:, m, cols])
-            if m not in (0, TILES - 1):
-                nc.vector.tensor_tensor(summed[:, m, :], residuals[m][:].indirect(offsets[:]), activated[:, m, :], ADD)
-            if m in (0, 2):
-                group_w8(1 + m // 2)
-                quantise(1 + m // 2)
+                    nc.vector.tensor_tensor(picked[:, m, cols], residuals[m][:].indirect(half_list(h)), activated[:, m, cols], ADD)
+                    nc.sync.dma_start(out=out_tiles[:, m, cols], in_=picked[:, m, cols])
+            if m < TILES - 1:
+                nc.gpsimd.tensor_tensor(picked[:, m, :], picked[:, m, :], activated[:, m, :], ADD)
             if m + 1 in STORE_ENDS:
                 place = STORE_ENDS.index(m + 1)
                 tiles = slice(STORE_ENDS[place - 1] if place else 0, m + 1)
-                nc.sync.dma_start(out=out_tiles[:, tiles, :], in_=summed[:, tiles, :])
+                nc.sync.dma_start(out=out_tiles[:, tiles, :], in_=picked[:, tiles, :])

@@ -32,7 +32,8 @@ DEALT_FROM = P - PASSES * SCALE_ROWS
 W8_PIECES = 2
 W8_COLS = M // W8_PIECES
 WINDOW = 4 * T
-STORE_ENDS = [3, 5, 6, 7]
+PIECE_TILES = TILES // W8_PIECES
+STORE_ENDS = [4, 6, 7]
 
 
 def tile_list_tabres_gelu_kernel(tc, tab_words, tab_scales, w8, w4_words, w4_scales, rT, b, offs, out):
@@ -40,7 +41,7 @@ def tile_list_tabres_gelu_kernel(tc, tab_words, tab_scales, w8, w4_words, w4_sca
     with ExitStack() as ctx:
         held = ctx.enter_context(tc.tile_pool(name="held", bufs=1))
         room = ctx.enter_context(tc.tile_pool(name="room", bufs=1))
-        psum = ctx.enter_context(tc.psum_pool(name="psum", bufs=4))
+        psum = ctx.enter_context(tc.psum_pool(name="psum", bufs=1))
         turned = ctx.enter_context(tc.psum_pool(name="turned", bufs=1))
 
         offsets = held.tile([P, S // LIST_ROWS], U16, name="offsets")
@@ -136,7 +137,7 @@ def tile_list_tabres_gelu_kernel(tc, tab_words, tab_scales, w8, w4_words, w4_sca
         nc.scalar.copy(bias[:], bias_psum[:, P - TILES : P])
 
         activated = held.tile([P, TILES, S], F32, name="activated")
-        picked = held.tile([P, TILES, S], F32, name="picked")
+        summed = held.tile([P, TILES, S], F32, name="summed")
         w4_scale_bytes = w4_planes[:].bitcast(U8)
         token_bytes = token_planes[:].bitcast(U8)
         out_tiles = out.rearrange("(m p) j -> p m j", p=P)
@@ -160,20 +161,20 @@ def tile_list_tabres_gelu_kernel(tc, tab_words, tab_scales, w8, w4_words, w4_sca
             )
 
         for m in range(TILES):
-            if m < TILES - 1:
-                nc.vector.tensor_copy(picked[:, m, :], residuals[m][:].indirect(offsets[:]))
+            pair = 0 if m < PIECE_TILES else (m + 1) % 2
             for h in range(HALVES):
                 cols = slice(h * BANK, (h + 1) * BANK)
-                bank = psum.tile([P, BANK], F32, name="bank")
+                bank = psum.tile([P, BANK], F32, name="bank%d" % (HALVES * pair + h))
                 for a in range(PASSES):
                     multiply(m, h, bank, a, a == 0, a == PASSES - 1)
                 nc.scalar.activation(activated[:, m, cols], bank[:], GELU, bias=bias[:, m : m + 1])
+                if m in (0, TILES - 1):
+                    nc.vector.tensor_tensor(summed[:, m, cols], residuals[m][:].indirect(half_list(h)), activated[:, m, cols], ADD)
                 if m == TILES - 1:
-                    nc.vector.tensor_tensor(picked[:, m, cols], residuals[m][:].indirect(half_list(h)), activated[:, m, cols], ADD)
-                    nc.sync.dma_start(out=out_tiles[:, m, cols], in_=picked[:, m, cols])
-            if m < TILES - 1:
-                nc.gpsimd.tensor_tensor(picked[:, m, :], picked[:, m, :], activated[:, m, :], ADD)
+                    nc.sync.dma_start(out=out_tiles[:, m, cols], in_=summed[:, m, cols])
+            if m not in (0, TILES - 1):
+                nc.vector.tensor_tensor(summed[:, m, :], residuals[m][:].indirect(offsets[:]), activated[:, m, :], ADD)
             if m + 1 in STORE_ENDS:
                 place = STORE_ENDS.index(m + 1)
                 tiles = slice(STORE_ENDS[place - 1] if place else 0, m + 1)
-                nc.sync.dma_start(out=out_tiles[:, tiles, :], in_=picked[:, tiles, :])
+                nc.sync.dma_start(out=out_tiles[:, tiles, :], in_=summed[:, tiles, :])

@@ -31,9 +31,11 @@ SCALE_ROWS = P * PACK // QUAD
 DEALT_FROM = P - PASSES * SCALE_ROWS
 W8_PIECES = 2
 W8_COLS = M // W8_PIECES
+VECTOR_COLS = 5 * P
 WINDOW = 4 * T
 PIECE_TILES = TILES // W8_PIECES
 STORE_ENDS = [4, 6, 7]
+LAST_CUTS = [768,256]
 
 
 def tile_list_tabres_gelu_kernel(tc, tab_words, tab_scales, w8, w4_words, w4_scales, rT, b, offs, out):
@@ -41,6 +43,7 @@ def tile_list_tabres_gelu_kernel(tc, tab_words, tab_scales, w8, w4_words, w4_sca
     with ExitStack() as ctx:
         held = ctx.enter_context(tc.tile_pool(name="held", bufs=1))
         room = ctx.enter_context(tc.tile_pool(name="room", bufs=1))
+        again = ctx.enter_context(tc.tile_pool(name="again", bufs=1))
         psum = ctx.enter_context(tc.psum_pool(name="psum", bufs=1))
         turned = ctx.enter_context(tc.psum_pool(name="turned", bufs=1))
 
@@ -66,28 +69,38 @@ def tile_list_tabres_gelu_kernel(tc, tab_words, tab_scales, w8, w4_words, w4_sca
         last_table_place = T + TILES * WINDOW
         word_tables = [held.tile([P, T], U32, name="word_table%d" % a, align_bytes=64) for a in range(FP4_PASSES)]
         word_tables.append(room.tile([P, T], U32, name="word_table2", align_bytes=64, offset=last_table_place))
-        w4_codes = room.tile([P, FP4_PASSES, 2 * M], U8, name="w4_codes", align_bytes=64, offset=last_table_place + WINDOW)
+        w4_codes = [
+            room.tile([P, FP4_PASSES, 2 * W8_COLS], U8, name="w4_codes%d" % i, align_bytes=64, offset=last_table_place + WINDOW + i * FP4_PASSES * 2 * W8_COLS)
+            for i in range(W8_PIECES)
+        ]
         w8_raw = held.tile([P, PACK, M], F32, name="w8_raw", align_bytes=64)
-        w8_grouped = [held.tile([P, W8_COLS, PACK], BF16, name="w8_grouped%d" % i, align_bytes=64) for i in range(W8_PIECES)]
+        w8_grouped = [
+            held.tile([P, W8_COLS, PACK], BF16, name="w8_grouped0", align_bytes=64),
+            again.tile([P, W8_COLS, PACK], BF16, name="w8_grouped1", align_bytes=64, offset=0),
+        ]
         w8_codes = held.tile([P, M], U32, name="w8_codes", align_bytes=64)
         w8_plane = held.tile([P, M], U8, name="w8_plane", align_bytes=64)
         residuals = [room.tile([P, T], F32, name="residual%d" % m, align_bytes=64, offset=T + m * WINDOW) for m in range(TILES)]
 
-        def half_list(h):
-            return offsets[:, h * BANK // LIST_ROWS : (h + 1) * BANK // LIST_ROWS]
+        def entries(first, count):
+            return offsets[:, first // LIST_ROWS : (first + count) // LIST_ROWS]
 
         def load_words(a):
             words = tab_words[a].rearrange("p t i -> p (t i)").bitcast(I32)
             nc.sync.dma_start(out=word_tables[a][:].bitcast(I32), in_=words)
 
+        def load_w4(piece):
+            words = w4_words.rearrange("a p n -> p a n")[:, :, 2 * piece * W8_COLS : 2 * (piece + 1) * W8_COLS]
+            nc.sync.dma_start(out=w4_codes[piece][:].bitcast(I32), in_=words.bitcast(I32))
+
         def load_residual(m):
             nc.sync.dma_start(out=residuals[m][:], in_=rT[m * P : (m + 1) * P, :])
 
-        def group_w8(piece):
-            copy = nc.vector.tensor_copy if piece == 0 else nc.scalar.copy
+        def group_w8(copy, first, end):
+            piece, within = divmod(first, W8_COLS)
             copy(
-                w8_grouped[piece][:].rearrange("p (c i) j -> p c j i", i=4),
-                w8_raw[:, :, piece * W8_COLS : (piece + 1) * W8_COLS].rearrange("p j (c i) -> p c j i", i=4),
+                w8_grouped[piece][:, within : within + end - first, :].rearrange("p (c i) j -> p c j i", i=4),
+                w8_raw[:, :, first:end].rearrange("p j (c i) -> p c j i", i=4),
             )
 
         def quantise(piece):
@@ -117,19 +130,23 @@ def tile_list_tabres_gelu_kernel(tc, tab_words, tab_scales, w8, w4_words, w4_sca
                 in_=picked_scales[first : first + quad_rows, :].bitcast(I32),
             )
         load_words(2)
-        nc.sync.dma_start(out=w4_codes[:].bitcast(I32), in_=w4_words.rearrange("a p n -> p a n").bitcast(I32))
+        load_w4(0)
         for m in range(TILES):
             load_residual(m)
+            if m == 1:
+                load_w4(1)
 
-        picked_words = [held.tile([P, S], U32, name="picked_words%d" % a, align_bytes=64) for a in range(PASSES)]
+        picked_words = [held.tile([P, S], U32, name="picked_words%d" % a, align_bytes=64) for a in range(FP4_PASSES)]
+        picked_words.append(again.tile([P, S], U32, name="picked_words2", align_bytes=64, offset=0))
         for a in range(FP4_PASSES):
             nc.vector.tensor_copy(picked_words[a][:], word_tables[a][:].indirect(offsets[:]))
-        for piece in range(W8_PIECES):
-            group_w8(piece)
+        group_w8(nc.vector.tensor_copy, 0, W8_COLS)
+        group_w8(nc.scalar.copy, VECTOR_COLS, M)
         quantise(0)
-        for h in range(HALVES):
-            nc.vector.tensor_copy(picked_words[2][:, h * BANK : (h + 1) * BANK], word_tables[2][:].indirect(half_list(h)))
+        group_w8(nc.vector.tensor_copy, W8_COLS, VECTOR_COLS)
         quantise(1)
+        for h in range(HALVES):
+            nc.vector.tensor_copy(picked_words[2][:, h * BANK : (h + 1) * BANK], word_tables[2][:].indirect(entries(h * BANK, BANK)))
 
         bias_psum = turned.tile([P, BANK], F32, name="bias_psum")
         nc.tensor.transpose(bias_psum[:, 0:P], bias_rows[:], identity[:])
@@ -148,7 +165,8 @@ def tile_list_tabres_gelu_kernel(tc, tab_words, tab_scales, w8, w4_words, w4_sca
             if a == 0:
                 weights, weight_scales = w8_codes[:, rows].bitcast(FP8X4), w8_plane[:, rows]
             else:
-                weights = w4_codes[:, a - 1, 2 * m * P : 2 * (m + 1) * P].bitcast(FP4X4)
+                piece, within = divmod(m, PIECE_TILES)
+                weights = w4_codes[piece][:, a - 1, 2 * within * P : 2 * (within + 1) * P].bitcast(FP4X4)
                 weight_scales = w4_scale_bytes[:, a - 1, rows]
             nc.tensor.matmul_mx(
                 out=bank[:],
@@ -162,18 +180,20 @@ def tile_list_tabres_gelu_kernel(tc, tab_words, tab_scales, w8, w4_words, w4_sca
 
         for m in range(TILES):
             pair = 0 if m < PIECE_TILES else (m + 1) % 2
+            order = [0, 1, 2] if m < PIECE_TILES else [1, 2, 0]
             for h in range(HALVES):
                 cols = slice(h * BANK, (h + 1) * BANK)
                 bank = psum.tile([P, BANK], F32, name="bank%d" % (HALVES * pair + h))
-                for a in range(PASSES):
-                    multiply(m, h, bank, a, a == 0, a == PASSES - 1)
+                for a in order:
+                    multiply(m, h, bank, a, a == order[0], a == order[-1])
                 nc.scalar.activation(activated[:, m, cols], bank[:], GELU, bias=bias[:, m : m + 1])
-                if m in (0, TILES - 1):
-                    nc.vector.tensor_tensor(summed[:, m, cols], residuals[m][:].indirect(half_list(h)), activated[:, m, cols], ADD)
+            cuts = [BANK, BANK] if m == 0 else LAST_CUTS if m == TILES - 1 else [S]
+            for i, count in enumerate(cuts):
+                first = sum(cuts[:i])
+                cols = slice(first, first + count)
+                nc.vector.tensor_tensor(summed[:, m, cols], residuals[m][:].indirect(entries(first, count)), activated[:, m, cols], ADD)
                 if m == TILES - 1:
                     nc.sync.dma_start(out=out_tiles[:, m, cols], in_=summed[:, m, cols])
-            if m not in (0, TILES - 1):
-                nc.vector.tensor_tensor(summed[:, m, :], residuals[m][:].indirect(offsets[:]), activated[:, m, :], ADD)
             if m + 1 in STORE_ENDS:
                 place = STORE_ENDS.index(m + 1)
                 tiles = slice(STORE_ENDS[place - 1] if place else 0, m + 1)

@@ -34,7 +34,7 @@ W8_COLS = M // W8_PIECES
 VECTOR_COLS = 5 * P
 WINDOW = 4 * T
 PIECE_TILES = TILES // W8_PIECES
-STORE_ENDS = [4, 6, 7]
+STORE_ENDS = [4,6,7]
 LAST_CUTS = [768,256]
 
 
@@ -69,10 +69,7 @@ def tile_list_tabres_gelu_kernel(tc, tab_words, tab_scales, w8, w4_words, w4_sca
         last_table_place = T + TILES * WINDOW
         word_tables = [held.tile([P, T], U32, name="word_table%d" % a, align_bytes=64) for a in range(FP4_PASSES)]
         word_tables.append(room.tile([P, T], U32, name="word_table2", align_bytes=64, offset=last_table_place))
-        w4_codes = [
-            room.tile([P, FP4_PASSES, 2 * W8_COLS], U8, name="w4_codes%d" % i, align_bytes=64, offset=last_table_place + WINDOW + i * FP4_PASSES * 2 * W8_COLS)
-            for i in range(W8_PIECES)
-        ]
+        w4_codes = room.tile([P, FP4_PASSES, 2 * M], U8, name="w4_codes", align_bytes=64, offset=last_table_place + WINDOW)
         w8_raw = held.tile([P, PACK, M], F32, name="w8_raw", align_bytes=64)
         w8_grouped = [
             held.tile([P, W8_COLS, PACK], BF16, name="w8_grouped0", align_bytes=64),
@@ -88,10 +85,6 @@ def tile_list_tabres_gelu_kernel(tc, tab_words, tab_scales, w8, w4_words, w4_sca
         def load_words(a):
             words = tab_words[a].rearrange("p t i -> p (t i)").bitcast(I32)
             nc.sync.dma_start(out=word_tables[a][:].bitcast(I32), in_=words)
-
-        def load_w4(piece):
-            words = w4_words.rearrange("a p n -> p a n")[:, :, 2 * piece * W8_COLS : 2 * (piece + 1) * W8_COLS]
-            nc.sync.dma_start(out=w4_codes[piece][:].bitcast(I32), in_=words.bitcast(I32))
 
         def load_residual(m):
             nc.sync.dma_start(out=residuals[m][:], in_=rT[m * P : (m + 1) * P, :])
@@ -112,8 +105,9 @@ def tile_list_tabres_gelu_kernel(tc, tab_words, tab_scales, w8, w4_words, w4_sca
             )
 
         table_rows = tab_scales.bitcast(I32)
-        for a in range(PASSES):
-            nc.sync.dma_start(out=scale_table[DEALT_FROM + a : P : PASSES, :], in_=table_rows[a])
+        fp4_from = DEALT_FROM + SCALE_ROWS
+        nc.sync.dma_start(out=scale_table[fp4_from:P, :], in_=table_rows[1:PASSES].rearrange("a q t -> q a t"))
+        nc.sync.dma_start(out=scale_table[DEALT_FROM:fp4_from, :], in_=table_rows[0])
         nc.sync.dma_start(offsets[:], offs)
         load_words(0)
         nc.sync.dma_start(out=bias_rows[P - TILES : P, :], in_=b.rearrange("(m p) -> m p", p=P))
@@ -122,19 +116,17 @@ def tile_list_tabres_gelu_kernel(tc, tab_words, tab_scales, w8, w4_words, w4_sca
 
         picked_scales = held.tile([P, S], U8, name="picked_scales", align_bytes=64)
         nc.vector.tensor_copy(picked_scales[:], scale_table.bitcast(U8).indirect(offsets[:]))
-        quad_rows = PASSES * ROWS
+        picked_rows = picked_scales[:].bitcast(I32)
         for q in range(P // QUAD):
-            first = DEALT_FROM + q * quad_rows
-            nc.sync.dma_start(
-                out=token_planes[q * QUAD : q * QUAD + ROWS, :, :],
-                in_=picked_scales[first : first + quad_rows, :].bitcast(I32),
-            )
+            first = DEALT_FROM + q * ROWS
+            nc.sync.dma_start(out=token_planes[q * QUAD + ROWS : q * QUAD + 2 * ROWS, 0, :], in_=picked_rows[first : first + ROWS, :])
         load_words(2)
-        load_w4(0)
+        for q in range(P // QUAD):
+            first = fp4_from + q * FP4_PASSES * ROWS
+            nc.sync.dma_start(out=token_planes[q * QUAD : q * QUAD + ROWS, 1:PASSES, :], in_=picked_rows[first : first + FP4_PASSES * ROWS, :])
+        nc.sync.dma_start(out=w4_codes[:].bitcast(I32), in_=w4_words.rearrange("a p n -> p a n").bitcast(I32))
         for m in range(TILES):
             load_residual(m)
-            if m == 1:
-                load_w4(1)
 
         picked_words = [held.tile([P, S], U32, name="picked_words%d" % a, align_bytes=64) for a in range(FP4_PASSES)]
         picked_words.append(again.tile([P, S], U32, name="picked_words2", align_bytes=64, offset=0))
@@ -164,16 +156,16 @@ def tile_list_tabres_gelu_kernel(tc, tab_words, tab_scales, w8, w4_words, w4_sca
             cols = slice(h * BANK, (h + 1) * BANK)
             if a == 0:
                 weights, weight_scales = w8_codes[:, rows].bitcast(FP8X4), w8_plane[:, rows]
+                token_scales = token_bytes[ROWS:P, 0, cols]
             else:
-                piece, within = divmod(m, PIECE_TILES)
-                weights = w4_codes[piece][:, a - 1, 2 * within * P : 2 * (within + 1) * P].bitcast(FP4X4)
-                weight_scales = w4_scale_bytes[:, a - 1, rows]
+                weights = w4_codes[:, a - 1, 2 * m * P : 2 * (m + 1) * P].bitcast(FP4X4)
+                weight_scales, token_scales = w4_scale_bytes[:, a - 1, rows], token_bytes[:, a, cols]
             nc.tensor.matmul_mx(
                 out=bank[:],
                 lhsT=weights,
                 lhsT_scale=weight_scales,
                 rhs=picked_words[a][:, cols].bitcast(FP8X4),
-                rhs_scale=token_bytes[:, a, cols],
+                rhs_scale=token_scales,
                 start=start,
                 stop=stop,
             )

@@ -28,72 +28,83 @@ TILES = M // P
 HALVES = S // BANK
 LIST_ROWS = 16
 SCALE_ROWS = P * PACK // QUAD
-DEALT_FROM = P - PASSES * SCALE_ROWS
+FP8_FROM = QUAD - SCALE_ROWS
+FP4_FROM = P - FP4_PASSES * SCALE_ROWS
 W8_PIECES = 2
 W8_COLS = M // W8_PIECES
-VECTOR_COLS = 5 * P
-WINDOW = 4 * T
 PIECE_TILES = TILES // W8_PIECES
-STORE_ENDS = [4,6,7]
-LAST_CUTS = [768,256]
+STORE_ENDS = [4, 6, 7]
+LAST_CUTS = [768, 256]
 
 
 def tile_list_tabres_gelu_kernel(tc, tab_words, tab_scales, w8, w4_words, w4_scales, rT, b, offs, out):
     nc = tc.nc
     with ExitStack() as ctx:
         held = ctx.enter_context(tc.tile_pool(name="held", bufs=1))
-        room = ctx.enter_context(tc.tile_pool(name="room", bufs=1))
-        again = ctx.enter_context(tc.tile_pool(name="again", bufs=1))
         psum = ctx.enter_context(tc.psum_pool(name="psum", bufs=1))
         turned = ctx.enter_context(tc.psum_pool(name="turned", bufs=1))
 
         offsets = held.tile([P, S // LIST_ROWS], U16, name="offsets")
-        scale_room = room.tile([P, (T + (TILES + 2) * WINDOW) // 4], I32, name="scale_room", align_bytes=64, offset=0)
-        scale_table = scale_room[:, 0 : T // 4]
+        scale_table = held.tile([P, T // 4], I32, name="scale_table", align_bytes=64)
         token_planes = held.tile([P, PASSES, S // 4], I32, name="token_planes", align_bytes=64)
         w4_planes = held.tile([P, FP4_PASSES, M // 4], I32, name="w4_planes", align_bytes=64)
         bias_rows = held.tile([P, P], F32, name="bias_rows")
         identity = held.tile([P, P], F32, name="identity")
+        word_tables = [held.tile([P, T], U32, name="word_table%d" % a, align_bytes=64) for a in range(PASSES)]
+        w4_codes = held.tile([P, FP4_PASSES, 2 * M], U8, name="w4_codes", align_bytes=64)
+        w8_raw = held.tile([P, PACK, M], F32, name="w8_raw", align_bytes=64)
+        residuals = [held.tile([P, T], F32, name="residual%d" % m, align_bytes=64) for m in range(TILES)]
 
-        nc.vector.memset(scale_table[0:64, :], 0)
-        nc.vector.memset(scale_table[64:DEALT_FROM, :], 0)
+        nc.vector.memset(scale_table[0:FP8_FROM, :], 0)
+        nc.vector.memset(scale_table[QUAD : 2 * QUAD, :], 0)
+        nc.vector.memset(scale_table[2 * QUAD : FP4_FROM, :], 0)
         nc.vector.memset(bias_rows[0:96, :], 0.0)
         nc.vector.memset(bias_rows[96 : P - TILES, :], 0.0)
         nc.vector.memset(token_planes[:], 0)
         nc.gpsimd.memset(w4_planes[:], 0)
-        w4_rows = w4_scales.bitcast(I32).rearrange("a (q r) n -> q r a n", r=ROWS)
-        for q in range(P // QUAD):
-            nc.gpsimd.dma_start(out=w4_planes[q * QUAD : q * QUAD + ROWS, :, :], in_=w4_rows[q])
+        w4_rows = w4_scales.bitcast(I32).rearrange("a (q r) n -> r q a n", r=ROWS)
+        for r in range(ROWS):
+            nc.gpsimd.dma_start(out=w4_planes[r:P:QUAD, :, :], in_=w4_rows[r])
         make_identity(nc, identity[:])
-
-        last_table_place = T + TILES * WINDOW
-        word_tables = [held.tile([P, T], U32, name="word_table%d" % a, align_bytes=64) for a in range(FP4_PASSES)]
-        word_tables.append(room.tile([P, T], U32, name="word_table2", align_bytes=64, offset=last_table_place))
-        w4_codes = room.tile([P, FP4_PASSES, 2 * M], U8, name="w4_codes", align_bytes=64, offset=last_table_place + WINDOW)
-        w8_raw = held.tile([P, PACK, M], F32, name="w8_raw", align_bytes=64)
-        w8_grouped = [
-            held.tile([P, W8_COLS, PACK], BF16, name="w8_grouped0", align_bytes=64),
-            again.tile([P, W8_COLS, PACK], BF16, name="w8_grouped1", align_bytes=64, offset=0),
-        ]
-        w8_codes = held.tile([P, M], U32, name="w8_codes", align_bytes=64)
-        w8_plane = held.tile([P, M], U8, name="w8_plane", align_bytes=64)
-        residuals = [room.tile([P, T], F32, name="residual%d" % m, align_bytes=64, offset=T + m * WINDOW) for m in range(TILES)]
-
-        def entries(first, count):
-            return offsets[:, first // LIST_ROWS : (first + count) // LIST_ROWS]
 
         def load_words(a):
             words = tab_words[a].rearrange("p t i -> p (t i)").bitcast(I32)
             nc.sync.dma_start(out=word_tables[a][:].bitcast(I32), in_=words)
 
-        def load_residual(m):
+        table_rows = tab_scales.bitcast(I32)
+        nc.sync.dma_start(out=scale_table[FP4_FROM:P, :], in_=table_rows[1:PASSES].rearrange("a q t -> q a t"))
+        nc.sync.dma_start(out=scale_table[FP8_FROM:QUAD, :], in_=table_rows[0])
+        nc.sync.dma_start(offsets[:], offs)
+        load_words(0)
+        nc.sync.dma_start(out=bias_rows[P - TILES : P, :], in_=b.rearrange("(m p) -> m p", p=P))
+        load_words(1)
+        nc.sync.dma_start(out=w8_raw[:], in_=w8.rearrange("(p j) n -> p j n", j=PACK))
+        load_words(2)
+        nc.sync.dma_start(out=w4_codes[:].bitcast(I32), in_=w4_words.rearrange("a p n -> p a n").bitcast(I32))
+        for m in range(TILES):
             nc.sync.dma_start(out=residuals[m][:], in_=rT[m * P : (m + 1) * P, :])
 
-        def group_w8(copy, first, end):
-            piece, within = divmod(first, W8_COLS)
+        def entries(first, count):
+            return offsets[:, first // LIST_ROWS : (first + count) // LIST_ROWS]
+
+        picked_scales = held.tile([P, S], U8, name="picked_scales", align_bytes=64)
+        nc.vector.tensor_copy(picked_scales[:], scale_table[:].bitcast(U8).indirect(offsets[:]))
+        picked_rows = picked_scales[:].bitcast(I32)
+        for q in range(P // QUAD):
+            first = FP4_FROM + q * FP4_PASSES * ROWS
+            nc.gpsimd.dma_start(out=token_planes[q * QUAD : q * QUAD + ROWS, 1:PASSES, :], in_=picked_rows[first : first + FP4_PASSES * ROWS, :])
+        for r in range(ROWS):
+            nc.gpsimd.dma_start(out=token_planes[ROWS + r : P : QUAD, 0, :], in_=picked_rows[FP8_FROM + r : QUAD : ROWS, :])
+
+        w8_grouped = [held.tile([P, W8_COLS, PACK], BF16, name="w8_grouped%d" % piece, align_bytes=64) for piece in range(W8_PIECES)]
+        w8_codes = held.tile([P, M], U32, name="w8_codes", align_bytes=64)
+        w8_plane = held.tile([P, M], U8, name="w8_plane", align_bytes=64)
+
+        def group_w8(copy, piece):
+            cols = slice(piece * W8_COLS, (piece + 1) * W8_COLS)
             copy(
-                w8_grouped[piece][:, within : within + end - first, :].rearrange("p (c i) j -> p c j i", i=4),
-                w8_raw[:, :, first:end].rearrange("p j (c i) -> p c j i", i=4),
+                w8_grouped[piece][:].rearrange("p (c i) j -> p c j i", i=4),
+                w8_raw[:, :, cols].rearrange("p j (c i) -> p c j i", i=4),
             )
 
         def quantise(piece):
@@ -104,41 +115,19 @@ def tile_list_tabres_gelu_kernel(tc, tab_words, tab_scales, w8, w4_words, w4_sca
                 in_=w8_grouped[piece][:].rearrange("p n j -> p (n j)"),
             )
 
-        table_rows = tab_scales.bitcast(I32)
-        fp4_from = DEALT_FROM + SCALE_ROWS
-        nc.sync.dma_start(out=scale_table[fp4_from:P, :], in_=table_rows[1:PASSES].rearrange("a q t -> q a t"))
-        nc.sync.dma_start(out=scale_table[DEALT_FROM:fp4_from, :], in_=table_rows[0])
-        nc.sync.dma_start(offsets[:], offs)
-        load_words(0)
-        nc.sync.dma_start(out=bias_rows[P - TILES : P, :], in_=b.rearrange("(m p) -> m p", p=P))
-        load_words(1)
-        nc.sync.dma_start(out=w8_raw[:], in_=w8.rearrange("(p j) n -> p j n", j=PACK))
+        picked_words = [held.tile([P, S], U32, name="picked_words%d" % a, align_bytes=64) for a in range(PASSES)]
 
-        picked_scales = held.tile([P, S], U8, name="picked_scales", align_bytes=64)
-        nc.vector.tensor_copy(picked_scales[:], scale_table.bitcast(U8).indirect(offsets[:]))
-        picked_rows = picked_scales[:].bitcast(I32)
-        for q in range(P // QUAD):
-            first = DEALT_FROM + q * ROWS
-            nc.sync.dma_start(out=token_planes[q * QUAD + ROWS : q * QUAD + 2 * ROWS, 0, :], in_=picked_rows[first : first + ROWS, :])
-        load_words(2)
-        for q in range(P // QUAD):
-            first = fp4_from + q * FP4_PASSES * ROWS
-            nc.sync.dma_start(out=token_planes[q * QUAD : q * QUAD + ROWS, 1:PASSES, :], in_=picked_rows[first : first + FP4_PASSES * ROWS, :])
-        nc.sync.dma_start(out=w4_codes[:].bitcast(I32), in_=w4_words.rearrange("a p n -> p a n").bitcast(I32))
-        for m in range(TILES):
-            load_residual(m)
+        def pick_words(a, first, count):
+            nc.vector.tensor_copy(picked_words[a][:, first : first + count], word_tables[a][:].indirect(entries(first, count)))
 
-        picked_words = [held.tile([P, S], U32, name="picked_words%d" % a, align_bytes=64) for a in range(FP4_PASSES)]
-        picked_words.append(again.tile([P, S], U32, name="picked_words2", align_bytes=64, offset=0))
         for a in range(FP4_PASSES):
-            nc.vector.tensor_copy(picked_words[a][:], word_tables[a][:].indirect(offsets[:]))
-        group_w8(nc.vector.tensor_copy, 0, W8_COLS)
-        group_w8(nc.scalar.copy, VECTOR_COLS, M)
+            pick_words(a, 0, S)
+        group_w8(nc.vector.tensor_copy, 0)
+        group_w8(nc.scalar.copy, 1)
         quantise(0)
-        group_w8(nc.vector.tensor_copy, W8_COLS, VECTOR_COLS)
+        pick_words(2, 0, BANK)
         quantise(1)
-        for h in range(HALVES):
-            nc.vector.tensor_copy(picked_words[2][:, h * BANK : (h + 1) * BANK], word_tables[2][:].indirect(entries(h * BANK, BANK)))
+        pick_words(2, BANK, BANK)
 
         bias_psum = turned.tile([P, BANK], F32, name="bias_psum")
         nc.tensor.transpose(bias_psum[:, 0:P], bias_rows[:], identity[:])

@@ -35,25 +35,31 @@ W8_COLS = M // W8_PIECES
 PIECE_TILES = TILES // W8_PIECES
 STORE_ENDS = [4, 6, 7]
 LAST_CUTS = [768, 256]
+WINDOW = 4 * T
+HALVED_TILES = 2
 
 
 def tile_list_tabres_gelu_kernel(tc, tab_words, tab_scales, w8, w4_words, w4_scales, rT, b, offs, out):
     nc = tc.nc
     with ExitStack() as ctx:
         held = ctx.enter_context(tc.tile_pool(name="held", bufs=1))
+        room = ctx.enter_context(tc.tile_pool(name="room", bufs=1))
         psum = ctx.enter_context(tc.psum_pool(name="psum", bufs=1))
         turned = ctx.enter_context(tc.psum_pool(name="turned", bufs=1))
 
         offsets = held.tile([P, S // LIST_ROWS], U16, name="offsets")
-        scale_table = held.tile([P, T // 4], I32, name="scale_table", align_bytes=64)
+        scale_room = room.tile([P, (T + (TILES + 2) * WINDOW) // 4], I32, name="scale_room", align_bytes=64, offset=0)
+        scale_table = scale_room[:, 0 : T // 4]
         token_planes = held.tile([P, PASSES, S // 4], I32, name="token_planes", align_bytes=64)
         w4_planes = held.tile([P, FP4_PASSES, M // 4], I32, name="w4_planes", align_bytes=64)
         bias_rows = held.tile([P, P], F32, name="bias_rows")
         identity = held.tile([P, P], F32, name="identity")
-        word_tables = [held.tile([P, T], U32, name="word_table%d" % a, align_bytes=64) for a in range(PASSES)]
-        w4_codes = held.tile([P, FP4_PASSES, 2 * M], U8, name="w4_codes", align_bytes=64)
+        word_tables = [held.tile([P, T], U32, name="word_table%d" % a, align_bytes=64) for a in range(FP4_PASSES)]
+        last_table_place = T + TILES * WINDOW
+        word_tables.append(room.tile([P, T], U32, name="word_table2", align_bytes=64, offset=last_table_place))
+        w4_codes = room.tile([P, FP4_PASSES, 2 * M], U8, name="w4_codes", align_bytes=64, offset=last_table_place + WINDOW)
         w8_raw = held.tile([P, PACK, M], F32, name="w8_raw", align_bytes=64)
-        residuals = [held.tile([P, T], F32, name="residual%d" % m, align_bytes=64) for m in range(TILES)]
+        residuals = [room.tile([P, T], F32, name="residual%d" % m, align_bytes=64, offset=T + m * WINDOW) for m in range(TILES)]
 
         nc.vector.memset(scale_table[0:FP8_FROM, :], 0)
         nc.vector.memset(scale_table[QUAD : 2 * QUAD, :], 0)
@@ -67,6 +73,9 @@ def tile_list_tabres_gelu_kernel(tc, tab_words, tab_scales, w8, w4_words, w4_sca
             nc.gpsimd.dma_start(out=w4_planes[r:P:QUAD, :, :], in_=w4_rows[r])
         make_identity(nc, identity[:])
 
+        warm = held.tile([P, 1], F32, name="warm")
+        nc.scalar.activation(warm[:], identity[:, 0:1], GELU)
+
         def load_words(a):
             words = tab_words[a].rearrange("p t i -> p (t i)").bitcast(I32)
             nc.sync.dma_start(out=word_tables[a][:].bitcast(I32), in_=words)
@@ -79,26 +88,29 @@ def tile_list_tabres_gelu_kernel(tc, tab_words, tab_scales, w8, w4_words, w4_sca
         nc.sync.dma_start(out=bias_rows[P - TILES : P, :], in_=b.rearrange("(m p) -> m p", p=P))
         load_words(1)
         nc.sync.dma_start(out=w8_raw[:], in_=w8.rearrange("(p j) n -> p j n", j=PACK))
-        load_words(2)
-        nc.sync.dma_start(out=w4_codes[:].bitcast(I32), in_=w4_words.rearrange("a p n -> p a n").bitcast(I32))
-        for m in range(TILES):
-            nc.sync.dma_start(out=residuals[m][:], in_=rT[m * P : (m + 1) * P, :])
 
         def entries(first, count):
             return offsets[:, first // LIST_ROWS : (first + count) // LIST_ROWS]
 
         picked_scales = held.tile([P, S], U8, name="picked_scales", align_bytes=64)
-        nc.vector.tensor_copy(picked_scales[:], scale_table[:].bitcast(U8).indirect(offsets[:]))
+        nc.vector.tensor_copy(picked_scales[:], scale_table.bitcast(U8).indirect(offsets[:]))
         picked_rows = picked_scales[:].bitcast(I32)
         for q in range(P // QUAD):
             first = FP4_FROM + q * FP4_PASSES * ROWS
             nc.gpsimd.dma_start(out=token_planes[q * QUAD : q * QUAD + ROWS, 1:PASSES, :], in_=picked_rows[first : first + FP4_PASSES * ROWS, :])
         for r in range(ROWS):
-            nc.gpsimd.dma_start(out=token_planes[ROWS + r : P : QUAD, 0, :], in_=picked_rows[FP8_FROM + r : QUAD : ROWS, :])
+            nc.sync.dma_start(out=token_planes[ROWS + r : P : QUAD, 0, :], in_=picked_rows[FP8_FROM + r : QUAD : ROWS, :])
+        load_words(2)
+        nc.sync.dma_start(out=w4_codes[:].bitcast(I32), in_=w4_words.rearrange("a p n -> p a n").bitcast(I32))
+        for m in range(TILES):
+            nc.sync.dma_start(out=residuals[m][:], in_=rT[m * P : (m + 1) * P, :])
 
         w8_grouped = [held.tile([P, W8_COLS, PACK], BF16, name="w8_grouped%d" % piece, align_bytes=64) for piece in range(W8_PIECES)]
-        w8_codes = held.tile([P, M], U32, name="w8_codes", align_bytes=64)
-        w8_plane = held.tile([P, M], U8, name="w8_plane", align_bytes=64)
+        w8_codes = [
+            held.tile([P, W8_COLS], U32, name="w8_codes0", align_bytes=64),
+            room.tile([P, W8_COLS], U32, name="w8_codes1", align_bytes=64, offset=last_table_place),
+        ]
+        w8_planes = [held.tile([P, W8_COLS], U8, name="w8_plane%d" % piece, align_bytes=64) for piece in range(W8_PIECES)]
 
         def group_w8(copy, piece):
             cols = slice(piece * W8_COLS, (piece + 1) * W8_COLS)
@@ -108,10 +120,9 @@ def tile_list_tabres_gelu_kernel(tc, tab_words, tab_scales, w8, w4_words, w4_sca
             )
 
         def quantise(piece):
-            cols = slice(piece * W8_COLS, (piece + 1) * W8_COLS)
             nc.vector.quantize_mx(
-                out=w8_codes[:, cols].bitcast(FP8X4),
-                scales=w8_plane[:, cols],
+                out=w8_codes[piece][:].bitcast(FP8X4),
+                scales=w8_planes[piece][:],
                 in_=w8_grouped[piece][:].rearrange("p n j -> p (n j)"),
             )
 
@@ -126,8 +137,8 @@ def tile_list_tabres_gelu_kernel(tc, tab_words, tab_scales, w8, w4_words, w4_sca
         group_w8(nc.scalar.copy, 1)
         quantise(0)
         pick_words(2, 0, BANK)
-        quantise(1)
         pick_words(2, BANK, BANK)
+        quantise(1)
 
         bias_psum = turned.tile([P, BANK], F32, name="bias_psum")
         nc.tensor.transpose(bias_psum[:, 0:P], bias_rows[:], identity[:])
@@ -144,7 +155,9 @@ def tile_list_tabres_gelu_kernel(tc, tab_words, tab_scales, w8, w4_words, w4_sca
             rows = slice(m * P, (m + 1) * P)
             cols = slice(h * BANK, (h + 1) * BANK)
             if a == 0:
-                weights, weight_scales = w8_codes[:, rows].bitcast(FP8X4), w8_plane[:, rows]
+                piece, within = divmod(m, PIECE_TILES)
+                piece_rows = slice(within * P, (within + 1) * P)
+                weights, weight_scales = w8_codes[piece][:, piece_rows].bitcast(FP8X4), w8_planes[piece][:, piece_rows]
                 token_scales = token_bytes[ROWS:P, 0, cols]
             else:
                 weights = w4_codes[:, a - 1, 2 * m * P : 2 * (m + 1) * P].bitcast(FP4X4)
@@ -161,14 +174,13 @@ def tile_list_tabres_gelu_kernel(tc, tab_words, tab_scales, w8, w4_words, w4_sca
 
         for m in range(TILES):
             pair = 0 if m < PIECE_TILES else (m + 1) % 2
-            order = [0, 1, 2] if m < PIECE_TILES else [1, 2, 0]
             for h in range(HALVES):
                 cols = slice(h * BANK, (h + 1) * BANK)
                 bank = psum.tile([P, BANK], F32, name="bank%d" % (HALVES * pair + h))
-                for a in order:
-                    multiply(m, h, bank, a, a == order[0], a == order[-1])
+                for a in range(PASSES):
+                    multiply(m, h, bank, a, a == 0, a == PASSES - 1)
                 nc.scalar.activation(activated[:, m, cols], bank[:], GELU, bias=bias[:, m : m + 1])
-            cuts = [BANK, BANK] if m == 0 else LAST_CUTS if m == TILES - 1 else [S]
+            cuts = [BANK, BANK] if m < HALVED_TILES else LAST_CUTS if m == TILES - 1 else [S]
             for i, count in enumerate(cuts):
                 first = sum(cuts[:i])
                 cols = slice(first, first + count)

@@ -36,7 +36,8 @@ PIECE_TILES = TILES // W8_PIECES
 STORE_ENDS = [4, 6, 7]
 LAST_CUTS = [768, 256]
 WINDOW = 4 * T
-HALVED_TILES = 2
+HALVED_TILES = [0, 1, 3]
+LATE_AFTER = 2
 
 
 def tile_list_tabres_gelu_kernel(tc, tab_words, tab_scales, w8, w4_words, w4_scales, rT, b, offs, out):
@@ -48,7 +49,7 @@ def tile_list_tabres_gelu_kernel(tc, tab_words, tab_scales, w8, w4_words, w4_sca
         turned = ctx.enter_context(tc.psum_pool(name="turned", bufs=1))
 
         offsets = held.tile([P, S // LIST_ROWS], U16, name="offsets")
-        scale_room = room.tile([P, (T + (TILES + 2) * WINDOW) // 4], I32, name="scale_room", align_bytes=64, offset=0)
+        scale_room = room.tile([P, (T + (TILES + 3) * WINDOW) // 4], I32, name="scale_room", align_bytes=64, offset=0)
         scale_table = scale_room[:, 0 : T // 4]
         token_planes = held.tile([P, PASSES, S // 4], I32, name="token_planes", align_bytes=64)
         w4_planes = held.tile([P, FP4_PASSES, M // 4], I32, name="w4_planes", align_bytes=64)
@@ -58,7 +59,8 @@ def tile_list_tabres_gelu_kernel(tc, tab_words, tab_scales, w8, w4_words, w4_sca
         last_table_place = T + TILES * WINDOW
         word_tables.append(room.tile([P, T], U32, name="word_table2", align_bytes=64, offset=last_table_place))
         w4_codes = room.tile([P, FP4_PASSES, 2 * M], U8, name="w4_codes", align_bytes=64, offset=last_table_place + WINDOW)
-        w8_raw = held.tile([P, PACK, M], F32, name="w8_raw", align_bytes=64)
+        w8_raw = [held.tile([P, PACK, W8_COLS], F32, name="w8_raw0", align_bytes=64)]
+        w8_raw.append(room.tile([P, PACK, W8_COLS], F32, name="w8_raw1", align_bytes=64, offset=last_table_place + 2 * WINDOW))
         residuals = [room.tile([P, T], F32, name="residual%d" % m, align_bytes=64, offset=T + m * WINDOW) for m in range(TILES)]
 
         nc.vector.memset(scale_table[0:FP8_FROM, :], 0)
@@ -80,6 +82,10 @@ def tile_list_tabres_gelu_kernel(tc, tab_words, tab_scales, w8, w4_words, w4_sca
             words = tab_words[a].rearrange("p t i -> p (t i)").bitcast(I32)
             nc.sync.dma_start(out=word_tables[a][:].bitcast(I32), in_=words)
 
+        def load_w8(piece):
+            cols = slice(piece * W8_COLS, (piece + 1) * W8_COLS)
+            nc.sync.dma_start(out=w8_raw[piece][:], in_=w8.rearrange("(p j) n -> p j n", j=PACK)[:, :, cols])
+
         table_rows = tab_scales.bitcast(I32)
         nc.sync.dma_start(out=scale_table[FP4_FROM:P, :], in_=table_rows[1:PASSES].rearrange("a q t -> q a t"))
         nc.sync.dma_start(out=scale_table[FP8_FROM:QUAD, :], in_=table_rows[0])
@@ -87,7 +93,7 @@ def tile_list_tabres_gelu_kernel(tc, tab_words, tab_scales, w8, w4_words, w4_sca
         load_words(0)
         nc.sync.dma_start(out=bias_rows[P - TILES : P, :], in_=b.rearrange("(m p) -> m p", p=P))
         load_words(1)
-        nc.sync.dma_start(out=w8_raw[:], in_=w8.rearrange("(p j) n -> p j n", j=PACK))
+        load_w8(0)
 
         def entries(first, count):
             return offsets[:, first // LIST_ROWS : (first + count) // LIST_ROWS]
@@ -100,30 +106,32 @@ def tile_list_tabres_gelu_kernel(tc, tab_words, tab_scales, w8, w4_words, w4_sca
             nc.gpsimd.dma_start(out=token_planes[q * QUAD : q * QUAD + ROWS, 1:PASSES, :], in_=picked_rows[first : first + FP4_PASSES * ROWS, :])
         for r in range(ROWS):
             nc.sync.dma_start(out=token_planes[ROWS + r : P : QUAD, 0, :], in_=picked_rows[FP8_FROM + r : QUAD : ROWS, :])
-        load_words(2)
         nc.sync.dma_start(out=w4_codes[:].bitcast(I32), in_=w4_words.rearrange("a p n -> p a n").bitcast(I32))
+        load_words(2)
         for m in range(TILES):
             nc.sync.dma_start(out=residuals[m][:], in_=rT[m * P : (m + 1) * P, :])
+            if m == LATE_AFTER:
+                load_w8(1)
 
-        w8_grouped = [held.tile([P, W8_COLS, PACK], BF16, name="w8_grouped%d" % piece, align_bytes=64) for piece in range(W8_PIECES)]
-        w8_codes = [
-            held.tile([P, W8_COLS], U32, name="w8_codes0", align_bytes=64),
-            room.tile([P, W8_COLS], U32, name="w8_codes1", align_bytes=64, offset=last_table_place),
+        summed = held.tile([P, TILES, S], F32, name="summed", align_bytes=64)
+        w8_grouped = [
+            held.tile([P, W8_COLS * PACK], BF16, name="w8_grouped0", align_bytes=64)[:],
+            summed[:, LATE_AFTER + 1, :].bitcast(BF16),
         ]
+        w8_codes = [held.tile([P, W8_COLS], U32, name="w8_codes%d" % piece, align_bytes=64) for piece in range(W8_PIECES)]
         w8_planes = [held.tile([P, W8_COLS], U8, name="w8_plane%d" % piece, align_bytes=64) for piece in range(W8_PIECES)]
 
-        def group_w8(copy, piece):
-            cols = slice(piece * W8_COLS, (piece + 1) * W8_COLS)
-            copy(
-                w8_grouped[piece][:].rearrange("p (c i) j -> p c j i", i=4),
-                w8_raw[:, :, cols].rearrange("p j (c i) -> p c j i", i=4),
+        def group_w8(piece):
+            nc.scalar.copy(
+                w8_grouped[piece].rearrange("p (c i j) -> p c j i", i=4, j=PACK),
+                w8_raw[piece][:].rearrange("p j (c i) -> p c j i", i=4),
             )
 
         def quantise(piece):
             nc.vector.quantize_mx(
                 out=w8_codes[piece][:].bitcast(FP8X4),
                 scales=w8_planes[piece][:],
-                in_=w8_grouped[piece][:].rearrange("p n j -> p (n j)"),
+                in_=w8_grouped[piece],
             )
 
         picked_words = [held.tile([P, S], U32, name="picked_words%d" % a, align_bytes=64) for a in range(PASSES)]
@@ -133,20 +141,19 @@ def tile_list_tabres_gelu_kernel(tc, tab_words, tab_scales, w8, w4_words, w4_sca
 
         for a in range(FP4_PASSES):
             pick_words(a, 0, S)
-        group_w8(nc.vector.tensor_copy, 0)
-        group_w8(nc.scalar.copy, 1)
+        group_w8(0)
         quantise(0)
-        pick_words(2, 0, BANK)
-        pick_words(2, BANK, BANK)
-        quantise(1)
+        for h in range(HALVES):
+            pick_words(2, h * BANK, BANK)
 
         bias_psum = turned.tile([P, BANK], F32, name="bias_psum")
         nc.tensor.transpose(bias_psum[:, 0:P], bias_rows[:], identity[:])
         bias = held.tile([P, TILES], F32, name="bias")
         nc.scalar.copy(bias[:], bias_psum[:, P - TILES : P])
 
-        activated = held.tile([P, TILES, S], F32, name="activated")
-        summed = held.tile([P, TILES, S], F32, name="summed")
+        activated = [held.tile([P, S], F32, name="activated%d" % m) for m in range(TILES) if m != LATE_AFTER + 1]
+        late_tile = (room.tile([P, S], F32, name="activated_late", align_bytes=64, offset=last_table_place + 2 * WINDOW))
+        activated = activated[: LATE_AFTER + 1] + [late_tile] + activated[LATE_AFTER + 1 :]
         w4_scale_bytes = w4_planes[:].bitcast(U8)
         token_bytes = token_planes[:].bitcast(U8)
         out_tiles = out.rearrange("(m p) j -> p m j", p=P)
@@ -173,18 +180,22 @@ def tile_list_tabres_gelu_kernel(tc, tab_words, tab_scales, w8, w4_words, w4_sca
             )
 
         for m in range(TILES):
+            if m == LATE_AFTER + 1:
+                group_w8(1)
+                quantise(1)
+            order = [1, 0, 2] if m < PIECE_TILES else [0, 1, 2]
             pair = 0 if m < PIECE_TILES else (m + 1) % 2
             for h in range(HALVES):
                 cols = slice(h * BANK, (h + 1) * BANK)
                 bank = psum.tile([P, BANK], F32, name="bank%d" % (HALVES * pair + h))
-                for a in range(PASSES):
-                    multiply(m, h, bank, a, a == 0, a == PASSES - 1)
-                nc.scalar.activation(activated[:, m, cols], bank[:], GELU, bias=bias[:, m : m + 1])
-            cuts = [BANK, BANK] if m < HALVED_TILES else LAST_CUTS if m == TILES - 1 else [S]
+                for a in order:
+                    multiply(m, h, bank, a, a == order[0], a == order[-1])
+                nc.scalar.activation(activated[m][:, cols], bank[:], GELU, bias=bias[:, m : m + 1])
+            cuts = [BANK, BANK] if m in HALVED_TILES else LAST_CUTS if m == TILES - 1 else [S]
             for i, count in enumerate(cuts):
                 first = sum(cuts[:i])
                 cols = slice(first, first + count)
-                nc.vector.tensor_tensor(summed[:, m, cols], residuals[m][:].indirect(entries(first, count)), activated[:, m, cols], ADD)
+                nc.vector.tensor_tensor(summed[:, m, cols], residuals[m][:].indirect(entries(first, count)), activated[m][:, cols], ADD)
                 if m == TILES - 1:
                     nc.sync.dma_start(out=out_tiles[:, m, cols], in_=summed[:, m, cols])
             if m + 1 in STORE_ENDS:

@@ -30,13 +30,16 @@ LIST_ROWS = 16
 SCALE_ROWS = P * PACK // QUAD
 FP8_FROM = QUAD - SCALE_ROWS
 FP4_FROM = P - FP4_PASSES * SCALE_ROWS
-W8_PIECES = 2
-W8_COLS = M // W8_PIECES
-PIECE_TILES = TILES // W8_PIECES
+W8_LOADS = 2
+W8_COLS = M // W8_LOADS
+PIECE_TILES = 2
+PIECE_COLS = PIECE_TILES * P
+W8_PIECES = TILES // PIECE_TILES
+BIAS_RUNS = [range(0, 3), range(3, 5), range(5, TILES)]
 STORE_ENDS = [4, 6, 7]
 LAST_CUTS = [768, 256]
 WINDOW = 4 * T
-HALVED_TILES = [0, 1, 3]
+HALVED_TILES = [0, 1]
 LATE_AFTER = 2
 
 
@@ -45,6 +48,7 @@ def tile_list_tabres_gelu_kernel(tc, tab_words, tab_scales, w8, w4_words, w4_sca
     with ExitStack() as ctx:
         held = ctx.enter_context(tc.tile_pool(name="held", bufs=1))
         room = ctx.enter_context(tc.tile_pool(name="room", bufs=1))
+        again = ctx.enter_context(tc.tile_pool(name="again", bufs=1))
         psum = ctx.enter_context(tc.psum_pool(name="psum", bufs=1))
         turned = ctx.enter_context(tc.psum_pool(name="turned", bufs=1))
 
@@ -113,25 +117,26 @@ def tile_list_tabres_gelu_kernel(tc, tab_words, tab_scales, w8, w4_words, w4_sca
             if m == LATE_AFTER:
                 load_w8(1)
 
-        summed = held.tile([P, TILES, S], F32, name="summed", align_bytes=64)
-        w8_grouped = [
-            held.tile([P, W8_COLS * PACK], BF16, name="w8_grouped0", align_bytes=64)[:],
-            summed[:, LATE_AFTER + 1, :].bitcast(BF16),
-        ]
-        w8_codes = [held.tile([P, W8_COLS], U32, name="w8_codes%d" % piece, align_bytes=64) for piece in range(W8_PIECES)]
-        w8_planes = [held.tile([P, W8_COLS], U8, name="w8_plane%d" % piece, align_bytes=64) for piece in range(W8_PIECES)]
+        piece_bytes = 2 * PACK * PIECE_COLS
+        biases = [again.tile([P, len(run)], F32, name="bias%d" % i, align_bytes=64, offset=i * piece_bytes) for i, run in enumerate(BIAS_RUNS)]
+        w8_grouped = [held.tile([P, PIECE_COLS * PACK], BF16, name="w8_grouped%d" % piece, align_bytes=64) for piece in range(2)]
+        for i in range(2):
+            w8_grouped.append(again.tile([P, PIECE_COLS * PACK], BF16, name="w8_grouped_late%d" % i, align_bytes=64, offset=i * piece_bytes))
+        w8_codes = [held.tile([P, PIECE_COLS], U32, name="w8_codes%d" % piece, align_bytes=64) for piece in range(W8_PIECES)]
+        w8_planes = [held.tile([P, PIECE_COLS], U8, name="w8_plane%d" % piece, align_bytes=64) for piece in range(W8_PIECES)]
 
-        def group_w8(piece):
-            nc.scalar.copy(
-                w8_grouped[piece].rearrange("p (c i j) -> p c j i", i=4, j=PACK),
-                w8_raw[piece][:].rearrange("p j (c i) -> p c j i", i=4),
+        def group_w8(copy, piece):
+            load, within = divmod(piece * PIECE_COLS, W8_COLS)
+            copy(
+                w8_grouped[piece][:].rearrange("p (c i j) -> p c j i", i=4, j=PACK),
+                w8_raw[load][:, :, within : within + PIECE_COLS].rearrange("p j (c i) -> p c j i", i=4),
             )
 
         def quantise(piece):
             nc.vector.quantize_mx(
                 out=w8_codes[piece][:].bitcast(FP8X4),
                 scales=w8_planes[piece][:],
-                in_=w8_grouped[piece],
+                in_=w8_grouped[piece][:],
             )
 
         picked_words = [held.tile([P, S], U32, name="picked_words%d" % a, align_bytes=64) for a in range(PASSES)]
@@ -141,19 +146,20 @@ def tile_list_tabres_gelu_kernel(tc, tab_words, tab_scales, w8, w4_words, w4_sca
 
         for a in range(FP4_PASSES):
             pick_words(a, 0, S)
-        group_w8(0)
+        group_w8(nc.scalar.copy, 0)
+        group_w8(nc.vector.tensor_copy, 1)
         quantise(0)
+        quantise(1)
         for h in range(HALVES):
             pick_words(2, h * BANK, BANK)
 
         bias_psum = turned.tile([P, BANK], F32, name="bias_psum")
         nc.tensor.transpose(bias_psum[:, 0:P], bias_rows[:], identity[:])
-        bias = held.tile([P, TILES], F32, name="bias")
-        nc.scalar.copy(bias[:], bias_psum[:, P - TILES : P])
+        for i, run in enumerate(BIAS_RUNS):
+            nc.scalar.copy(biases[i][:], bias_psum[:, P - TILES + run.start : P - TILES + run.stop])
 
-        activated = [held.tile([P, S], F32, name="activated%d" % m) for m in range(TILES) if m != LATE_AFTER + 1]
-        late_tile = (room.tile([P, S], F32, name="activated_late", align_bytes=64, offset=last_table_place + 2 * WINDOW))
-        activated = activated[: LATE_AFTER + 1] + [late_tile] + activated[LATE_AFTER + 1 :]
+        activated = held.tile([P, TILES, S], F32, name="activated")
+        summed = held.tile([P, TILES, S], F32, name="summed")
         w4_scale_bytes = w4_planes[:].bitcast(U8)
         token_bytes = token_planes[:].bitcast(U8)
         out_tiles = out.rearrange("(m p) j -> p m j", p=P)
@@ -180,22 +186,23 @@ def tile_list_tabres_gelu_kernel(tc, tab_words, tab_scales, w8, w4_words, w4_sca
             )
 
         for m in range(TILES):
-            if m == LATE_AFTER + 1:
-                group_w8(1)
-                quantise(1)
-            order = [1, 0, 2] if m < PIECE_TILES else [0, 1, 2]
-            pair = 0 if m < PIECE_TILES else (m + 1) % 2
+            run = [m in tiles for tiles in BIAS_RUNS].index(True)
+            if run > 0 and m == BIAS_RUNS[run].start:
+                group_w8(nc.scalar.copy, run + 1)
+                quantise(run + 1)
+            bias = biases[run][:, m - BIAS_RUNS[run].start : m - BIAS_RUNS[run].start + 1]
+            order = [1, 0, 2] if m == 0 else [1, 2, 0]
             for h in range(HALVES):
                 cols = slice(h * BANK, (h + 1) * BANK)
-                bank = psum.tile([P, BANK], F32, name="bank%d" % (HALVES * pair + h))
+                bank = psum.tile([P, BANK], F32, name="bank%d" % h)
                 for a in order:
                     multiply(m, h, bank, a, a == order[0], a == order[-1])
-                nc.scalar.activation(activated[m][:, cols], bank[:], GELU, bias=bias[:, m : m + 1])
+                nc.scalar.activation(activated[:, m, cols], bank[:], GELU, bias=bias)
             cuts = [BANK, BANK] if m in HALVED_TILES else LAST_CUTS if m == TILES - 1 else [S]
             for i, count in enumerate(cuts):
                 first = sum(cuts[:i])
                 cols = slice(first, first + count)
-                nc.vector.tensor_tensor(summed[:, m, cols], residuals[m][:].indirect(entries(first, count)), activated[m][:, cols], ADD)
+                nc.vector.tensor_tensor(summed[:, m, cols], residuals[m][:].indirect(entries(first, count)), activated[:, m, cols], ADD)
                 if m == TILES - 1:
                     nc.sync.dma_start(out=out_tiles[:, m, cols], in_=summed[:, m, cols])
             if m + 1 in STORE_ENDS:

@@ -105,13 +105,13 @@ def tile_list_tabres_gelu_kernel(tc, tab_words, tab_scales, w8, w4_words, w4_sca
         picked_scales = held.tile([P, S], U8, name="picked_scales", align_bytes=64)
         nc.vector.tensor_copy(picked_scales[:], scale_table.bitcast(U8).indirect(offsets[:]))
         picked_rows = picked_scales[:].bitcast(I32)
-        for q in range(P // QUAD):
-            first = FP4_FROM + q * FP4_PASSES * ROWS
-            nc.gpsimd.dma_start(out=token_planes[q * QUAD : q * QUAD + ROWS, 1:PASSES, :], in_=picked_rows[first : first + FP4_PASSES * ROWS, :])
         for r in range(ROWS):
             nc.sync.dma_start(out=token_planes[ROWS + r : P : QUAD, 0, :], in_=picked_rows[FP8_FROM + r : QUAD : ROWS, :])
         nc.sync.dma_start(out=w4_codes[:].bitcast(I32), in_=w4_words.rearrange("a p n -> p a n").bitcast(I32))
         load_words(2)
+        for q in range(P // QUAD):
+            first = FP4_FROM + q * FP4_PASSES * ROWS
+            nc.sync.dma_start(out=token_planes[q * QUAD : q * QUAD + ROWS, 1:PASSES, :], in_=picked_rows[first : first + FP4_PASSES * ROWS, :])
         for m in range(TILES):
             nc.sync.dma_start(out=residuals[m][:], in_=rT[m * P : (m + 1) * P, :])
             if m == LATE_AFTER:
@@ -191,7 +191,7 @@ def tile_list_tabres_gelu_kernel(tc, tab_words, tab_scales, w8, w4_words, w4_sca
                 group_w8(nc.scalar.copy, run + 1)
                 quantise(run + 1)
             bias = biases[run][:, m - BIAS_RUNS[run].start : m - BIAS_RUNS[run].start + 1]
-            order = [1, 0, 2] if m == 0 else [1, 2, 0]
+            order = [0, 1, 2] if m == 0 else [1, 2, 0]
             for h in range(HALVES):
                 cols = slice(h * BANK, (h + 1) * BANK)
                 bank = psum.tile([P, BANK], F32, name="bank%d" % h)

@@ -32,10 +32,8 @@ FP8_FROM = QUAD - SCALE_ROWS
 FP4_FROM = P - FP4_PASSES * SCALE_ROWS
 W8_LOADS = 2
 W8_COLS = M // W8_LOADS
-PIECE_TILES = 2
-PIECE_COLS = PIECE_TILES * P
-W8_PIECES = TILES // PIECE_TILES
-BIAS_RUNS = [range(0, 3), range(3, 5), range(5, TILES)]
+W8_PIECES = [range(0, 2), range(2, 4)] + [range(m, m + 1) for m in range(4, TILES)]
+BIAS_RUNS = [range(0, 3)] + [range(m, m + 1) for m in range(3, 6)] + [range(6, TILES)]
 STORE_ENDS = [4, 6, 7]
 LAST_CUTS = [768, 256]
 WINDOW = 4 * T
@@ -117,19 +115,20 @@ def tile_list_tabres_gelu_kernel(tc, tab_words, tab_scales, w8, w4_words, w4_sca
             if m == LATE_AFTER:
                 load_w8(1)
 
-        piece_bytes = 2 * PACK * PIECE_COLS
-        biases = [again.tile([P, len(run)], F32, name="bias%d" % i, align_bytes=64, offset=i * piece_bytes) for i, run in enumerate(BIAS_RUNS)]
-        w8_grouped = [held.tile([P, PIECE_COLS * PACK], BF16, name="w8_grouped%d" % piece, align_bytes=64) for piece in range(2)]
-        for i in range(2):
-            w8_grouped.append(again.tile([P, PIECE_COLS * PACK], BF16, name="w8_grouped_late%d" % i, align_bytes=64, offset=i * piece_bytes))
-        w8_codes = [held.tile([P, PIECE_COLS], U32, name="w8_codes%d" % piece, align_bytes=64) for piece in range(W8_PIECES)]
-        w8_planes = [held.tile([P, PIECE_COLS], U8, name="w8_plane%d" % piece, align_bytes=64) for piece in range(W8_PIECES)]
+        late_bytes = 2 * PACK * P
+        biases = [again.tile([P, len(run)], F32, name="bias%d" % i, align_bytes=64, offset=i * late_bytes) for i, run in enumerate(BIAS_RUNS)]
+        widths = [len(piece) * P for piece in W8_PIECES]
+        w8_grouped = [held.tile([P, widths[piece] * PACK], BF16, name="w8_grouped%d" % piece, align_bytes=64) for piece in range(2)]
+        for i in range(len(W8_PIECES) - 2):
+            w8_grouped.append(again.tile([P, P * PACK], BF16, name="w8_grouped_late%d" % i, align_bytes=64, offset=i * late_bytes))
+        w8_codes = [held.tile([P, width], U32, name="w8_codes%d" % piece, align_bytes=64) for piece, width in enumerate(widths)]
+        w8_planes = [held.tile([P, width], U8, name="w8_plane%d" % piece, align_bytes=64) for piece, width in enumerate(widths)]
 
         def group_w8(copy, piece):
-            load, within = divmod(piece * PIECE_COLS, W8_COLS)
+            load, within = divmod(W8_PIECES[piece].start * P, W8_COLS)
             copy(
                 w8_grouped[piece][:].rearrange("p (c i j) -> p c j i", i=4, j=PACK),
-                w8_raw[load][:, :, within : within + PIECE_COLS].rearrange("p j (c i) -> p c j i", i=4),
+                w8_raw[load][:, :, within : within + widths[piece]].rearrange("p j (c i) -> p c j i", i=4),
             )
 
         def quantise(piece):
@@ -168,7 +167,8 @@ def tile_list_tabres_gelu_kernel(tc, tab_words, tab_scales, w8, w4_words, w4_sca
             rows = slice(m * P, (m + 1) * P)
             cols = slice(h * BANK, (h + 1) * BANK)
             if a == 0:
-                piece, within = divmod(m, PIECE_TILES)
+                piece = [m in tiles for tiles in W8_PIECES].index(True)
+                within = m - W8_PIECES[piece].start
                 piece_rows = slice(within * P, (within + 1) * P)
                 weights, weight_scales = w8_codes[piece][:, piece_rows].bitcast(FP8X4), w8_planes[piece][:, piece_rows]
                 token_scales = token_bytes[ROWS:P, 0, cols]

@@ -105,8 +105,8 @@ def tile_list_tabres_gelu_kernel(tc, tab_words, tab_scales, w8, w4_words, w4_sca
         picked_rows = picked_scales[:].bitcast(I32)
         for r in range(ROWS):
             nc.sync.dma_start(out=token_planes[ROWS + r : P : QUAD, 0, :], in_=picked_rows[FP8_FROM + r : QUAD : ROWS, :])
-        nc.sync.dma_start(out=w4_codes[:].bitcast(I32), in_=w4_words.rearrange("a p n -> p a n").bitcast(I32))
         load_words(2)
+        nc.sync.dma_start(out=w4_codes[:].bitcast(I32), in_=w4_words.rearrange("a p n -> p a n").bitcast(I32))
         for q in range(P // QUAD):
             first = FP4_FROM + q * FP4_PASSES * ROWS
             nc.sync.dma_start(out=token_planes[q * QUAD : q * QUAD + ROWS, 1:PASSES, :], in_=picked_rows[first : first + FP4_PASSES * ROWS, :])
@@ -121,12 +121,13 @@ def tile_list_tabres_gelu_kernel(tc, tab_words, tab_scales, w8, w4_words, w4_sca
         w8_grouped = [held.tile([P, widths[piece] * PACK], BF16, name="w8_grouped%d" % piece, align_bytes=64) for piece in range(2)]
         for i in range(len(W8_PIECES) - 2):
             w8_grouped.append(again.tile([P, P * PACK], BF16, name="w8_grouped_late%d" % i, align_bytes=64, offset=i * late_bytes))
-        w8_codes = [held.tile([P, width], U32, name="w8_codes%d" % piece, align_bytes=64) for piece, width in enumerate(widths)]
+        w8_codes = [held.tile([P, width], U32, name="w8_codes%d" % piece, align_bytes=64) for piece, width in enumerate(widths) if piece != 1]
+        w8_codes[1:1] = [room.tile([P, widths[1]], U32, name="w8_codes1", align_bytes=64, offset=last_table_place)]
         w8_planes = [held.tile([P, width], U8, name="w8_plane%d" % piece, align_bytes=64) for piece, width in enumerate(widths)]
 
-        def group_w8(copy, piece):
+        def group_w8(piece):
             load, within = divmod(W8_PIECES[piece].start * P, W8_COLS)
-            copy(
+            nc.scalar.copy(
                 w8_grouped[piece][:].rearrange("p (c i j) -> p c j i", i=4, j=PACK),
                 w8_raw[load][:, :, within : within + widths[piece]].rearrange("p j (c i) -> p c j i", i=4),
             )
@@ -145,12 +146,12 @@ def tile_list_tabres_gelu_kernel(tc, tab_words, tab_scales, w8, w4_words, w4_sca
 
         for a in range(FP4_PASSES):
             pick_words(a, 0, S)
-        group_w8(nc.scalar.copy, 0)
-        group_w8(nc.vector.tensor_copy, 1)
+        group_w8(0)
+        group_w8(1)
         quantise(0)
-        quantise(1)
         for h in range(HALVES):
             pick_words(2, h * BANK, BANK)
+        quantise(1)
 
         bias_psum = turned.tile([P, BANK], F32, name="bias_psum")
         nc.tensor.transpose(bias_psum[:, 0:P], bias_rows[:], identity[:])
@@ -188,7 +189,7 @@ def tile_list_tabres_gelu_kernel(tc, tab_words, tab_scales, w8, w4_words, w4_sca
         for m in range(TILES):
             run = [m in tiles for tiles in BIAS_RUNS].index(True)
             if run > 0 and m == BIAS_RUNS[run].start:
-                group_w8(nc.scalar.copy, run + 1)
+                group_w8(run + 1)
                 quantise(run + 1)
             bias = biases[run][:, m - BIAS_RUNS[run].start : m - BIAS_RUNS[run].start + 1]
             order = [0, 1, 2] if m == 0 else [1, 2, 0]

from contextlib import ExitStack

import concourse.mybir as mybir
from concourse.masks import make_identity

K, M, T, S = 1536, 1024, 2048, 1024
FLOPS = 2 * K * M * S

F32 = mybir.dt.float32
BF16 = mybir.dt.bfloat16
I32 = mybir.dt.int32
U32 = mybir.dt.uint32
U16 = mybir.dt.uint16
U8 = mybir.dt.uint8
FP8X4 = mybir.dt.float8_e4m3fn_x4
FP4X4 = mybir.dt.float4_e2m1fn_x4
GELU = mybir.ActivationFunctionType.Gelu_apprx_tanh
ADD = mybir.AluOpType.add

P = 128
PACK = 4
PASSES = K // (P * PACK)
FP4_PASSES = PASSES - 1
QUAD = 32
ROWS = 4
BANK = 512
TILES = M // P
HALVES = S // BANK
LIST_ROWS = 16
SCALE_ROWS = P * PACK // QUAD
FP8_FROM = QUAD - SCALE_ROWS
FP4_FROM = P - FP4_PASSES * SCALE_ROWS
W8_LOADS = 2
W8_COLS = M // W8_LOADS
W8_PIECES = [range(0, 2), range(2, 4)] + [range(m, m + 1) for m in range(4, TILES)]
BIAS_RUNS = [range(0, 3)] + [range(m, m + 1) for m in range(3, 6)] + [range(6, TILES)]
STORE_ENDS = [4, 6, 7]
LAST_CUTS = [768, 256]
WINDOW = 4 * T
HALVED_TILES = [0, 1]
LATE_AFTER = 2


def tile_list_tabres_gelu_kernel(tc, tab_words, tab_scales, w8, w4_words, w4_scales, rT, b, offs, out):
    nc = tc.nc
    with ExitStack() as ctx:
        held = ctx.enter_context(tc.tile_pool(name="held", bufs=1))
        room = ctx.enter_context(tc.tile_pool(name="room", bufs=1))
        again = ctx.enter_context(tc.tile_pool(name="again", bufs=1))
        psum = ctx.enter_context(tc.psum_pool(name="psum", bufs=1))
        turned = ctx.enter_context(tc.psum_pool(name="turned", bufs=1))

        offsets = held.tile([P, S // LIST_ROWS], U16, name="offsets")
        scale_room = room.tile([P, (T + (TILES + 3) * WINDOW) // 4], I32, name="scale_room", align_bytes=64, offset=0)
        scale_table = scale_room[:, 0 : T // 4]
        token_planes = held.tile([P, PASSES, S // 4], I32, name="token_planes", align_bytes=64)
        w4_planes = held.tile([P, FP4_PASSES, M // 4], I32, name="w4_planes", align_bytes=64)
        bias_rows = held.tile([P, P], F32, name="bias_rows")
        identity = held.tile([P, P], F32, name="identity")
        word_tables = [held.tile([P, T], U32, name="word_table%d" % a, align_bytes=64) for a in range(FP4_PASSES)]
        last_table_place = T + TILES * WINDOW
        word_tables.append(room.tile([P, T], U32, name="word_table2", align_bytes=64, offset=last_table_place))
        w4_codes = room.tile([P, FP4_PASSES, 2 * M], U8, name="w4_codes", align_bytes=64, offset=last_table_place + WINDOW)
        w8_raw = [held.tile([P, PACK, W8_COLS], F32, name="w8_raw0", align_bytes=64)]
        w8_raw.append(room.tile([P, PACK, W8_COLS], F32, name="w8_raw1", align_bytes=64, offset=last_table_place + 2 * WINDOW))
        residuals = [room.tile([P, T], F32, name="residual%d" % m, align_bytes=64, offset=T + m * WINDOW) for m in range(TILES)]

        nc.vector.memset(scale_table[0:FP8_FROM, :], 0)
        nc.vector.memset(scale_table[QUAD : 2 * QUAD, :], 0)
        nc.vector.memset(scale_table[2 * QUAD : FP4_FROM, :], 0)
        nc.vector.memset(bias_rows[0:96, :], 0.0)
        nc.vector.memset(bias_rows[96 : P - TILES, :], 0.0)
        nc.vector.memset(token_planes[:], 0)
        nc.gpsimd.memset(w4_planes[:], 0)
        w4_rows = w4_scales.bitcast(I32).rearrange("a (q r) n -> r q a n", r=ROWS)
        for r in range(ROWS):
            nc.gpsimd.dma_start(out=w4_planes[r:P:QUAD, :, :], in_=w4_rows[r])
        make_identity(nc, identity[:])

        warm = held.tile([P, 1], F32, name="warm")
        nc.scalar.activation(warm[:], identity[:, 0:1], GELU)

        def load_words(a):
            words = tab_words[a].rearrange("p t i -> p (t i)").bitcast(I32)
            nc.sync.dma_start(out=word_tables[a][:].bitcast(I32), in_=words)

        def load_w8(piece):
            cols = slice(piece * W8_COLS, (piece + 1) * W8_COLS)
            nc.sync.dma_start(out=w8_raw[piece][:], in_=w8.rearrange("(p j) n -> p j n", j=PACK)[:, :, cols])

        table_rows = tab_scales.bitcast(I32)
        nc.sync.dma_start(out=scale_table[FP4_FROM:P, :], in_=table_rows[1:PASSES].rearrange("a q t -> q a t"))
        nc.sync.dma_start(out=scale_table[FP8_FROM:QUAD, :], in_=table_rows[0])
        nc.sync.dma_start(offsets[:], offs)
        load_words(0)
        nc.sync.dma_start(out=bias_rows[P - TILES : P, :], in_=b.rearrange("(m p) -> m p", p=P))
        load_words(1)
        load_w8(0)

        def entries(first, count):
            return offsets[:, first // LIST_ROWS : (first + count) // LIST_ROWS]

        picked_scales = held.tile([P, S], U8, name="picked_scales", align_bytes=64)
        nc.vector.tensor_copy(picked_scales[:], scale_table.bitcast(U8).indirect(offsets[:]))
        picked_rows = picked_scales[:].bitcast(I32)
        for r in range(ROWS):
            nc.sync.dma_start(out=token_planes[ROWS + r : P : QUAD, 0, :], in_=picked_rows[FP8_FROM + r : QUAD : ROWS, :])
        load_words(2)
        nc.sync.dma_start(out=w4_codes[:].bitcast(I32), in_=w4_words.rearrange("a p n -> p a n").bitcast(I32))
        for q in range(P // QUAD):
            first = FP4_FROM + q * FP4_PASSES * ROWS
            nc.sync.dma_start(out=token_planes[q * QUAD : q * QUAD + ROWS, 1:PASSES, :], in_=picked_rows[first : first + FP4_PASSES * ROWS, :])
        for m in range(TILES):
            nc.sync.dma_start(out=residuals[m][:], in_=rT[m * P : (m + 1) * P, :])
            if m == LATE_AFTER:
                load_w8(1)

        late_bytes = 2 * PACK * P
        biases = [again.tile([P, len(run)], F32, name="bias%d" % i, align_bytes=64, offset=i * late_bytes) for i, run in enumerate(BIAS_RUNS)]
        widths = [len(piece) * P for piece in W8_PIECES]
        w8_grouped = [held.tile([P, widths[piece] * PACK], BF16, name="w8_grouped%d" % piece, align_bytes=64) for piece in range(2)]
        for i in range(len(W8_PIECES) - 2):
            w8_grouped.append(again.tile([P, P * PACK], BF16, name="w8_grouped_late%d" % i, align_bytes=64, offset=i * late_bytes))
        w8_codes = [held.tile([P, width], U32, name="w8_codes%d" % piece, align_bytes=64) for piece, width in enumerate(widths) if piece != 1]
        w8_codes[1:1] = [room.tile([P, widths[1]], U32, name="w8_codes1", align_bytes=64, offset=last_table_place)]
        w8_planes = [held.tile([P, width], U8, name="w8_plane%d" % piece, align_bytes=64) for piece, width in enumerate(widths)]

        def group_w8(piece):
            load, within = divmod(W8_PIECES[piece].start * P, W8_COLS)
            nc.scalar.copy(
                w8_grouped[piece][:].rearrange("p (c i j) -> p c j i", i=4, j=PACK),
                w8_raw[load][:, :, within : within + widths[piece]].rearrange("p j (c i) -> p c j i", i=4),
            )

        def quantise(piece):
            nc.vector.quantize_mx(
                out=w8_codes[piece][:].bitcast(FP8X4),
                scales=w8_planes[piece][:],
                in_=w8_grouped[piece][:],
            )

        picked_words = [held.tile([P, S], U32, name="picked_words%d" % a, align_bytes=64) for a in range(PASSES)]

        def pick_words(a, first, count):
            nc.vector.tensor_copy(picked_words[a][:, first : first + count], word_tables[a][:].indirect(entries(first, count)))

        for a in range(FP4_PASSES):
            pick_words(a, 0, S)
        group_w8(0)
        group_w8(1)
        quantise(0)
        for h in range(HALVES):
            pick_words(2, h * BANK, BANK)
        quantise(1)

        bias_psum = turned.tile([P, BANK], F32, name="bias_psum")
        nc.tensor.transpose(bias_psum[:, 0:P], bias_rows[:], identity[:])
        for i, run in enumerate(BIAS_RUNS):
            nc.scalar.copy(biases[i][:], bias_psum[:, P - TILES + run.start : P - TILES + run.stop])

        activated = held.tile([P, TILES, S], F32, name="activated")
        summed = held.tile([P, TILES, S], F32, name="summed")
        w4_scale_bytes = w4_planes[:].bitcast(U8)
        token_bytes = token_planes[:].bitcast(U8)
        out_tiles = out.rearrange("(m p) j -> p m j", p=P)

        def multiply(m, h, bank, a, start, stop):
            rows = slice(m * P, (m + 1) * P)
            cols = slice(h * BANK, (h + 1) * BANK)
            if a == 0:
                piece = [m in tiles for tiles in W8_PIECES].index(True)
                within = m - W8_PIECES[piece].start
                piece_rows = slice(within * P, (within + 1) * P)
                weights, weight_scales = w8_codes[piece][:, piece_rows].bitcast(FP8X4), w8_planes[piece][:, piece_rows]
                token_scales = token_bytes[ROWS:P, 0, cols]
            else:
                weights = w4_codes[:, a - 1, 2 * m * P : 2 * (m + 1) * P].bitcast(FP4X4)
                weight_scales, token_scales = w4_scale_bytes[:, a - 1, rows], token_bytes[:, a, cols]
            nc.tensor.matmul_mx(
                out=bank[:],
                lhsT=weights,
                lhsT_scale=weight_scales,
                rhs=picked_words[a][:, cols].bitcast(FP8X4),
                rhs_scale=token_scales,
                start=start,
                stop=stop,
            )

        for m in range(TILES):
            run = [m in tiles for tiles in BIAS_RUNS].index(True)
            if run > 0 and m == BIAS_RUNS[run].start:
                group_w8(run + 1)
                quantise(run + 1)
            bias = biases[run][:, m - BIAS_RUNS[run].start : m - BIAS_RUNS[run].start + 1]
            order = [0, 1, 2] if m == 0 else [1, 2, 0]
            for h in range(HALVES):
                cols = slice(h * BANK, (h + 1) * BANK)
                bank = psum.tile([P, BANK], F32, name="bank%d" % h)
                for a in order:
                    multiply(m, h, bank, a, a == order[0], a == order[-1])
                nc.scalar.activation(activated[:, m, cols], bank[:], GELU, bias=bias)
            cuts = [BANK, BANK] if m in HALVED_TILES else LAST_CUTS if m == TILES - 1 else [S]
            for i, count in enumerate(cuts):
                first = sum(cuts[:i])
                cols = slice(first, first + count)
                nc.vector.tensor_tensor(summed[:, m, cols], residuals[m][:].indirect(entries(first, count)), activated[:, m, cols], ADD)
                if m == TILES - 1:
                    nc.sync.dma_start(out=out_tiles[:, m, cols], in_=summed[:, m, cols])
            if m + 1 in STORE_ENDS:
                place = STORE_ENDS.index(m + 1)
                tiles = slice(STORE_ENDS[place - 1] if place else 0, m + 1)
                nc.sync.dma_start(out=out_tiles[:, tiles, :], in_=summed[:, tiles, :])
